import numpy as np, ml_dtypes
CORES = [1,5,17,21,33,37,49,53]
N = 8
BF = ml_dtypes.bfloat16
def gentries(a):
    return np.ascontiguousarray(a.reshape(8, 16, -1).transpose(0, 2, 1)).reshape(8, -1)
def gtable(e):
    e = np.asarray(e); return np.ascontiguousarray(e.reshape(8, -1, 16).transpose(0, 2, 1)).reshape(128, -1).astype(np.int32)
V, K, B, CAP, E0, EC, RO = 640, 12, 80, 48, 2048, 512, 2
E = E0 + RO * EC
JJ, KK = np.triu_indices(K, 1)
def turn(ends):
    f = ends.reshape(-1); o = np.argsort(f, kind="stable"); s = f[o]; r = np.empty(len(f), np.int64); r[o] = np.arange(len(f)) - np.searchsorted(s, s)
    return r.reshape(-1, 2)
def place(rng, a, b):
    a = np.concatenate(a); b = np.concatenate(b); lo = np.minimum(a, b); hi = np.maximum(a, b)
    first = np.sort(np.unique(lo * V + hi, return_index=True)[1]); first = first[lo[first] != hi[first]]
    ends = np.stack([lo[first], hi[first]], 1); ends = ends[np.all(turn(ends) < K, axis=1)][:E0]
    slot = np.argsort(rng.random((V, K)), axis=1)[ends, turn(ends)]
    name = rng.permutation(np.concatenate([np.array([0, E0 - 1]), rng.permutation(np.arange(1, E0 - 1))[:len(ends) - 2]]))
    nb = np.full((V, K), -1); en = np.full((V, K), -1); nb[ends, slot] = ends[:, ::-1]; en[ends, slot] = name[:, None]
    return nb, en
def world(rng, make):
    pl = np.argsort(rng.random((N, 8, B)), axis=-1)
    got = [[place(rng, *make(q, g, pl[q - 1, g], pl[q, g])) for g in range(8)] for q in range(N)]
    return np.array([[h[0] for h in r] for r in got]), np.array([[h[1] for h in r] for r in got])
def seam(first, last, lo, hi):
    i = np.arange(lo, hi - 1)
    return np.concatenate([first[i], last[i] + V - B]), np.concatenate([first[i + 1], last[i + 1] + V - B])
def roads(rng, share, first, last):
    n = V - 2 * B; p = B + rng.permutation(n); t = rng.permutation(n); h = 3 * B // 4; i = 4 * np.arange(8); j = i + 33
    a = [last[i] + V - B, first[i], first[j], last[j] + V - B]; b = [last[i + 2], first[i + 2], first[j + 2] + V - B, last[j + 2] + V - B]
    for w in (first, last + V - B):
        for d, c in ((1, 0.85), (3, 0.5)):
            i = np.flatnonzero(rng.random(B - d) < c); a.append(w[i]); b.append(w[i + d])
    for s, w in enumerate((first, last + V - B)):
        c = p[t[s * h:(s + 1) * h]]; i = rng.permutation(B - 1)[:h]; a += [c, c]; b += [w[i], w[i + 1]]
    m = int(share * 1.3 * (E0 - len(np.concatenate(a)))); i = (n * rng.random(m) ** 1.5).astype(np.int64)
    a.append(p[i]); b.append(p[(i + rng.integers(1, 7, m)) % n])
    return a, b
def shares(rng):
    return np.stack([rng.permutation(np.repeat(np.array([0.25, 0.5, 0.75, 1.0]), 2)) for q in range(N)])
def tri(t):
    out = []; c = K
    while t > 0:
        while c * (c - 1) // 2 > t: c -= 1
        out.append(c); t -= c * (c - 1) // 2
    return out
def hubs(rng, iso, t, first, last):
    a, b = [], []; v = B + iso; use = [0, 0]
    for i, c in enumerate(tri(t)):
        s = i % 2
        if use[s] + c > B: s = 1 - s
        w = (first, last + V - B)[s][use[s]:use[s] + c]; use[s] += c
        a.append(np.full(len(w), v)); b.append(w); v += 1
    for i in range(CAP // 4):
        m = v + np.arange(5); a.append(m); b.append(np.roll(m, 1)); v += 5
    r = rng.permutation(np.arange(v, V - B)); r = r[:len(r) // 5 * 5].reshape(-1, 5); i, j = np.triu_indices(5, 1)
    a.append(r[:, i].reshape(-1)); b.append(r[:, j].reshape(-1)); x, y = seam(first, last, B - 8, B); a.append(x); b.append(y)
    return a, b
def fives(rng, n, first, last):
    a, b = [], []
    for i, c in enumerate(np.array_split(B + rng.permutation(V - 2 * B), n)):
        m = len(c)
        if i % 3 == 0: x, y = np.triu_indices(m, 1); a.append(c[x]); b.append(c[y])
        elif i % 3 == 1: a.append(np.full(m - 1, c[0])); b.append(c[1:])
        else: a.append(np.repeat(c[:2], m - 2)); b.append(np.tile(c[2:], 2))
        w = (first, last + V - B)[i % 2][i // 2 * 2:i // 2 * 2 + 2]; a.append(np.full(len(w), c[0])); b.append(w)
    x, y = seam(first, last, 0, B); a.append(x); b.append(y)
    return a, b
def full(rng, first, last):
    n = min((E0 - 2 * B) // (K * K), (V - 2 * B) // (2 * K)); p = (B + rng.permutation(n * 2 * K)).reshape(n, 2, K); x, y = seam(first, last, 0, B)
    return [np.repeat(p[:, 0], K, axis=1).reshape(-1), x], [np.tile(p[:, 1], (1, K)).reshape(-1), y]
def knots(rng):
    n = min(E0 // (K * (K + 1) // 2), (V - 2 * B) // (K + 1)); p = (B + rng.permutation(n * (K + 1))).reshape(n, K + 1); x, y = np.triu_indices(K + 1, 1)
    return [p[:, x].reshape(-1)], [p[:, y].reshape(-1)]
def stuffed(rng, first, last):
    h = B // K; n = min((E0 - 2 * h * K) // (K * (K + 1) // 2), (V - 2 * B - 2 * h) // (K + 1)); z = n * K; i = np.arange(z)
    c = B + rng.permutation(n); v = B + n + rng.permutation(2 * h); p = B + n + 2 * h + rng.permutation(z); w = np.concatenate([first[:h * K], last[:h * K] + V - B])
    a = [np.repeat(v, K), c[i % n], p[::2]]; b = [w, p, p[(i[::2] + K - 1) % z]]
    for d in range(1, K // 2): a.append(p); b.append(p[(i + d) % z])
    return a, b
def around(w):
    d = np.arange(1, K // 2 + 1)[:, None]; i = np.arange(B)[None, :]
    return np.tile(w, K // 2), w[(i + d) % B].reshape(-1)
def rims(rng, shift, first, last):
    r = B + rng.permutation(V - 2 * B); r = r[:len(r) // 5 * 5].reshape(-1, 5)
    x, y = around((first + shift) % B); s, t = around(last + V - B)
    return [x, s, r.reshape(-1)], [y, t, np.roll(r, 1, axis=1).reshape(-1)]
def small(rng, start, first, last):
    n = V - 2 * B; p = B + rng.permutation(n); i = np.arange(1, n); far = np.maximum(i - rng.integers(1, 4, n - 1), 0); on = rng.random(n - 1) >= start
    a, b = [p[i][on]], [p[far][on]]; x, y = seam(first, last, 0, B); a.append(x); b.append(y); h = B // 4; t = rng.permutation(n)
    for s, w in enumerate((first, last + V - B)):
        c = p[t[s * h:(s + 1) * h]]; a += [c, c]; b += [w[0:2 * h:2], w[1:2 * h:2]]
    return a, b
def which(nb, en):
    bl = np.full(V + 1, 2); bl[:B] = 0; bl[V - B:V] = 1; bl[V] = 3; own = bl[:V][None, None, :, None]
    q, g, v, k = np.nonzero((bl[nb] == own) & (own < 2)); m = np.full((N, 8, E0), -1); m[q, g, en[q, g, v, k]] = bl[v]
    return m[:, :, None, :]
def usual(rng, nb, en):
    v = np.clip(np.exp2(2 + 5.5 * rng.random((N, 8, 1, E0))) * (0.5 + rng.random((N, 8, 16, E0))), 1, 255).astype(np.int64)
    near = np.where(rng.random((1, 8, 1, 1)) < 0.5, rng.integers(15, 60, v.shape), 20 + 10 * rng.integers(0, 3, v.shape))
    return np.where(which(nb, en) >= 0, near, v)
def pack(v, nb, en):
    return {"lens": np.ascontiguousarray(v.reshape(N, 128, E0)).astype(np.float32).astype(BF), "en": np.stack([gtable(a.transpose(0, 2, 1).reshape(8, -1)) for a in en]),
            "nb": np.stack([gtable(a.transpose(0, 2, 1).reshape(8, -1)) for a in nb])}
def setup_inputs(rng):
    sh = shares(rng); nb, en = world(rng, lambda q, g, first, last: roads(rng, sh[q, g], first, last))
    return pack(usual(rng, nb, en), nb, en)
def setup_inputs_spread(rng):
    sh = shares(rng); nb, en = world(rng, lambda q, g, first, last: roads(rng, sh[q, g], first, last))
    return pack(np.clip(np.exp2(8 * rng.random((N, 8, 1, E0))) * rng.random((N, 8, 16, E0)), 1, 255).astype(np.int64), nb, en)
def setup_inputs_ends(rng):
    sh = shares(rng)
    def make(q, g, first, last):
        if g % 2:
            a, b = hubs(rng, CAP * (1 + (g // 2 + q + 1) % (RO - 1)), EC - CAP // 4 + 3 * len(JJ), first, last); far = [[0, V - 1]]
        else:
            a, b = roads(rng, sh[q, g], first, last); far = [[0, V - 1], [B, V - B - 1], [0, B], [V - 1, V - B - 1], [0, V - B - 1], [V - 1, B]]
        far = np.array(far); return [far[:, 0]] + a, [far[:, 1]] + b
    nb, en = world(rng, make); pr = rng.choice(np.array([0.0, 0.25, 0.75, 0.75, 0.9, 1.0]), (N, 8, 1, E0))
    return pack(np.where(rng.random((N, 8, 16, E0)) < pr, 1, 255), nb, en)
def setup_inputs_corners(rng):
    c4 = CAP // 4
    def make(q, g, first, last):
        c = (q + g) % 8
        if c < 4: return hubs(rng, 0, EC - c4 + (0, -1, 1, 3 * len(JJ))[c], first, last)
        if c == 4: return hubs(rng, CAP * (RO - 1), EC - c4, first, last)
        return fives(rng, CAP + (0, -1, 1)[c - 5], first, last)
    nb, en = world(rng, make)
    return pack(usual(rng, nb, en), nb, en)
def setup_inputs_crowd(rng):
    def make(q, g, first, last):
        if g >= 6: return rims(rng, g - 6, first, last)
        if g == 3: return stuffed(rng, first, last)
        if g == 4: return knots(rng)
        if g % 3 == 0: return full(rng, first, last)
        if g % 3 == 1: return fives(rng, CAP, first, last)
        return hubs(rng, 0, EC - CAP // 4 + 3 * len(JJ), first, last)
    nb, en = world(rng, make); w = which(nb, en); r = np.argsort(rng.random((1, 8, 16, 1)), axis=2)
    c = rng.choice(np.array([0, 1, 7, 8, 9, 10, 15, 16]), (N, 8, 1, E0))
    for q in range(0, N, 2):
        for s, k in ((q, 1), ((q + 1) % N, 0)):
            c[s, 6] = np.where(w[s, 6] == k, rng.integers(0, 2, (1, E0)) + 7 * int(k == 1 - q // 2 % 2), c[s, 6])
    side = 20 + (r < c)
    return pack(np.where((rng.random((N, 8, 1, E0)) < 0.5) & (w < 0), 10, side), nb, en)
def setup_inputs_calm(rng):
    st = np.stack([rng.permutation(np.array([0.05, 0.1, 0.15, 0.2, 0.25, 0.35, 0.5, 0.7])) for q in range(N)])
    nb, en = world(rng, lambda q, g, first, last: small(rng, st[q, g], first, last))
    return pack(rng.integers(1, 5, (N, 8, 16, E0)), nb, en)
def check_inputs(d):
    bad = []
    for k, lo, hi in (("lens", 1, 255), ("en", -1, E0 - 1), ("nb", -1, V - 1)):
        a = np.asarray(d[k]).astype(np.float64)
        if not (np.all(a >= lo) and np.all(a <= hi)): bad.append("range of " + k)
        elif not np.all(a == np.floor(a)): bad.append("whole numbers of " + k)
    if bad: return bad
    for q in range(N):
        nl = gentries(np.asarray(d["nb"][q])).astype(np.int64); el = gentries(np.asarray(d["en"][q])).astype(np.int64)
        for g in range(8):
            n, e = nl[g], el[g]; f = np.flatnonzero(e >= 0)
            if np.any((n >= 0) != (e >= 0)): bad.append("empty slots alike in en and nb"); continue
            v = f % V; u = n[f]; o = np.argsort(e[f], kind="stable"); s = e[f][o]
            if len(s) % 2 or np.any(s[0::2] != s[1::2]) or np.any(s[2::2] == s[1:-1:2]): bad.append("every edge in two slots"); continue
            a, b = o[0::2], o[1::2]
            if np.any(v[a] != u[b]) or np.any(v[b] != u[a]): bad.append("ends of an edge name each other")
            if np.any(v[a] == v[b]): bad.append("two different ends")
            if len(np.unique(np.minimum(v[a], v[b]) * V + np.maximum(v[a], v[b]))) != len(a): bad.append("no two edges between the same vertices")
    return sorted(set(bad))
def contract(nb, en, x, mid, live, t):
    me = np.arange(V); big = (K + 1) * V; deg = np.add.reduce((nb >= 0).astype(np.int64), axis=1)
    key = np.where(live & (me >= B) & (me < V - B), deg * V + me, big); m = key
    for hop in range(2): m = np.minimum(m, np.min(np.append(m, big)[nb], axis=1))
    go = np.flatnonzero((m == key) & (key < big))[:CAP]
    un, ue = nb[go], en[go]; u, w = un[:, JJ], un[:, KK]; ok = (u >= 0) & (w >= 0)
    z = np.minimum(x[:, ue[:, JJ]] + x[:, ue[:, KK]], 255)
    same = (nb[u] == w[..., None]) & ok[..., None]; has = np.any(same, axis=2); side = np.max(np.where(same, en[u], -1), axis=2)
    a, p = np.nonzero(has); zz = z[:, a, p]; e = side[a, p]; old = x[:, e]
    win = np.add.reduce((zz < old).astype(np.int64), axis=0) >= 9
    x[:, e] = np.minimum(zz, old); mid[e[win]] = go[a[win]]
    live[go] = False; dead = np.zeros(V + 1, bool); dead[go] = True; hit = dead[nb]
    nb[hit] = -1; en[hit] = -1; nb[go] = -1; en[go] = -1
    new = ok & ~has; s = np.zeros((len(go), K, K), np.int64); s[:, JJ, KK] = new; s[:, KK, JJ] = new
    before = np.add.accumulate(s, axis=2) - s; free = nb[un] < 0
    fits = before < np.add.reduce(free.astype(np.int64), axis=2)[..., None]
    given = np.take_along_axis(np.argsort(~free, axis=2, kind="stable"), before, 2)
    a, p = np.nonzero(new & fits[:, JJ, KK] & fits[:, KK, JJ]); a, p = a[:EC], p[:EC]; j, k = JJ[p], KK[p]; e = E0 + EC * t + np.arange(len(a))
    x[:, e] = z[:, a, p]; mid[e] = go[a]
    u, w = un[a, j], un[a, k]; nb[u, given[a, j, k]] = w; en[u, given[a, j, k]] = e; nb[w, given[a, k, j]] = u; en[w, given[a, k, j]] = e
def meet(nr, er, xr, ns, es, xs):
    far = nr[V - B:] - (V - B); same = (far[:, :, None] == ns[:B][:, None, :]) & (far >= 0)[:, :, None]
    a, l, m = np.nonzero(same); e = er[V - B + a, l]; f = es[a, m]; p = xr[:, e]; o = xs[:, f]
    xr[:, e] = np.minimum(p, o); xs[:, f] = np.minimum(p, o)
    c = np.add.reduce((p > o).astype(np.int64), axis=0) >= 9; nr[V - B + a[c], l[c]] = -1; er[V - B + a[c], l[c]] = -1
    c = np.add.reduce((o > p).astype(np.int64), axis=0) >= 9; ns[a[c], m[c]] = -1; es[a[c], m[c]] = -1
def reference(lens, en, nb):
    fn = np.ascontiguousarray(np.stack([gentries(a) for a in nb]).astype(np.int64).reshape(N, 8, K, V).transpose(0, 1, 3, 2))
    fe = np.ascontiguousarray(np.stack([gentries(a) for a in en]).astype(np.int64).reshape(N, 8, K, V).transpose(0, 1, 3, 2))
    x = np.zeros((N, 8, 16, E), np.int64); x[..., :E0] = lens.astype(np.float32).astype(np.int64).reshape(N, 8, 16, E0)
    mid = np.full((N, 8, E), -1, np.int64); live = np.ones((N, 8, V), bool)
    for t in range(RO):
        for q in range(N):
            for g in range(8): contract(fn[q, g], fe[q, g], x[q, g], mid[q, g], live[q, g], t)
        for q in range(N):
            s = (q + 1) % N
            for g in range(8): meet(fn[q, g], fe[q, g], x[q, g], fn[s, g], fe[s, g], x[s, g])
    return {"ylen": x.reshape(N, 128, E).astype(np.float32).astype(BF), "ymid": mid.astype(np.float32),
            "yen": fe.transpose(0, 1, 3, 2).reshape(N, 8, K * V).astype(np.float32), "ynb": fn.transpose(0, 1, 3, 2).reshape(N, 8, K * V).astype(np.float32)}

@@ -1,0 +1,920 @@
+import numpy as np
+from concourse.mybir import dt, AluOpType, AxisListType, ActivationFunctionType
+
+AL = AluOpType
+AF = ActivationFunctionType
+ADD, SUB, MUL, MAX, MIN = AL.add, AL.subtract, AL.mult, AL.max, AL.min
+GE, GT, LE, LT, EQ, NE = AL.is_ge, AL.is_gt, AL.is_le, AL.is_lt, AL.is_equal, AL.not_equal
+AND, SHR = AL.bitwise_and, AL.arith_shift_right
+MAGIC = 1.5 * 2.0 ** 36
+U13 = 2.0 ** -13
+ALL = slice(None)
+
+SHAPES = {}
+POOL = {"f": ["float32", 0, 4], "b": ["bfloat16", 0, 2], "h": ["float16", 0, 2], "i": ["int32", 0, 4], "u": ["uint16", 0, 2]}
+OPS = []
+SEMS = ["ev", "es", "et", "eg"]
+
+
+SCOPE, SEEN, DBG = [None, 0], {}, {}
+
+
+def al(kind, n):
+    if SCOPE[0] is not None:
+        key = (SCOPE[0], SCOPE[1])
+        SCOPE[1] += 1
+        if key not in SEEN:
+            SCOPE[0] = None
+            SEEN[key] = al(kind, n)
+            SCOPE[0] = key[0]
+        return SEEN[key]
+    p = POOL[kind]
+    o = p[1]
+    p[1] = o + (n + 15) // 16 * 16
+    return ("p" + kind, o, n)
+
+
+def own(name, where, shape, dtype):
+    SHAPES[name] = (where, shape, dtype)
+    return name
+
+
+def A(b, lo=0, hi=None, st=1, p=None):
+    if isinstance(b, str):
+        b = (b, 0, SHAPES[b][1][1])
+    hi = b[2] if hi is None else hi
+    n = (hi - lo + st - 1) // st
+    rows = ALL if p is None else slice(*p)
+    return (b[0], (rows, slice(b[1] + lo, b[1] + lo + (n - 1) * st + 1, st)), b[1] + lo, b[1] + lo + (n - 1) * st, n, None)
+
+
+def A3(name, s1=ALL, s2=ALL):
+    sh = SHAPES[name][1]
+    ix = np.arange(sh[1] * sh[2]).reshape(sh[1], sh[2])[s1, s2]
+    return (name, (ALL, s1, s2), int(ix.min()), int(ix.max()), int(ix.size), None)
+
+
+def IND(win, off):
+    return win[:4] + (16 * off[4], off)
+
+
+def X(name, *ix):
+    return (name, ix, 0, 1 << 30, 0, None)
+
+
+def real(T, ap):
+    if not isinstance(ap, tuple):
+        return ap
+    r = T[ap[0]][ap[1]]
+    return r if ap[5] is None else r.indirect(real(T, ap[5]))
+
+
+def two(ap):
+    return ap[0] in ("pb", "ph", "pu") or (ap[0] in SHAPES and SHAPES[ap[0]][2] in ("bfloat16", "float16", "uint16"))
+
+
+def flt(ap):
+    return ap[0] in ("pf", "pb") or (ap[0] in SHAPES and SHAPES[ap[0]][2] in ("bfloat16", "float32"))
+
+
+def psum(ap):
+    return ap[0] in SHAPES and SHAPES[ap[0]][0] == "psum"
+
+
+def op(alts, outs, ins, **kw):
+    rd, wr = [], []
+    reg = lambda ap: ap[0:1] + ap[2:4] + (ap[1][1].step if len(ap[1]) == 2 and isinstance(ap[1][1], slice) and ap[1][1].step else 1,)
+    for ap in ins:
+        if isinstance(ap, tuple):
+            rd.append(reg(ap))
+            if ap[5] is not None:
+                rd.append(reg(ap[5]))
+    for ap in outs:
+        wr.append(reg(ap))
+        if ap[5] is not None:
+            rd.append(reg(ap[5]))
+    OPS.append(dict(alts=alts, rd=rd, wr=wr, **kw))
+
+
+def vcost(out, ins, tt=False):
+    n = out[4]
+    if out[5] is not None:
+        return 60 + 3.8 * n
+    if ins[0][5] is not None:
+        return 60 + 1.5 * n
+    if tt:
+        return max(64, n * (1 if psum(ins[0]) or psum(ins[1]) else 2))
+    return max(64, n * (0.5 if two(out) and two(ins[0]) else 1))
+
+
+def ts(out, in0, s1, o0, s2=None, o1=None):
+    def f(g, T):
+        if o1 is None:
+            return g.vector.tensor_scalar(real(T, out), real(T, in0), real(T, s1), None, o0)
+        return g.vector.tensor_scalar(real(T, out), real(T, in0), real(T, s1), real(T, s2), o0, o1)
+    alts = [("v", f, vcost(out, [in0]))]
+    if flt(out) and flt(in0) and not any(isinstance(s, tuple) and psum(s) for s in (s1, s2)):
+        if o1 is None and o0 in (MUL, ADD):
+            alts.append(act_alt(out, in0, AF.Identity, s1 if o0 == ADD else 0.0, s1 if o0 == MUL else 1.0, None))
+        elif o0 == MUL and o1 == ADD:
+            alts.append(act_alt(out, in0, AF.Identity, s2, s1, None))
+    op(alts, [out], [in0, s1, s2])
+
+
+def tt(out, in0, in1, o):
+    op([("v", lambda g, T: g.vector.tensor_tensor(real(T, out), real(T, in0), real(T, in1), o), vcost(out, [in0, in1], True))], [out], [in0, in1])
+
+
+def act_alt(out, in_, func, bias, scale, acc):
+    def f(g, T):
+        if acc is None:
+            return g.scalar.activation(real(T, out), real(T, in_), func, bias=real(T, bias), scale=real(T, scale))
+        return g.scalar.activation(real(T, out), real(T, in_), func, bias=real(T, bias), scale=real(T, scale), accum_out=real(T, acc))
+    return ("s", f, 80 + 1.5 * out[4] if in_[5] is not None else max(64, out[4]) + 30)
+
+
+def act(out, in_, func=None, bias=0.0, scale=1.0, acc=None):
+    op([act_alt(out, in_, func or AF.Identity, bias, scale, acc)], [out] + ([acc] if acc else []), [in_, bias, scale])
+
+
+def cp(out, in_, on="v"):
+    alts = []
+    if "v" in on:
+        alts.append(("v", lambda g, T: g.vector.tensor_copy(real(T, out), real(T, in_)), vcost(out, [in_])))
+    if flt(out) and flt(in_) and out[5] is None:
+        alts.append(act_alt(out, in_, AF.Copy, 0.0, 1.0, None))
+    op(alts, [out], [in_])
+
+
+def lin(out, in_, scale, bias, on="vs"):
+    alts = []
+    if "v" in on:
+        alts.append(("v", lambda g, T: g.vector.tensor_scalar(real(T, out), real(T, in_), real(T, scale), real(T, bias), MUL, ADD), vcost(out, [in_])))
+    if flt(out) and flt(in_):
+        alts.append(act_alt(out, in_, AF.Identity, bias, scale, None))
+    op(alts, [out], [in_, scale, bias])
+
+
+def ms(out, c):
+    op([("v", lambda g, T: g.vector.memset(real(T, out), c), max(40, out[4] * (0.5 if two(out) else 1)))], [out], [])
+
+
+def scan(out, d0, d1, o0, o1):
+    op([("v", lambda g, T: g.vector.tensor_tensor_scan(real(T, out), real(T, d0), real(T, d1), 0.0, o0, o1), vcost(out, [d1]))], [out], [d0, d1])
+
+
+def tr(out, in_):
+    op([("v", lambda g, T: g.vector.transpose(real(T, out), real(T, in_)), vcost(out, [in_]))], [out], [in_])
+
+
+def mm(parts):
+    def f(g, T):
+        r = None
+        for o, l, x, s, e in parts:
+            r = g.tensor.matmul(real(T, o), real(T, l), real(T, x), s, e)
+        return r
+    c = sum(max(64, x[4]) * (1 if two(x) else 4) * PEC for o, l, x, s, e in parts)
+    op([("t", f, c + 60)], [q[0] for q in parts], [q[1] for q in parts] + [q[2] for q in parts])
+
+
+def acc(out, pairs):
+    return [(out, l, x, i == 0, i == len(pairs) - 1) for i, (l, x) in enumerate(pairs)]
+
+
+def iota(out, pat, base, cm=0):
+    def f(g, T):
+        if out[0] == "pi" or SHAPES.get(out[0], "  i")[2] == "int32":
+            return g.iota(real(T, out), pat, base, cm)
+        return g.iota(real(T, out), pat, base, cm, allow_small_or_imprecise_dtypes=True)
+    op([("g", f, 160 + 2 * out[4])], [out], [])
+
+
+def asel(out, cmp, fill, base, cm):
+    op([("g", lambda g, T: g.affine_select(real(T, out), real(T, out), [[0, 1]], cmp, fill, base, cm), 205)], [out], [out])
+
+
+def dma(out, in_, q="y", lat=2600):
+    s = "d%d" % len(SEMS)
+    SEMS.append(s)
+
+    def f(g, T):
+        e = g.sync if q == "y" else g.scalar if q == "s" else g
+        return e.dma_start(real(T, out), real(T, in_))
+    op([(q, f, 1200 if q == "g" else 100)], [out], [in_], sem=s, inc=16, lat=lat)
+
+
+def send(dst, src, step, lat):
+    k = len(SEMS)
+    SEMS.extend(["l%d" % k, "r%d" % k])
+    op([("g", None, 600)], [], [src], sem="l%d" % k, send=(dst, src, step, "r%d" % k), lat=lat)
+    op([("n", None, 0)], [dst], [], sem="r%d" % k, step=step, after=len(OPS) - 1, lat=0)
+
+
+PEC = 0.6
+
+
+def program():
+    f, b, h, ii, u = (lambda n: al("f", n)), (lambda n: al("b", n)), (lambda n: al("h", n)), (lambda n: al("i", n)), (lambda n: al("u", n))
+    B = [own("B%d" % k, "psum", [128, 512], "float32") for k in range(6)]
+    C = own("C", "psum", [128, 1024], "float32")
+    DD, CC = f(3168), h(3168)
+    SEL = own("SEL", "sbuf", [128, 16, 144], "bfloat16")
+    BL = own("BL", "sbuf", [128, 12, 128], "bfloat16")
+    L1, R2 = u(480), f(128)
+    UD = own("UD", "sbuf", [128, 66, 3], "float32")
+    UL, DL, J3, K3 = (own(n, "sbuf", [128, 3, 66], "float32") for n in ("UL", "DL", "J3", "K3"))
+    XL = own("XL", "sbuf", [128, 4032], "bfloat16")
+    XW = [ii(1040), ii(1040)]
+    EN, NB = XW[0][:2] + (480,), (XW[0][0], XW[0][1] + 480, 480)
+    UW = own("UW", "sbuf", [128, 8704], "bfloat16")
+    MW = own("MW", "sbuf", [128, 8928], "bfloat16")
+    col = lambda t, k: A(t, k, k + 1)
+    Z = lambda z, t: A(z, 15 - t, 143 - t)
+
+    def ext(out, z, src, n, lo=0):
+        return [(Z(z, i), A(src, lo + i, lo + 16 * n, 16)) for i in range(16)]
+
+    dma(A(NB), X("nb", ALL, ALL), "y")
+    dma(A(EN), X("en", ALL, ALL), "s")
+    dma(A(XL, 0, 2048), X("lens", ALL, ALL), "y", 4000)
+    PI, PJ = ii(4), f(8)
+    iota(col(PI, 0), [[0, 1]], 0, 1)
+    X16, XG, XZ = f(128), f(128), f(144)
+    iota(A(X16), [[0, 8], [1, 16]], 0)
+    iota(A(XZ), [[1, 144]], -15)
+    iota(A(XG), [[1, 8], [0, 16]], 0)
+    J, JH = f(208), f(64)
+    iota(A(J), [[16, 208]], 0)
+    ts(col(PI, 1), col(PI, 0), 15, AND)
+    ts(col(PI, 2), col(PI, 0), 4, SHR)
+    ts(col(PI, 3), col(PI, 2), 1, AND)
+    cp(A(PJ, 0, 4), A(PI))
+    PM, PG, PH, G16 = col(PJ, 1), col(PJ, 2), col(PJ, 3), col(PJ, 4)
+    ts(G16, PG, 16.0, MUL)
+    ts(A(J), A(J), PM, ADD)
+    lin(A(JH), A(J, 0, 64), 1.0, 0.5, "v")
+    OH, ZB, BD, ID = f(128), b(144), b(128), b(128)
+    ts(A(OH), A(X16), PM, EQ)
+    ts(A(ZB), A(XZ), G16, EQ)
+    ts(A(BD), A(XG), PG, EQ)
+    ts(A(ID), A(XZ, 15, 143), col(PJ, 0), EQ)
+    early = [("key", [1024] * 12 + [128, 32, 1, -229376]), ("fs", [1] * 13 + [U13, 1, 1]), ("fc", [1] * 12 + [4096] * 4),
+             ("pd", [0] * 12 + [1920, 22 * 8192 + 3072, 0, 1]), ("fd", [0] * 12 + [1920, 22.375, 0, 1]),
+             ("dg", [1] * 12 + [1 / 128, 0, 0, -13])]
+    late = [("vb", {13: 262144, 14: 8192, 15: -90112}), ("got", {13: 32, 14: 1, 15: -12}), ("wa", {0: 1, 1: 16, 2: 48}),
+            ("wb", {0: 1, 1: 16, 3: 48}), ("sa", {1: 192, 2: 16, 3: 1}), ("sb", {1: 192, 2: 1, 3: 16}),
+            ("upd", {12: 1, 13: 262144, 14: 8192, 15: 32}), ("nmc", {12: 1, 13: -0.375, 14: 1, 15: 63})]
+    W16, WC, W = f(16), f(32), {}
+    for k, (n, w) in enumerate(early):
+        for r in range(16, 0, -1):
+            if r == 16 or w[r - 1] != w[r]:
+                ms(A(W16, k, k + 1, p=(0, r)), float(w[r - 1]))
+        W[n] = col(WC, k)
+    mm([(A(B[2], 0, 6), A(OH, p=(0, 16)), A(W16, 0, 6, p=(0, 16)), True, True)])
+    cp(A(WC, 0, 6), A(B[2], 0, 6))
+    ms(A(W16, 8, 16, p=(0, 16)), 0.0)
+    for e in range(4):
+        for k, (n, w) in enumerate(late):
+            if e < len(w):
+                r = sorted(w)[e]
+                asel(A(W16, 8 + k, 9 + k, p=(0, 16)), NE, float(w[r]), -r, 1)
+            W[n] = col(WC, 8 + k)
+    mm([(A(B[5], 0, 8), A(OH, p=(0, 16)), A(W16, 8, 16, p=(0, 16)), True, True)])
+    cp(A(WC, 8, 16), A(B[5], 0, 8))
+    for k, (n, o, v, w) in enumerate([("s01", LT, 2, 1), ("o14", LT, 14, 1), ("w640", LT, 12, -320), ("l12", LT, 12, 1),
+                                      ("cm", GE, 12, 1), ("cx", EQ, 12, 1920), ("ps", GE, 13, 1), ("n15", LT, 15, 1), ("m12", LT, 12, -1)]):
+        W[n] = col(WC, 16 + k)
+        ts(W[n], PM, float(v), o, float(w), MUL)
+    W["uba"], W["wu"] = col(WC, 26), col(WC, 27)
+    tt(W["uba"], W["vb"], W["n15"], MUL)
+    tt(W["wu"], W["got"], W["n15"], MUL)
+
+    def zt(n, kind="b"):
+        z = al(kind, 144)
+        lin(A(z), A(ZB), W[n], 0.0, "v" if kind == "h" else "vs")
+        return z
+
+    def bt(n, src=BD):
+        z = b(128)
+        lin(A(z), A(src), W[n], 0.0)
+        return A(z)
+    ZKEY = zt("key")
+    BKEY, BDG, BS01, BVB, BGOT, PAS = bt("key"), bt("dg"), bt("s01"), bt("vb"), None, bt("ps", ID)
+    Z14, ZL12, ZA, ZBB, ZSA, ZSB, Z640, ZU, ZUP = zt("o14", "h"), zt("l12"), zt("wa"), zt("wb"), zt("sa"), zt("sb"), zt("w640"), zt("wu"), zt("upd")
+    for i in range(16):
+        lin(A3(SEL, i), A(ZB), col(OH, i), 0.0)
+    for i in range(12):
+        lin(A3(BL, i), A(BD), col(OH, i), 0.0)
+    PERM, pc = f(96), f(2)
+    ts(col(pc, 0), PG, -4.0, MUL, col(PJ, 0), ADD)
+    ts(col(pc, 1), W["cx"], col(pc, 0), ADD)
+    ts(col(pc, 0), W["ps"], 1920.0, MUL, col(pc, 1), ADD)
+    ts(A(PERM), A(XZ, 15, 111), col(pc, 0), EQ)
+    Z0F = f(144)
+    lin(A(Z0F), A(ZB), col(OH, 0), 0.0)
+    TS, SFX, NBD, UBM, t1, t2 = b(128), b(128), b(128), b(128), f(128), f(128)
+    ts(A(t1), A(X16), PM, GT)
+    tt(A(TS), A(t1), A(BD), MUL)
+    t3 = f(128)
+    ts(A(t3), A(X16), PM, LT, W["m12"], MUL)
+    tt(A(SFX), A(t3), A(BD), MUL)
+    lin(A(NBD), A(BD), -1.0, 0.0)
+    ms(A(R2), -88064.0)
+    ms(A(R2, 12, 128, 16), -716.0 * 8192)
+    ms(A(R2, 13, 128, 16), 182272.0)
+    t4, t5 = f(128), f(128)
+    ts(A(t2), A(X16), 13.0, LT, W["uba"], MUL)
+    lin(A(t4), A(R2), col(OH, 15), 0.0)
+    tt(A(t5), A(t2), A(t4), ADD)
+    tt(A(UBM), A(t5), A(BD), MUL)
+    ZT, ONE = b(1024), b(512)
+    ms(A(ZT), 0.0)
+
+    def fl(out, c):
+        ms(out, c)
+        z = A(ZT, 0, out[4])
+        OPS[-1]["alts"].append(act_alt(out, z, AF.Identity, c, 1.0, None))
+        OPS[-1]["rd"].append(z[0:1] + z[2:4] + (1,))
+    fl(A(ONE), 1.0)
+    M3, M4, NID = b(512), b(512), b(128)
+    fl(A(M3), 9.0)
+    fl(A(M4), 10.0)
+    fl(A(XL, 2048, 3072), 255.0)
+    fl(A(XL, 3072, 4032), 255.0)
+    lin(A(NID), A(ID), -1.0, 0.0)
+    P, F, W2, Y, PFU, ST, WW, RR = f(1280), b(1280), b(656), b(656), b(656), f(592), f(256), ii(208)
+    lin(A(P, 0, 16), A(ZT, 0, 16), 1.0, W["pd"])
+    lin(A(P, 656, 1280), A(ZT, 0, 624), 1.0, W["pd"], "s")
+    lin(A(F, 0, 16), A(ZT, 0, 16), 1.0, W["fd"])
+    lin(A(F, 656, 1280), A(ZT, 0, 624), 1.0, W["fd"])
+    ms(A(W2, 0, 16), 0.0)
+    ms(A(Y, 576, 624), 255.0)
+    ms(A(Y, 624, 656), 0.0)
+    ms(A(PFU, 576, 656), 0.0)
+    ms(A(ST, 576, 592), 0.0)
+    GR, LGT, gi, gc_, gf = f(96), u(4), ii(3), f(3), f(3)
+    ms(A(GR), 0.0)
+    ts(A(gi), A(J, 0, 3), 1 / 3, MUL, -1 / 3, ADD)
+    ts(A(gc_), A(gi), -3.0, MUL)
+    tt(A(gc_), A(gc_), A(J, 0, 3), ADD)
+    ts(A(gf), A(gc_), 16.0, MUL)
+    tt(A(gf), A(gf), A(gi), ADD)
+    ts(A(gi), A(gc_), PH, ADD)
+    ts(A(gi), A(gi), 1, AND)
+    ts(A(gc_), A(gi), 80.0, MUL)
+    tt(A(gf), A(gf), A(gc_), ADD)
+    cp(A(LGT, 0, 3), A(gf))
+    ms(A(WW, 192, 256), 0.0)
+    ms(A(RR, 192, 208), 0)
+
+    def clear():
+        for k in range(8):
+            dma(A(UW, 960 * k, 960 * (k + 1)), A(ZT, 0, 960), "y", 5000)
+
+    def fill(t):
+        for k in range(5 + t):
+            dma(A(MW, 512 * k, 512 * (k + 1)), A(M3 if k < 4 + t else M4), "y", 4000)
+    fill(0)
+    CI, CE, CF, LVS = ii(40), ii(40), f(40), u(40)
+    iota(A(CI), [[1, 40]], 0)
+    ts(A(CE), A(CI), PH, ADD)
+    ts(A(CE), A(CE), 1, AND)
+    ts(A(CF), A(CE), 656.0, MUL)
+    tt(A(CF), A(CF), A(J, 0, 40), ADD)
+    cp(A(LVS), A(CF))
+    KI, KC, KE, KF, LSV = ii(30), f(30), ii(30), f(30), u(30)
+    ts(A(KI), A(J, 0, 30), 1 / 40, MUL, -0.4875, ADD)
+    ts(A(KC), A(KI), -40.0, MUL)
+    tt(A(KC), A(KC), A(J, 0, 30), ADD)
+    ts(A(KE), A(KC), PH, ADD)
+    ts(A(KE), A(KE), 1, AND)
+    ts(A(KF), A(KE), 41.0, MUL)
+    tt(A(KF), A(KF), A(KC), ADD)
+    ts(A(KF), A(KF), 16.0, MUL)
+    tt(A(KF), A(KF), A(KI), ADD)
+    cp(A(LSV), A(KF))
+    TIN, TT, NX, VI, VH = f(672), f(1312), f(480), ii(40), ii(40)
+    ms(A(TIN, 0, 16), 0.0)
+    ms(A(TIN, 656, 672), 0.0)
+    ms(A(TIN, 28, 28 + 80, 16), 1920.0)
+    ms(A(TIN, 28 + 80, 28 + 560, 16), 1792.0)
+    ms(A(TIN, 28 + 560, 656, 16), 1920.0)
+    ms(A(TIN, 31, 656, 16), 1.0)
+    cp(A(VI), A(J, 0, 40))
+    ts(A(VH), A(VI), 5, SHR)
+    ts(A(TIN, 29, 656, 16), A(VH), 8192.0, MUL, 3072.0, ADD)
+    ts(A(VI), A(VI), 31, AND)
+    cp(A(TIN, 30, 656, 16), A(VI))
+    ts(A(L1), A(NB), 16.0, ADD)
+    lin(A(NX), A(NB), 8192.0, 8193.0, "v")
+    for k in range(12):
+        tt(A(TIN, 16 + k, 656, 16), A(NX, 40 * k, 40 * k + 40), A(EN, 40 * k, 40 * k + 40), ADD)
+    tr(A(TT, 0, 640), A(TIN, 16, 656))
+    tr(A(TT, 640, 1312), A(TIN))
+    cp(A(P, 16, 656), IND(A(TT), A(LVS)), "vs")
+    off = [0]
+    for d in range(1, 12):
+        off.append(off[-1] + 12 - d)
+    lex = [0]
+    for j in range(11):
+        lex.append(lex[-1] + 11 - j)
+    for d in range(1, 12):
+        iota(A3(UD, slice(off[d - 1], off[d])), [[17, 12 - d], [192, 3]], d + 1)
+    for j in range(11):
+        iota(A3(UL, ALL, slice(lex[j], lex[j + 1])), [[192, 3], [1, 11 - j]], 17 * j + 2)
+        iota(A3(DL, ALL, slice(lex[j], lex[j + 1])), [[192, 3], [16, 11 - j]], 17 * j + 17)
+        iota(A3(J3, ALL, slice(lex[j], lex[j + 1])), [[0, 3], [0, 11 - j]], j)
+        iota(A3(K3, ALL, slice(lex[j], lex[j + 1])), [[0, 3], [1, 11 - j]], j + 1)
+    YM = f(3072)
+    sub = lambda o, n: (YM[0], YM[1] + o, n)
+    R3, E2, CR, KK, JJ = sub(0, 624), sub(624, 208), b(198), b(198), b(198)
+    iota(A(E2), [[1, 208]], 0)
+    iota(A(CR), [[1, 3], [0, 66]], 0)
+    for k in range(3):
+        lin(A(R3, 208 * k + 198, 208 * k + 208), A(E2, 0, 10), 1.0, 576.0)
+        cp(A(R3, 208 * k, 208 * k + 198), A3((UD, UL, DL)[k]), "vs")
+    cp(A(JJ), A3(J3), "vs")
+    cp(A(KK), A3(K3), "vs")
+    parts = acc(A(B[5], 0, 39), ext(None, Z0F, R3, 39))
+    for k in range(0, 16, 4):
+        mm(parts[k:k + 4])
+    LUD, LUP, LDN, LEX, LSQ = u(14), u(14), u(14), u(14), u(36)
+    for k, l in enumerate((LUD, LUP, LDN)):
+        cp(A(l, 0, 13), A(B[5], 13 * k, 13 * k + 13))
+    S1, S2, SX = sub(1248, 592), sub(1840, 592), sub(2432, 208)
+    fl(A(S1), 198.0)
+    fl(A(S2), 198.0)
+    iota(A(S2, 0, 576, 16), [[1, 3], [3, 12]], 200)
+    cp(IND(A(S1), A(LUD, 0, 13)), A(E2))
+    cp(IND(A(S2), A(LUP, 0, 13)), A(E2))
+    cp(IND(A(S2), A(LDN, 0, 13)), A(E2))
+    cp(A(SX), IND(A(S1), A(LUP, 0, 13)))
+    parts = acc(A(B[5], 0, 13), ext(None, Z0F, SX, 13)) + acc(A(B[5], 16, 52), ext(None, Z0F, S2, 36))
+    for k in range(0, 32, 4):
+        mm(parts[k:k + 4])
+    cp(A(LEX, 0, 13), A(B[5], 0, 13))
+    cp(A(LSQ), A(B[5], 16, 52))
+    DG, SD, OI = f(198), b(3168), f(16)
+    mm(acc(A(B[5], 0, 198), [(A3(SEL, 0, slice(14, 142)), A(CR)), (A3(SEL, 0, slice(13, 141)), A(JJ)), (A3(SEL, 0, slice(12, 140)), A(KK))]))
+    cp(A(DG), A(B[5], 0, 198), "vs")
+    lin(A(OI), A(X16, 0, 16), col(OH, 0), 0.0)
+    for i in range(16):
+        lin(A(SD, i, 3168, 16), A(DG), 1.0, col(OI, i))
+    RS1, RS2 = f(576), f(198)
+    fl(A(RS1), 1.0)
+    ms(A(RS1, 0, 576, 16), 0.0)
+    fl(A(RS2), 1.0)
+    ms(A(RS2, 0, 198, 66), 0.0)
+    N1, N2, NM = b(512), b(512), [b(512), b(512)]
+    iota(A(N1), [[0, 16], [1, 32]], 0)
+    iota(A(N2), [[1, 16], [0, 32]], 0)
+    lin(A(N1), A(N1), col(OH, 12), W["nmc"])
+    lin(A(N2), A(N2), col(OH, 15), 0.0)
+    mm(acc(A(B[5]), [(A(ID), A(N1)), (A(ID), A(N2))]))
+    cp(A(NM[0]), A(B[5]), "vs")
+    O16 = f(1)
+    ts(A(O16), col(OH, 15), 16.0, MUL)
+    lin(A(NM[1]), A(NM[0]), 1.0, A(O16))
+    JG, JU, JM, JP, JQ = f(3), f(36), f(198), f(64), f(64)
+    for t, n, m, c in ((JG, 3, 1.0, 656.0), (JU, 36, 8192.0, 641.0 * 8192), (JM, 198, 1.0, 5760.0), (JP, 64, 1.0, 7681.0), (JQ, 64, 1.0, 3852.0)):
+        lin(A(t), A(J, 0, n), m, c)
+    MID, GOT = f(192), f(1200)
+    fl(A(MID), 0.0)
+    ms(A(GOT, 0, 16), -1.0)
+    ms(A(GOT, 592, 608), -1.0)
+    ms(A(GOT, 1184, 1200), -1.0)
+
+    RH, PV = UW, NX
+    GA, GB, LTT = b(3072), b(3072), (MW, 5760, 3072)
+
+    def choose(t):
+        SCOPE[:] = ["a", 0]
+        ts(A(F, 16, 656), A(P, 16, 656), W["fs"], MUL, W["fc"], MIN)
+        KV, E, DS, AC, M1, HL = f(40), f(480), f(480), f(120), f(40), b(80)
+        mm(acc(A(B[2], 0, 40), ext(None, ZKEY, F, 40, 16)))
+        cp(A(KV), A(B[2], 0, 40), "vs")
+        mm([(A(B[2], 0, 480), BDG, A(F, 96, 576), True, True)])
+        cp(A(DS), A(B[2], 0, 480), "vs")
+        mm([(A(B[2], 0, 480), BKEY, A(F, 96, 576), True, True)])
+        tt(A(E), A(B[2], 0, 480), A(DS), MUL)
+        for c in range(4):
+            for s in range(3):
+                k = 3 * c + s
+                l = A(L1, 40 * k, 40 * k + 40)
+                cp(A(RH, 640 * k, 640 * k + 640), IND(A(F, 0, 656), l), "vs")
+            mm(acc(A(B[c % 2], 0, 120), ext(None, ZKEY, RH, 120, 1920 * c)))
+            if c == 0:
+                cp(A(AC), A(B[0], 0, 120))
+            else:
+                tt(A(AC), A(B[c % 2], 0, 120), A(AC), MIN)
+        tt(A(KV), A(KV), A(AC, 0, 40), MIN)
+        tt(A(M1), A(AC, 40, 80), A(AC, 80, 120), MIN)
+        tt(A(M1), A(M1), A(KV), MIN)
+        cp(A(HL, 0, 40), A(M1))
+        tt(A(HL, 40, 80), A(M1), A(HL, 0, 40), SUB)
+        for k, (c0, c1) in enumerate(((0, 20), (20, 40))):
+            parts = []
+            for i in range(16):
+                parts += acc(A(B[k], i, 320, 16), [(A3(SEL, i, slice(15, 143)), A(HL, c0, c1)), (A3(SEL, i, slice(14, 142)), A(HL, 40 + c0, 40 + c1))])
+            mm(parts)
+            cp(A(W2, 16 + 16 * c0, 16 + 16 * c1), A(B[k], 0, 320), "vs")
+        for k in range(12):
+            cp(A(RH, 496 * k, 496 * k + 496), IND(A(W2), A(L1, 40 * k + 4, 40 * k + 35)), "vs")
+            mm([(A(B[0], 0, 480), BS01, A(W2, 96, 576), True, False)] * (k == 0) + [(A(B[0], 0, 480), BS01, A(RH, 496 * k + 16, 496 * k + 496), False, k == 11)])
+        CH, PR, JK_, GN, G2, LG = b(480), f(480), None, f(3), f(3), u(4)
+        tt(A(CH), A(B[0], 0, 480), A(E), EQ)
+        scan(A(PR), A(ONE, 0, 480), A(CH), MUL, ADD)
+        for c in range(3):
+            act(A(RH, 6000 + 480 * c, 6480 + 480 * c), A(PR), AF.Sign, col(JH, c), -1.0, col(GN, c))
+        ts(A(G2), A(GN), 480.0, EQ)
+        tt(A(G2), A(G2), A(JG), MUL)
+        ts(A(GN), A(GN), 0.5, MUL, 336.0, ADD)
+        tt(A(GN), A(GN), A(G2), ADD)
+        cp(A(LG, 0, 3), A(GN))
+        clear()
+        return A(LG, 0, 3)
+
+    def contract(t, LG):
+        n, n0 = 2560 + 512 * t, 2048 + 512 * t
+        nc = n // 16
+        SCOPE[:] = ["b", 0]
+        GT2, GV, FG, U1, U2, GH, GC, LU, LE_, FU = f(128), f(48), b(48), f(36), f(36), f(36), f(48), u(36), u(36), b(576)
+        NR, NH, NK, FRE, VS = f(576), f(576), f(576), b(576), f(48)
+        cp(A(GR, 16, 64), IND(A(P), LG))
+        cp(A(FG), IND(A(F), LG), "s")
+        tr(A(GT2, 0, 64), A(GR, 16, 80))
+        tr(A(GT2, 64, 128), A(GR, 0, 64))
+        cp(A(GV), IND(A(GT2), A(LGT, 0, 3)))
+        ts(A(U2), A(GV, 0, 36), 1.0, LT)
+        tt(A(U2), A(U2), A(JU), MUL)
+        tt(A(U1), A(GV, 0, 36), A(U2), ADD)
+        ts(A(LU), A(U1), U13, MUL, 15.0, ADD)
+        cp(A(NR), IND(A(P), A(LU)))
+        cp(A(FU), IND(A(F), A(LU)), "s")
+        ts(A(GH), A(GV, 0, 36), MAGIC, ADD, MAGIC, SUB)
+        tt(A(GH), A(GV, 0, 36), A(GH), SUB)
+        ts(A(LE_), A(GH), -1.0, ADD)
+        cp(A(Y, 0, 576), IND(A(XL), A(LE_)), "s")
+        mm([(A(C, 0, 512), A(UBM), A(FU, 0, 512), True, True), (A(C, 512, 576), A(UBM), A(FU, 512, 576), True, True)])
+        for d0, d1 in ((1, 3), (3, 6), (6, 12)):
+            for d in range(d0, d1):
+                tt(A(DD, 48 * off[d - 1], 48 * off[d]), A(NR, 0, 48 * (12 - d)), A(C, 48 * d, 576), SUB)
+            q0, q1 = off[d0 - 1], off[d1 - 1]
+            ts(A(CC, 48 * q0, 48 * q1), A(DD, 48 * q0, 48 * q1), -2048.0, MAX, 2048.0, MIN)
+            mm(acc(A(B[0], 3 * q0, 3 * q1), ext(None, Z14, CC, 3 * (q1 - q0), 48 * q0)))
+        act(A(NK), A(NR), AF.Identity, MAGIC)
+        act(A(NH), A(NK), AF.Identity, -MAGIC)
+        for k in range(2):
+            mm([(A(B[1 + k], 48 * j, 48 * j + 48), BVB, A(FG), True, True) for j in range(6)])
+            lin(A(GOT, 592 * t + 16 + 288 * k, 592 * t + 304 + 288 * k), A(B[1 + k], 0, 288), U13, -1.0, "s")
+            tt(A(NK, 288 * k, 288 * k + 288), A(B[1 + k], 0, 288), A(NH, 288 * k, 288 * k + 288), NE)
+        tt(A(NK), A(NK), A(NR), MUL)
+        act(A(FRE), A(NK), AF.Relu, 1.0, -1.0)
+        mm(acc(A(B[1], 0, 36), ext(None, ZL12, FRE, 36)))
+        lin(A(WW, 200, 236), A(B[1], 0, 36), -1.0, 0.0)
+        for k in range(2):
+            s = (288 * k, 288 * k + 288)
+            mm(acc(A(B[2 - k], 0, 288), [(A(SFX), A(FRE, *s)), (PAS, A(FU, *s))]))
+            cp(A(PFU, *s), A(B[2 - k], 0, 288), "s")
+        for c in range(0, 36, 12):
+            cp(IND(A(P), A(LU, c, c + 12)), A(NK, 16 * c, 16 * c + 192))
+        ts(A(GC), A(GR, 16, 64), W["cm"], MUL, W["cx"], MAX)
+        cp(IND(A(P), LG), A(GC))
+        RI, RL, SQ, SU, SV, IN, TO, OF, JC, EE, LM = ii(198), f(208), f(576), f(208), f(208), f(198), b(4), f(198), f(198), f(198), u(198)
+        NW = f(198)
+        ts(A(RI), A(B[0], 0, 198), 65535.0, ADD)
+        ts(A(RR, 0, 198), A(RI), 4095, AND)
+        cp(A(RL), IND(A(RR), A(LEX, 0, 13)))
+        ts(A(WW, 0, 198), A(RL, 0, 198), 4095.0, EQ)
+        act(A(NW), A(RL, 0, 198), AF.Relu, 4095.0, -1.0)
+        act(A(JC), A(RL, 0, 198), AF.Relu, -2559.5 * 32768, 32768.0)
+        cp(A(SQ), IND(A(WW), A(LSQ)))
+        scan(A(ST, 0, 576), A(RS1), A(SQ), MUL, ADD)
+        cp(A(SU), IND(A(ST), A(LUP, 0, 13)))
+        tt(A(SV), IND(A(ST), A(LDN, 0, 13)), A(SU), MAX)
+        tt(A(SV, 0, 198), A(SV, 0, 198), A(NW), MAX)
+        ts(A(SU, 0, 198), A(SV, 0, 198), 0.0, LE)
+        scan(A(IN), A(RS2), A(SU, 0, 198), MUL, ADD)
+        act(A(EE), A(SV, 0, 198), AF.Relu, 0.0, 16384.0)
+        cp(A(TO, 0, 3), A(IN, 65, 198, 66))
+        mm([(A(B[1], 0, 3), A(TS), A(TO, 0, 3), True, False), (A(B[1], 1, 3), A(BD), A(TO, 0, 2), False, False), (A(B[1], 2, 3), A(BD), A(TO, 0, 1), False, True)])
+        tt(A(JC), A(JC), A(JM), MIN)
+        tt(A(JC), A(JC), A(RL, 0, 198), MAX)
+        tt(A(IN), A(IN), A(EE), ADD)
+        for c in range(3):
+            ts(A(OF, 66 * c, 66 * c + 66), A(IN, 66 * c, 66 * c + 66), col(B[1], c), ADD, float(n0 - 1), ADD)
+        tt(A(JC), A(JC), A(OF), MIN)
+        cp(A(LM), A(JC))
+        cp(IND(A(MW), A(LM)), A(SD))
+        LA, LB, LN, LS, AN = u(192)[:2] + (nc,), u(192)[:2] + (nc,), u(64), u(64), f(64)
+        mm(acc(A(B[0], 0, 32), ext(None, ZA, MW, 32, n0)) + acc(A(B[0], 32, 64), ext(None, ZBB, MW, 32, n0)))
+        cp(A(LN), A(B[0], 0, 64))
+        ts(A(AN), A(B[0], 0, 64), 576.0, LT)
+        mm(acc(A(B[1], 0, 32), ext(None, ZSA, MW, 32, n0)) + acc(A(B[1], 32, 64), ext(None, ZSB, MW, 32, n0)))
+        ts(A(LS), A(B[1], 0, 64), 1.0, ADD, 591.0, MIN)
+        mm([(A(B[2]), A3(BL, 0), A(MW, n0, n), True, True)])
+        MK, SM, G, CM, PO, PE_, LP = b(512), b(1024), b(1024), b(1024), f(64), f(64), u(64)
+        ts(A(MK), A(B[2]), PM, EQ)
+        for e in range(2):
+            s = (512 * e, 512 * e + 512)
+            cp(A(G, *s), IND(A(PFU), A(LN, 32 * e, 32 * e + 32)), "s")
+            tt(A(SM, *s), IND(A(ST), A(LS, 32 * e, 32 * e + 32)), A(MK), MUL)
+            mm(acc(A(B[e]), [(A(ID), A(G, *s)), (A(NBD), A(SM, *s))]))
+            act(A(CM, *s), A(B[e]), AF.Sign, 0.5)
+        mm(acc(A(B[2], 0, 64), ext(None, ZU, G, 64) + ext(None, Z640, CM, 64)))
+        tt(A(PO), A(B[2], 0, 64), A(JQ), SUB)
+        tt(A(PO), A(PO), A(AN), MUL)
+        tt(A(PO), A(PO), A(JP), ADD)
+        ts(A(LP), A(PO), -1.0, ADD)
+        tt(IND(A(UW), A(LP, 0, 32)), A(G, 512, 1024), A(NM[t]), ADD)
+        tt(IND(A(UW), A(LP, 32, 64)), A(G, 0, 512), A(NM[t]), ADD)
+        for k, (v0, v1) in enumerate(((0, 96), (544, 640), (96, 544))):
+            mm(acc(A(B[k], 0, v1 - v0), [(Z(ZUP, l), A(UW, 640 * l + v0, 640 * l + v1)) for l in range(12)]))
+            tt(A(P, 16 + v0, 16 + v1), A(B[k], 0, v1 - v0), A(P, 16 + v0, 16 + v1), ADD)
+        AC2, WN = f(192)[:2] + (nc,), f(192)[:2] + (nc,)
+        mm(acc(A(B[3], 0, nc), ext(None, ZA, MW, nc)))
+        cp(A(LA), A(B[3], 0, nc))
+        lin(A(AC2), A(B[3], 0, nc), 1.0, float(592 * t + 16), "v")
+        mm(acc(A(B[4], 0, nc), ext(None, ZBB, MW, nc)))
+        cp(A(LB), A(B[4], 0, nc))
+        for k in range(n // 512):
+            s = (512 * k, 512 * k + 512)
+            cp(A(GA, *s), IND(A(Y), A(LA, 32 * k, 32 * k + 32)), "vs")
+            cp(A(GB, *s), IND(A(Y), A(LB, 32 * k, 32 * k + 32)), "vs")
+            bk, dk = A(B[3 + k % 2]), A(C if k % 2 else B[5], 0, 512)
+            if k < n0 // 512:
+                mm(acc(dk, [(A(ID), A(XL, *s)), (A(NID), A(GA, *s)), (A(NID), A(GB, *s))]))
+                act(A(LTT, *s), dk, AF.Sign, -0.5)
+            mm(acc(bk, [(A(ID), A(GA, *s)), (A(ID), A(GB, *s))]))
+            tt(A(XL, *s), bk, A(XL, *s), MIN)
+        mm(acc(A(B[3], 0, n0 // 16), ext(None, ZB, LTT, n0 // 16)))
+        tt(A(AC2), A(AC2), A(MID, 0, nc), SUB)
+        ts(A(WN, 0, n0 // 16), A(B[3], 0, n0 // 16), 2.0, GE)
+        cp(A(WN, n0 // 16, nc), A(AN, 0, 32))
+        tt(A(AC2), A(AC2), A(WN), MUL)
+        tt(A(MID, 0, nc), A(MID, 0, nc), A(AC2), ADD)
+
+    def seam(t):
+        SCOPE[:] = ["c", 0]
+        side = (A(P, 16, 96), A(P, 576, 656))
+        buf = lambda nm, w, d: [own("%s%d%d" % (nm, t, e), "sbuf", [128, w], d) for e in range(2)]
+        TB, TR, XS, XR = buf("TB", 80, "bfloat16"), buf("TR", 80, "bfloat16"), buf("XS", 480, "uint16"), buf("XR", 480, "uint16")
+        T4, PS, HS, LN_, NMF, O1, RI, O2, LI, LS_ = f(384), f(128), f(120), u(120), f(120), f(120), f(120), f(120), u(120), u(120)
+        for o, c in ((0, 16), (96, 0), (192, 560), (288, 576)):
+            tr(A(T4, o, o + 96), A(P, c, c + 96))
+        cp(A(PS), IND(A(T4), A(LSE)))
+        ts(A(HS), A(PS, 0, 120), MAGIC, ADD, MAGIC, SUB)
+        tt(A(NMF), A(PS, 0, 120), A(HS), SUB)
+        ts(A(LN_), A(NMF), -1.0, ADD)
+        tt(A(O1), A(HS), A(AV), LE)
+        for e in range(2):
+            H, V1, V2 = f(80), f(80), f(80)
+            ts(A(H), side[e], MAGIC, ADD, MAGIC + 0.0, SUB)
+            lin(A(H), A(H), 1.0, -8192.0 * (705 + 560 * e), "v")
+            ts(A(V1), A(H), -8192.0 * 704, GE, W["l12"], MUL)
+            if e == 0:
+                ts(A(V2), A(H), -8192.0 * 624, LT)
+                tt(A(V1), A(V1), A(V2), MUL)
+            tt(A(H), A(H), A(V1), MUL)
+            ts(A(TB[e]), A(H), 704.0 * 8192, ADD)
+            send(A(TR[1 - e]), A(TB[e]), 2 * e - 1, 4000)
+        own_ = (A(GA, 0, 960), A(GA, 960, 1920))
+        for e in range(2):
+            cp(own_[e], IND(A(XL), A(LN_, 60 * e, 60 * e + 60)), "vs")
+            mm(acc(A(B[3], 0, 480), [(A(ID), A(GA, 960 * e, 960 * e + 480)), (A(I256), A(GA, 960 * e + 480, 960 * e + 960))]))
+            cp(A(XS[e]), A(B[3], 0, 480))
+            send(A(XR[1 - e]), A(XS[e]), 2 * e - 1, 5500)
+        for e in range(2):
+            Q = b(80)
+            ts(A(Q), A(TR[e]), 600.0 * 8192, MIN)
+            for k in range(2):
+                s = (960 * e + 480 * k, 960 * e + 480 * k + 480)
+                mm(sum([acc(A(B[4 + k], 80 * l, 80 * l + 80), [(A3(BL, 6 * k + l), A(TB[e])), (A(NID), A(Q))]) for l in range(6)], []))
+                act(A(DD, *s), A(B[4 + k], 0, 480), AF.Abs)
+                act(A(LTT, *s), A(DD, *s), AF.Relu, 1.0, -1.0)
+            mm(acc(A(B[4], 0, 60), ext(None, ZM, LTT, 60, 960 * e)))
+            cp(A(RI, 60 * e, 60 * e + 60), A(B[4], 0, 60))
+        ts(A(O2), A(RI), 0.0, EQ)
+        tt(A(O1), A(O1), A(O2), MAX)
+        ts(A(O2), A(O2), 13.0, MUL)
+        tt(A(O2), A(O2), A(RI), ADD)
+        ts(A(O2), A(O2), 80.0, MUL)
+        tt(A(O2), A(O2), A(JA), ADD)
+        cp(A(LI), A(O2))
+        tt(A(O1), A(O1), A(JX), MUL)
+        tt(A(O1), A(O1), A(NMF), MAX)
+        ts(A(LS_), A(O1), -1.0, ADD)
+        for e in range(2):
+            XI, KP = ii(480), f(80)
+            mn, sg = A(GB, 960 * e, 960 * e + 960), A(LTT, 960 * e, 960 * e + 960)
+            cp(A(XI), A(XR[e]))
+            ts(A(XW[e], 0, 480), A(XI), 255, AND)
+            ts(A(XW[e], 480, 960), A(XI), 8, SHR)
+            tt(mn, IND(A(XW[e]), A(LI, 60 * e, 60 * e + 60)), own_[e], MIN)
+            for k in range(2):
+                s = (960 * e + 480 * k, 960 * e + 480 * k + 480)
+                mm(acc(A(B[4 + k], 0, 480), [(A(ID), A(GA, *s)), (A(NID), A(GB, *s))]))
+                act(A(LTT, *s), A(B[4 + k], 0, 480), AF.Sign, -0.5)
+            mm(acc(A(B[3], 0, 80), [(Z(ZB, l), A(LTT, 960 * e + 80 * l, 960 * e + 80 * l + 80)) for l in range(12)]))
+            ts(A(KP), A(B[3], 0, 80), 2.0, LT)
+            tt(side[e], side[e], A(KP), MUL)
+        for e in range(2):
+            for c0, c1 in ((0, 10), (10, 20), (20, 30), (30, 40), (40, 50), (50, 60)) if t == 0 else ((0, 30), (30, 60)):
+                cp(IND(A(XL), A(LS_, 60 * e + c0, 60 * e + c1)), A(GB, 960 * e + 16 * c0, 960 * e + 16 * c1))
+
+    LSE, s1, s2, s3, s4, si, JA, AV, JX, QC, I256 = u(8), f(8), f(8), f(8), f(8), ii(8), f(120), f(120), f(120), f(1), b(128)
+    ts(A(s1), A(J, 0, 8), 60.0, GE)
+    ts(A(s2), A(s1), -60.0, MUL)
+    tt(A(s2), A(s2), A(J, 0, 8), ADD)
+    ts(A(si), A(s2), 0.2, MUL, -0.4, ADD)
+    ts(A(s3), A(si), -5.0, MUL)
+    tt(A(s2), A(s2), A(s3), ADD)
+    ts(A(s3), A(s2), 16.0, MUL)
+    tt(A(s3), A(s3), A(si), ADD)
+    tt(A(s2), A(s2), A(s1), ADD)
+    ts(A(si), A(s2), PH, ADD)
+    ts(A(si), A(si), 1, AND)
+    ts(A(s4), A(s1), -32.0, MUL, 112.0, ADD)
+    tt(A(s4), A(s4), A(si), MUL)
+    ts(A(s1), A(s1), 208.0, MUL)
+    tt(A(s3), A(s3), A(s1), ADD)
+    tt(A(s3), A(s3), A(s4), ADD)
+    cp(A(LSE), A(s3))
+    JB = f(120)
+    iota(A(JB), [[0, 24], [16, 5]], -80)
+    lin(A(JA), A(JB), 1.0, PM)
+    for e in range(2):
+        lin(A(AV, 60 * e, 60 * e + 60), A(JA, 0, 60), 8192.0, 8192.0 * (81 + 560 * e))
+        lin(A(JX, 60 * e, 60 * e + 60), A(J, 0, 60), 1.0, 3073.0)
+        ms(A(XW[e], 960, 1040), 255)
+    ts(A(QC), PM, 1.0, ADD, W["l12"], MUL)
+    W["m1"] = A(QC)
+    ZM = zt("m1")
+    lin(A(I256), A(ID), 256.0, 0.0)
+    lg = choose(0)
+    contract(0, lg)
+    fill(1)
+    tr(A(TT, 0, 640), A(P, 16, 656))
+    tr(A(TT, 640, 1312), A(P, 0, 672))
+    cp(A(PV), IND(A(TT), A(LSV)), "vs")
+    ts(A(L1), A(PV), U13, MUL, 15.0, ADD)
+    lg = choose(1)
+    seam(0)
+    contract(1, lg)
+    SCOPE[0] = None
+    LMID = u(192)
+    cp(A(LMID), A(MID))
+    for k in range(4):
+        cp(A(YM, 768 * k, 768 * k + 768), IND(A(GOT), A(LMID, 48 * k, 48 * k + 48)), "vs")
+    dma(X("ymid", ALL, ALL), A(YM, p=(0, 128, 16)), "y")
+    seam(1)
+    YL, HF, YE, YN = GA, TIN, (TT[0], TT[1], 640), (TT[0], TT[1] + 640, 640)
+    dma(X("ylen", ALL, ALL), A(XL, 0, 3072), "y", 4000)
+    q = (0, 96)
+    for bk, v0, v1 in ((0, 80, 560), (1, 0, 80), (2, 560, 640)):
+        o = A(B[bk], 0, v1 - v0, p=q)
+        mm([(o, A(PERM), A(P, 16 + v0, 16 + v1), True, True)])
+        ts(A(HF, v0, v1, p=q), o, MAGIC, ADD, MAGIC + 0.0, SUB)
+        lin(A(YN, v0, v1, p=q), A(HF, v0, v1, p=q), U13, -1.0)
+        tt(A(HF, v0, v1, p=q), o, A(HF, v0, v1, p=q), SUB)
+        lin(A(YE, v0, v1, p=q), A(HF, v0, v1, p=q), 1.0, -1.0)
+    dma(X("ynb", ALL, ALL), A(YN, p=q), "y")
+    dma(X("yen", ALL, ALL), A(YE, p=q), "s")
+
+
+def schedule():
+    n = len(OPS)
+    hist = {}
+    for k, o in enumerate(OPS):
+        dep = {}
+        for kind, regs in (("r", o["rd"]), ("w", o["wr"])):
+            for nm, lo, hi, st in regs:
+                ps = nm in SHAPES and SHAPES[nm][0] == "psum"
+                for j, kd, l2, h2, s2 in hist.get(nm, []):
+                    meet = l2 <= hi and lo <= h2 and (kd == "w" or kind == "w") and not (st == s2 and (lo - l2) % st)
+                    if ps or meet:
+                        dep[j] = dep.get(j, False) or (meet and not ps)
+        dep.pop(k, None)
+        for kind, regs in (("r", o["rd"]), ("w", o["wr"])):
+            for nm, lo, hi, st in regs:
+                if hi < 1 << 30:
+                    hist.setdefault(nm, []).append((k, kind, lo, hi, st))
+        o["dep"] = dep
+    succ = [[] for _ in range(n)]
+    pred = [set(o["dep"]) | ({o["after"]} if "after" in o else set()) for o in OPS]
+    for k in range(n):
+        for j in pred[k]:
+            succ[j].append(k)
+    pri = [0.0] * n
+    for k in range(n - 1, -1, -1):
+        pri[k] = min(a[2] for a in OPS[k]["alts"]) + OPS[k].get("lat", 0) + SYNC + max([pri[j] for j in succ[k]] + [0])
+
+    def place(pr, bias):
+        busy = dict(v=[], s=[], t=[], g=[], y=[], n=[])
+        done, use, at, left = {}, {}, {}, [len(p) for p in pred]
+        rdy = [k for k in range(n) if not left[k]]
+        while rdy:
+            k = max(rdy, key=lambda q: pr[q])
+            rdy.remove(k)
+            best = None
+            for a in OPS[k]["alts"]:
+                st = max([done[i] - (SYNC if use[i][0] == a[0] and "sem" not in OPS[i] and "sem" not in OPS[k] and not OPS[k]["dep"][i] else 0) for i in pred[k]] + [0.0])
+                d, pos = (a[2] + 20 if a[0] != "n" else 0), 0
+                for pos, (b0, b1) in enumerate(busy[a[0]] + [(1e12, 1e12)]):
+                    if b1 > st:
+                        if st + d <= b0:
+                            break
+                        st = b1
+                c = st + d + (bias if a[0] == "v" else 0)
+                if best is None or c < best[0]:
+                    best = (c, a, st, d, pos)
+            c, a, st, d, pos = best
+            if d:
+                busy[a[0]].insert(pos, (st, st + d))
+            use[k], at[k], done[k] = a, st, st + a[2] + OPS[k].get("lat", 0) + SYNC
+            for j in succ[k]:
+                left[j] -= 1
+                if not left[j]:
+                    rdy.append(j)
+        return max(done.values()), use, at, done
+
+    pr = np.array(pri)
+    for a, b, d in NUDGE:
+        pr[a:b] += d
+    best = place(pr, BIAS)
+    rng = np.random.RandomState(SEARCH[1])
+    for it in range(SEARCH[0]):
+        a = int(rng.randint(0, n))
+        b, d = a + int(rng.choice([1, 3, 10, 30, 80])), int(rng.choice([-1, 1]) * rng.choice([300, 1000, 3000, 10000, 30000]))
+        p2 = pr.copy()
+        p2[a:b] += d
+        got = place(p2, BIAS)
+        if got[0] < best[0]:
+            best, pr = got, p2
+            NUDGE.append((a, b, d))
+    for k in range(n):
+        OPS[k]["use"], OPS[k]["at"] = best[1][k], best[2][k]
+    return sorted(range(n), key=lambda k: (best[2][k], k)), best[0]
+
+
+SYNC, BIAS, SEARCH = 100.0, 300.0, [0, 1]
+NUDGE = [(586, 587, -1000), (896, 897, 30000), (532, 612, 30000), (489, 499, -3000), (253, 333, 3000), (206, 209, 10000), (317, 397, 3000), (506, 516, -3000), (358, 388, -1000), (1007, 1010, 1000), (117, 120, -3000), (249, 329, -300), (633, 643, -3000), (976, 1056, -1000), (849, 879, -1000), (849, 879, -1000), (488, 498, 1000), (858, 861, 3000), (304, 384, -300), (432, 462, -1000), (991, 1001, 3000), (924, 925, 3000), (913, 943, -300), (628, 658, -1000), (704, 707, 1000), (932, 962, -300), (909, 919, 1000), (987, 990, 1000), (582, 612, 10000), (621, 631, -3000), (517, 547, 10000), (664, 667, -300), (850, 860, 1000), (740, 741, -3000), (566, 569, -30000), (952, 955, 10000), (563, 566, -3000), (965, 975, -300), (853, 856, 3000), (381, 411, -3000), (946, 1026, 300), (922, 923, 1000)]
+program()
+ORDER, SPAN = schedule()
+SCRATCH = {"p" + k: ("sbuf", [128, v[1]], v[0]) for k, v in POOL.items()}
+SCRATCH.update(SHAPES)
+SEMAPHORES = list(SEMS)
+
+
+def rank_program(g, core, T, topo):
+    rank = T.rank_of(core)
+    if rank is None:
+        return
+    n = len(T.cores)
+    Q = dict(v=g.vector, s=g.scalar, t=g.tensor, g=g, y=g.sync)
+    known = dict(v={}, s={}, t={}, g={}, y={})
+    count, mark, clock = {}, {}, {}
+
+    def engines(src, dst):
+        return topo.engines(src, dst)[:8]
+
+    for k in ORDER:
+        o = OPS[k]
+        e, fn = o["use"][0], o["use"][1]
+        if e == "n":
+            mark[k] = (o["sem"], len(engines(T.cores[(rank - o["step"]) % n], core)))
+            count[o["sem"]] = mark[k][1]
+            clock[k] = {}
+            continue
+        kn = known[e]
+        need = {}
+        for j, raw in o["dep"].items():
+            if raw or OPS[j]["use"][0] != e or "sem" in OPS[j] or "sem" in o:
+                s, v = mark[j]
+                if kn.get(s, 0) < v and need.get(s, (0, 0))[0] < v:
+                    need[s] = (v, j)
+        for s, (v, j) in sorted(need.items(), key=lambda q: -OPS[q[1][1]]["at"]):
+            if kn.get(s, 0) < v:
+                Q[e].wait_ge(T.sem[s], v)
+                kn[s] = v
+                for s2, v2 in clock[j].items():
+                    kn[s2] = max(kn.get(s2, 0), v2)
+        clock[k] = dict(kn)
+        if "send" in o:
+            dst, src, step, rs = o["send"]
+            peer = T.cores[(rank + step) % n]
+            es = engines(core, peer)
+            rid, pid, se = topo.addr(peer)
+            g.remote_dma(real(T, dst), real(T, src), T.sem[rs], T.sem[o["sem"]], pid, rid, sum(1 << x for x in es))
+            mark[k] = (o["sem"], len(es))
+        elif "sem" in o:
+            fn(g, T).then_inc(T.sem[o["sem"]], 16)
+            mark[k] = (o["sem"], 16)
+        else:
+            s = "e" + e
+            fn(g, T).then_inc(T.sem[s], 1)
+            mark[k] = (s, count.get(s, 0) + 1)
+        count[mark[k][0]] = mark[k][1]
+    for s, v in count.items():
+        if max(known[e].get(s, 0) for e in known) < v or s[0] == "e":
+            g.wait_ge(T.sem[s], v)

@@ -93,13 +93,13 @@ def op(alts, outs, ins, **kw):
         wr.append(reg(ap))
         if ap[5] is not None:
             rd.append(reg(ap[5]))
-    OPS.append(dict(alts=alts, rd=rd, wr=wr, **kw))
+    OPS.append(dict(alts=alts, rd=rd, wr=wr, sc=any(ap[5] is not None for ap in outs), ga=any(isinstance(ap, tuple) and ap[5] is not None for ap in ins), **kw))
 
 
 def vcost(out, ins, tt=False):
     n = out[4]
     if out[5] is not None:
-        return 60 + 3.8 * n
+        return 60 + 4.2 * n
     if ins[0][5] is not None:
         return 60 + 1.5 * n
     if tt:
@@ -168,6 +168,11 @@ def tr(out, in_):
 
 
 def mm(parts):
+    if len(parts) >= 8 and sum(max(64, q[2][4]) * (1 if two(q[2]) else 4) for q in parts) > 2200:
+        mm(parts[:len(parts) // 2])
+        mm(parts[len(parts) // 2:])
+        return
+
     def f(g, T):
         r = None
         for o, l, x, s, e in parts:
@@ -211,6 +216,7 @@ def send(dst, src, step, lat):
 
 
 PEC = 0.6
+OPT = [[], [0, 2], [0, 2, 4]]
 
 
 def program():
@@ -310,6 +316,9 @@ def program():
     ts(col(pc, 1), W["cx"], col(pc, 0), ADD)
     ts(col(pc, 0), W["ps"], 1920.0, MUL, col(pc, 1), ADD)
     ts(A(PERM), A(XZ, 15, 111), col(pc, 0), EQ)
+    ZN14, NPM = f(144), f(1)
+    ts(A(NPM), PM, -1.0, MUL)
+    ts(A(ZN14), A(ZB), W["o14"], MUL, -1.0, MUL)
     Z0F = f(144)
     lin(A(Z0F), A(ZB), col(OH, 0), 0.0)
     TS, SFX, NBD, UBM, t1, t2 = b(128), b(128), b(128), b(128), f(128), f(128)
@@ -489,7 +498,7 @@ def program():
 
     def choose(t):
         SCOPE[:] = ["a", 0]
-        ts(A(F, 16, 656), A(P, 16, 656), W["fs"], MUL, W["fc"], MIN)
+        ts(A(F, 16, 656), A(P, 16, 656) if t else IND(A(TT), A(LVS)), W["fs"], MUL, W["fc"], MIN)
         KV, E, DS, AC, M1, HL = f(40), f(480), f(480), f(120), f(40), b(80)
         mm(acc(A(B[2], 0, 40), ext(None, ZKEY, F, 40, 16)))
         cp(A(KV), A(B[2], 0, 40), "vs")
@@ -497,19 +506,18 @@ def program():
         cp(A(DS), A(B[2], 0, 480), "vs")
         mm([(A(B[2], 0, 480), BKEY, A(F, 96, 576), True, True)])
         tt(A(E), A(B[2], 0, 480), A(DS), MUL)
-        for c in range(4):
-            for s in range(3):
-                k = 3 * c + s
+        for c in range(6):
+            for s in range(2):
+                k = 2 * c + s
                 l = A(L1, 40 * k, 40 * k + 40)
                 cp(A(RH, 640 * k, 640 * k + 640), IND(A(F, 0, 656), l), "vs")
-            mm(acc(A(B[c % 2], 0, 120), ext(None, ZKEY, RH, 120, 1920 * c)))
+            mm(acc(A(B[c % 2], 0, 80), ext(None, ZKEY, RH, 80, 1280 * c)))
             if c == 0:
-                cp(A(AC), A(B[0], 0, 120))
+                tt(A(AC, 0, 40), A(B[0], 0, 40), A(KV), MIN)
+                cp(A(AC, 40, 80), A(B[0], 40, 80))
             else:
-                tt(A(AC), A(B[c % 2], 0, 120), A(AC), MIN)
-        tt(A(KV), A(KV), A(AC, 0, 40), MIN)
-        tt(A(M1), A(AC, 40, 80), A(AC, 80, 120), MIN)
-        tt(A(M1), A(M1), A(KV), MIN)
+                tt(A(AC, 0, 80), A(B[c % 2], 0, 80), A(AC, 0, 80), MIN)
+        tt(A(M1), A(AC, 0, 40), A(AC, 40, 80), MIN)
         cp(A(HL, 0, 40), A(M1))
         tt(A(HL, 40, 80), A(M1), A(HL, 0, 40), SUB)
         for k, (c0, c1) in enumerate(((0, 20), (20, 40))):
@@ -534,7 +542,7 @@ def program():
         clear()
         return A(LG, 0, 3)
 
-    def contract(t, LG):
+    def contract(t, LG, store=None):
         n, n0 = 2560 + 512 * t, 2048 + 512 * t
         nc = n // 16
         SCOPE[:] = ["b", 0]
@@ -555,11 +563,18 @@ def program():
         tt(A(GH), A(GV, 0, 36), A(GH), SUB)
         ts(A(LE_), A(GH), -1.0, ADD)
         cp(A(Y, 0, 576), IND(A(XL), A(LE_)), "s")
+        if store:
+            store()
         mm([(A(C, 0, 512), A(UBM), A(FU, 0, 512), True, True), (A(C, 512, 576), A(UBM), A(FU, 512, 576), True, True)])
         for d0, d1 in ((1, 3), (3, 6), (6, 12)):
             for d in range(d0, d1):
                 tt(A(DD, 48 * off[d - 1], 48 * off[d]), A(NR, 0, 48 * (12 - d)), A(C, 48 * d, 576), SUB)
             q0, q1 = off[d0 - 1], off[d1 - 1]
+            if d0 == 1:
+                act(A(DD, 0, 1008), A(DD, 0, 1008), AF.Relu, 2048.0)
+                act(A(DD, 0, 1008), A(DD, 0, 1008), AF.Relu, 4096.0, -1.0)
+                mm(acc(A(B[3], 0, 63), ext(None, ZN14, DD, 63)))
+                continue
             ts(A(CC, 48 * q0, 48 * q1), A(DD, 48 * q0, 48 * q1), -2048.0, MAX, 2048.0, MIN)
             mm(acc(A(B[0], 3 * q0, 3 * q1), ext(None, Z14, CC, 3 * (q1 - q0), 48 * q0)))
         act(A(NK), A(NR), AF.Identity, MAGIC)
@@ -567,8 +582,10 @@ def program():
         for k in range(2):
             mm([(A(B[1 + k], 48 * j, 48 * j + 48), BVB, A(FG), True, True) for j in range(6)])
             lin(A(GOT, 592 * t + 16 + 288 * k, 592 * t + 304 + 288 * k), A(B[1 + k], 0, 288), U13, -1.0, "s")
-            tt(A(NK, 288 * k, 288 * k + 288), A(B[1 + k], 0, 288), A(NH, 288 * k, 288 * k + 288), NE)
-        tt(A(NK), A(NK), A(NR), MUL)
+            s = (288 * k, 288 * k + 288)
+            tt(A(NK, *s), A(B[1 + k], 0, 288), A(NH, *s), SUB)
+            act(A(B[1 + k], 0, 288), A(NK, *s), AF.Abs, 0.0, 1024.0)
+            tt(A(NK, *s), A(B[1 + k], 0, 288), A(NR, *s), MIN)
         act(A(FRE), A(NK), AF.Relu, 1.0, -1.0)
         mm(acc(A(B[1], 0, 36), ext(None, ZL12, FRE, 36)))
         lin(A(WW, 200, 236), A(B[1], 0, 36), -1.0, 0.0)
@@ -582,10 +599,12 @@ def program():
         cp(IND(A(P), LG), A(GC))
         RI, RL, SQ, SU, SV, IN, TO, OF, JC, EE, LM = ii(198), f(208), f(576), f(208), f(208), f(198), b(4), f(198), f(198), f(198), u(198)
         NW = f(198)
-        ts(A(RI), A(B[0], 0, 198), 65535.0, ADD)
+        ts(A(RI, 0, 63), A(B[3], 0, 63), 65535.0, ADD)
+        ts(A(RI, 63, 198), A(B[0], 63, 198), 65535.0, ADD)
         ts(A(RR, 0, 198), A(RI), 4095, AND)
         cp(A(RL), IND(A(RR), A(LEX, 0, 13)))
         ts(A(WW, 0, 198), A(RL, 0, 198), 4095.0, EQ)
+        NW, JC, EE = (C, 0, 198), (C, 512, 198), (B[2], 0, 198)
         act(A(NW), A(RL, 0, 198), AF.Relu, 4095.0, -1.0)
         act(A(JC), A(RL, 0, 198), AF.Relu, -2559.5 * 32768, 32768.0)
         cp(A(SQ), IND(A(WW), A(LSQ)))
@@ -603,8 +622,8 @@ def program():
         tt(A(IN), A(IN), A(EE), ADD)
         for c in range(3):
             ts(A(OF, 66 * c, 66 * c + 66), A(IN, 66 * c, 66 * c + 66), col(B[1], c), ADD, float(n0 - 1), ADD)
-        tt(A(JC), A(JC), A(OF), MIN)
-        cp(A(LM), A(JC))
+        tt(A(OF), A(JC), A(OF), MIN)
+        cp(A(LM), A(OF))
         cp(IND(A(MW), A(LM)), A(SD))
         LA, LB, LN, LS, AN = u(192)[:2] + (nc,), u(192)[:2] + (nc,), u(64), u(64), f(64)
         mm(acc(A(B[0], 0, 32), ext(None, ZA, MW, 32, n0)) + acc(A(B[0], 32, 64), ext(None, ZBB, MW, 32, n0)))
@@ -614,7 +633,8 @@ def program():
         ts(A(LS), A(B[1], 0, 64), 1.0, ADD, 591.0, MIN)
         mm([(A(B[2]), A3(BL, 0), A(MW, n0, n), True, True)])
         MK, SM, G, CM, PO, PE_, LP = b(512), b(1024), b(1024), b(1024), f(64), f(64), u(64)
-        ts(A(MK), A(B[2]), PM, EQ)
+        act(A(CM, 0, 512), A(B[2]), AF.Abs, A(NPM))
+        act(A(MK), A(CM, 0, 512), AF.Relu, 1.0, -1.0)
         for e in range(2):
             s = (512 * e, 512 * e + 512)
             cp(A(G, *s), IND(A(PFU), A(LN, 32 * e, 32 * e + 32)), "s")
@@ -645,14 +665,17 @@ def program():
             if k < n0 // 512:
                 mm(acc(dk, [(A(ID), A(XL, *s)), (A(NID), A(GA, *s)), (A(NID), A(GB, *s))]))
                 act(A(LTT, *s), dk, AF.Sign, -0.5)
-            mm(acc(bk, [(A(ID), A(GA, *s)), (A(ID), A(GB, *s))]))
-            tt(A(XL, *s), bk, A(XL, *s), MIN)
+            if k in OPT[1 + t]:
+                act(bk, dk, AF.Relu)
+                tt(A(XL, *s), A(XL, *s), bk, SUB)
+            else:
+                mm(acc(bk, [(A(ID), A(GA, *s)), (A(ID), A(GB, *s))]))
+                tt(A(XL, *s), bk, A(XL, *s), MIN)
         mm(acc(A(B[3], 0, n0 // 16), ext(None, ZB, LTT, n0 // 16)))
-        tt(A(AC2), A(AC2), A(MID, 0, nc), SUB)
-        ts(A(WN, 0, n0 // 16), A(B[3], 0, n0 // 16), 2.0, GE)
-        cp(A(WN, n0 // 16, nc), A(AN, 0, 32))
-        tt(A(AC2), A(AC2), A(WN), MUL)
-        tt(A(MID, 0, nc), A(MID, 0, nc), A(AC2), ADD)
+        ts(A(WN, 0, n0 // 16), A(B[3], 0, n0 // 16), 2.0, GE, 4096.0, MUL)
+        ts(A(WN, n0 // 16, nc), A(AN, 0, 32), 4096.0, MUL)
+        tt(A(AC2), A(AC2), A(WN), MIN)
+        tt(A(MID, 0, nc), A(MID, 0, nc), A(AC2), MAX)
 
     def seam(t):
         SCOPE[:] = ["c", 0]
@@ -667,6 +690,8 @@ def program():
         tt(A(NMF), A(PS, 0, 120), A(HS), SUB)
         ts(A(LN_), A(NMF), -1.0, ADD)
         tt(A(O1), A(HS), A(AV), LE)
+        tt(A(O1), A(O1), A(JX), MUL)
+        tt(A(O1), A(O1), A(NMF), MAX)
         for e in range(2):
             H, V1, V2 = f(80), f(80), f(80)
             ts(A(H), side[e], MAGIC, ADD, MAGIC + 0.0, SUB)
@@ -690,20 +715,19 @@ def program():
             for k in range(2):
                 s = (960 * e + 480 * k, 960 * e + 480 * k + 480)
                 mm(sum([acc(A(B[4 + k], 80 * l, 80 * l + 80), [(A3(BL, 6 * k + l), A(TB[e])), (A(NID), A(Q))]) for l in range(6)], []))
-                act(A(DD, *s), A(B[4 + k], 0, 480), AF.Abs)
-                act(A(LTT, *s), A(DD, *s), AF.Relu, 1.0, -1.0)
+                if t == 0 and (e, k) in OPT[0]:
+                    act(A(DD, *s), A(B[4 + k], 0, 480), AF.Abs)
+                    act(A(LTT, *s), A(DD, *s), AF.Relu, 1.0, -1.0)
+                else:
+                    ts(A(LTT, *s), A(B[4 + k], 0, 480), 0.0, EQ)
             mm(acc(A(B[4], 0, 60), ext(None, ZM, LTT, 60, 960 * e)))
-            cp(A(RI, 60 * e, 60 * e + 60), A(B[4], 0, 60))
-        ts(A(O2), A(RI), 0.0, EQ)
-        tt(A(O1), A(O1), A(O2), MAX)
-        ts(A(O2), A(O2), 13.0, MUL)
-        tt(A(O2), A(O2), A(RI), ADD)
-        ts(A(O2), A(O2), 80.0, MUL)
-        tt(A(O2), A(O2), A(JA), ADD)
-        cp(A(LI), A(O2))
-        tt(A(O1), A(O1), A(JX), MUL)
-        tt(A(O1), A(O1), A(NMF), MAX)
-        ts(A(LS_), A(O1), -1.0, ADD)
+            s = (60 * e, 60 * e + 60)
+            tt(A(RI, *s), A(JA, *s), A(B[4], 0, 60), SUB)
+            cp(A(LI, *s), A(RI, *s))
+            ts(A(O2, *s), A(RI, *s), 960.0, GE, 8192.0, MUL)
+            tt(A(O2, *s), A(O2, *s), A(JX, *s), MIN)
+            tt(A(O2, *s), A(O2, *s), A(O1, *s), MAX)
+            ts(A(LS_, *s), A(O2, *s), -1.0, ADD)
         for e in range(2):
             XI, KP = ii(480), f(80)
             mn, sg = A(GB, 960 * e, 960 * e + 960), A(LTT, 960 * e, 960 * e + 960)
@@ -718,9 +742,12 @@ def program():
             mm(acc(A(B[3], 0, 80), [(Z(ZB, l), A(LTT, 960 * e + 80 * l, 960 * e + 80 * l + 80)) for l in range(12)]))
             ts(A(KP), A(B[3], 0, 80), 2.0, LT)
             tt(side[e], side[e], A(KP), MUL)
-        for e in range(2):
-            for c0, c1 in ((0, 10), (10, 20), (20, 30), (30, 40), (40, 50), (50, 60)) if t == 0 else ((0, 30), (30, 60)):
-                cp(IND(A(XL), A(LS_, 60 * e + c0, 60 * e + c1)), A(GB, 960 * e + 16 * c0, 960 * e + 16 * c1))
+
+        def store():
+            for e in range(2):
+                for c0, c1 in ((0, 10), (10, 20), (20, 30), (30, 40), (40, 50), (50, 60)) if t == 0 else ((0, 30), (30, 60)):
+                    cp(IND(A(XL), A(LS_, 60 * e + c0, 60 * e + c1)), A(GB, 960 * e + 16 * c0, 960 * e + 16 * c1))
+        return store
 
     LSE, s1, s2, s3, s4, si, JA, AV, JX, QC, I256 = u(8), f(8), f(8), f(8), f(8), ii(8), f(120), f(120), f(120), f(1), b(128)
     ts(A(s1), A(J, 0, 8), 60.0, GE)
@@ -741,13 +768,14 @@ def program():
     tt(A(s3), A(s3), A(s4), ADD)
     cp(A(LSE), A(s3))
     JB = f(120)
-    iota(A(JB), [[0, 24], [16, 5]], -80)
+    iota(A(JB), [[0, 24], [16, 5]], 960)
     lin(A(JA), A(JB), 1.0, PM)
     for e in range(2):
-        lin(A(AV, 60 * e, 60 * e + 60), A(JA, 0, 60), 8192.0, 8192.0 * (81 + 560 * e))
+        lin(A(AV, 60 * e, 60 * e + 60), A(JA, 0, 60), 8192.0, 8192.0 * (560 * e - 959))
         lin(A(JX, 60 * e, 60 * e + 60), A(J, 0, 60), 1.0, 3073.0)
         ms(A(XW[e], 960, 1040), 255)
-    ts(A(QC), PM, 1.0, ADD, W["l12"], MUL)
+    ts(A(QC), PM, -80.0, MUL, 960.0, ADD)
+    ts(A(QC), A(QC), 0.0, MAX)
     W["m1"] = A(QC)
     ZM = zt("m1")
     lin(A(I256), A(ID), 256.0, 0.0)
@@ -759,22 +787,25 @@ def program():
     cp(A(PV), IND(A(TT), A(LSV)), "vs")
     ts(A(L1), A(PV), U13, MUL, 15.0, ADD)
     lg = choose(1)
-    seam(0)
-    contract(1, lg)
+    contract(1, lg, seam(0))
     SCOPE[0] = None
     LMID = u(192)
     cp(A(LMID), A(MID))
     for k in range(4):
         cp(A(YM, 768 * k, 768 * k + 768), IND(A(GOT), A(LMID, 48 * k, 48 * k + 48)), "vs")
     dma(X("ymid", ALL, ALL), A(YM, p=(0, 128, 16)), "y")
-    seam(1)
+    seam(1)()
     YL, HF, YE, YN = GA, TIN, (TT[0], TT[1], 640), (TT[0], TT[1] + 640, 640)
     dma(X("ylen", ALL, ALL), A(XL, 0, 3072), "y", 4000)
     q = (0, 96)
     for bk, v0, v1 in ((0, 80, 560), (1, 0, 80), (2, 560, 640)):
         o = A(B[bk], 0, v1 - v0, p=q)
         mm([(o, A(PERM), A(P, 16 + v0, 16 + v1), True, True)])
-        ts(A(HF, v0, v1, p=q), o, MAGIC, ADD, MAGIC + 0.0, SUB)
+        if bk:
+            ts(A(HF, v0, v1, p=q), o, MAGIC, ADD, MAGIC, SUB)
+        else:
+            act(A(YE, v0, v1, p=q), o, AF.Identity, MAGIC)
+            act(A(HF, v0, v1, p=q), A(YE, v0, v1, p=q), AF.Identity, -MAGIC)
         lin(A(YN, v0, v1, p=q), A(HF, v0, v1, p=q), U13, -1.0)
         tt(A(HF, v0, v1, p=q), o, A(HF, v0, v1, p=q), SUB)
         lin(A(YE, v0, v1, p=q), A(HF, v0, v1, p=q), 1.0, -1.0)
@@ -793,18 +824,41 @@ def schedule():
                 for j, kd, l2, h2, s2 in hist.get(nm, []):
                     meet = l2 <= hi and lo <= h2 and (kd == "w" or kind == "w") and not (st == s2 and (lo - l2) % st)
                     if ps or meet:
-                        dep[j] = dep.get(j, False) or (meet and not ps)
+                        dep[j] = dep.get(j, False) or (meet and not (ps and o["alts"][0][0] == "t"))
         dep.pop(k, None)
         for kind, regs in (("r", o["rd"]), ("w", o["wr"])):
             for nm, lo, hi, st in regs:
                 if hi < 1 << 30:
                     hist.setdefault(nm, []).append((k, kind, lo, hi, st))
         o["dep"] = dep
-    succ = [[] for _ in range(n)]
+    succ, after, near, above = [[] for _ in range(n)], [[] for _ in range(n)], [], []
     pred = [set(o["dep"]) | ({o["after"]} if "after" in o else set()) for o in OPS]
     for k in range(n):
+        far = 0
         for j in pred[k]:
+            far |= above[j]
+        pred[k] = sorted(j for j in pred[k] if not far >> j & 1 or "sem" in OPS[j])
+        for j in pred[k]:
+            far |= 1 << j
+        above.append(far)
+        near.append([(j, "sem" not in OPS[j] and "sem" not in OPS[k] and not OPS[k]["dep"][j]) for j in pred[k]])
+        for j, soft in near[k]:
             succ[j].append(k)
+            after[j].append((k, soft))
+
+    def gap(busy, st, d):
+        lo, hi = 0, len(busy)
+        while lo < hi:
+            m = (lo + hi) // 2
+            if busy[m][1] > st:
+                hi = m
+            else:
+                lo = m + 1
+        while lo < len(busy) and st + d > busy[lo][0]:
+            st = busy[lo][1]
+            lo += 1
+        return st, lo
+
     pri = [0.0] * n
     for k in range(n - 1, -1, -1):
         pri[k] = min(a[2] for a in OPS[k]["alts"]) + OPS[k].get("lat", 0) + SYNC + max([pri[j] for j in succ[k]] + [0])
@@ -818,13 +872,9 @@ def schedule():
             rdy.remove(k)
             best = None
             for a in OPS[k]["alts"]:
-                st = max([done[i] - (SYNC if use[i][0] == a[0] and "sem" not in OPS[i] and "sem" not in OPS[k] and not OPS[k]["dep"][i] else 0) for i in pred[k]] + [0.0])
-                d, pos = (a[2] + 20 if a[0] != "n" else 0), 0
-                for pos, (b0, b1) in enumerate(busy[a[0]] + [(1e12, 1e12)]):
-                    if b1 > st:
-                        if st + d <= b0:
-                            break
-                        st = b1
+                st = max([done[i] - (SYNC if soft and use[i][0] == a[0] else 0) for i, soft in near[k]] + [0.0])
+                d = a[2] + 20 if a[0] != "n" else 0
+                st, pos = gap(busy[a[0]], st, d)
                 c = st + d + (bias if a[0] == "v" else 0)
                 if best is None or c < best[0]:
                     best = (c, a, st, d, pos)
@@ -838,10 +888,36 @@ def schedule():
                     rdy.append(j)
         return max(done.values()), use, at, done
 
+    def back(got):
+        use, done = got[1], got[3]
+        busy, end = dict(v=[], s=[], t=[], g=[], y=[], n=[]), [0.0] * n
+        left = [len(q) for q in succ]
+        rdy = [k for k in range(n) if not left[k]]
+        while rdy:
+            k = max(rdy, key=lambda q: done[q])
+            rdy.remove(k)
+            a = use[k]
+            lat = OPS[k].get("lat", 0) + SYNC
+            st = max([end[j] + (0 if soft and use[j][0] == a[0] else lat) for j, soft in after[k]] + [lat])
+            d = a[2] + 20 if a[0] != "n" else 0
+            st, pos = gap(busy[a[0]], st, d)
+            if d:
+                busy[a[0]].insert(pos, (st, st + d))
+            end[k] = st + d
+            for j in pred[k]:
+                left[j] -= 1
+                if not left[j]:
+                    rdy.append(j)
+        return np.array(end)
+
     pr = np.array(pri)
-    for a, b, d in NUDGE:
-        pr[a:b] += d
-    best = place(pr, BIAS)
+    got = best = place(pr, BIAS)
+    for it in range(TURNS):
+        p2 = back(got)
+        got = place(p2, BIAS)
+        if got[0] < best[0]:
+            best, pr = got, p2
+    now = best
     rng = np.random.RandomState(SEARCH[1])
     for it in range(SEARCH[0]):
         a = int(rng.randint(0, n))
@@ -849,16 +925,54 @@ def schedule():
         p2 = pr.copy()
         p2[a:b] += d
         got = place(p2, BIAS)
-        if got[0] < best[0]:
-            best, pr = got, p2
-            NUDGE.append((a, b, d))
+        if got[0] < now[0] + 1500 and it % 4 == 0:
+            p3 = back(got)
+            g3 = place(p3, BIAS)
+            if g3[0] < got[0]:
+                got, p2 = g3, p3
+        if got[0] < now[0] + 150 * (1 - it / SEARCH[0]):
+            now, pr = got, p2
+            if got[0] < best[0]:
+                best = got
+
+    def weigh(got):
+        use, total = got[1], 0.0
+        order = sorted(range(n), key=lambda k: (got[2][k], k))
+        for sc, ga, sync, pe, far, unit in RANGES:
+            free, done = dict(v=0.0, s=0.0, t=0.0, g=0.0, y=0.0, n=0.0), [0.0] * n
+            for k in order:
+                o, e, c = OPS[k], use[k][0], use[k][2]
+                c = 60 + (c - 60) * sc if o["sc"] else 70 + (c - 70) * ga if o["ga"] else c * pe if e == "t" else c
+                st = free[e]
+                for i, soft in near[k]:
+                    r = done[i] - sync if soft and use[i][0] == e else done[i]
+                    if r > st:
+                        st = r
+                if e != "n":
+                    free[e] = st + c + 20
+                done[k] = st + c + o.get("lat", 0) * (far if "send" in o else 1) + sync
+            total += max(done) / unit
+        return total
+
+    mark = weigh(best)
+    pr = np.array([-best[2][k] for k in range(n)])
+    for it in range(SEARCH[2]):
+        a = int(rng.randint(0, n))
+        p2 = pr.copy()
+        p2[a:a + int(rng.choice([1, 3, 10, 30]))] += int(rng.choice([-1, 1]) * rng.choice([300, 1000, 3000, 10000]))
+        got = place(p2, BIAS)
+        if got[0] < best[0] + 2500:
+            m = weigh(got)
+            if m < mark:
+                best, pr, mark = got, p2, m
     for k in range(n):
         OPS[k]["use"], OPS[k]["at"] = best[1][k], best[2][k]
     return sorted(range(n), key=lambda k: (best[2][k], k)), best[0]
 
 
-SYNC, BIAS, SEARCH = 100.0, 300.0, [0, 1]
-NUDGE = [(586, 587, -1000), (896, 897, 30000), (532, 612, 30000), (489, 499, -3000), (253, 333, 3000), (206, 209, 10000), (317, 397, 3000), (506, 516, -3000), (358, 388, -1000), (1007, 1010, 1000), (117, 120, -3000), (249, 329, -300), (633, 643, -3000), (976, 1056, -1000), (849, 879, -1000), (849, 879, -1000), (488, 498, 1000), (858, 861, 3000), (304, 384, -300), (432, 462, -1000), (991, 1001, 3000), (924, 925, 3000), (913, 943, -300), (628, 658, -1000), (704, 707, 1000), (932, 962, -300), (909, 919, 1000), (987, 990, 1000), (582, 612, 10000), (621, 631, -3000), (517, 547, 10000), (664, 667, -300), (850, 860, 1000), (740, 741, -3000), (566, 569, -30000), (952, 955, 10000), (563, 566, -3000), (965, 975, -300), (853, 856, 3000), (381, 411, -3000), (946, 1026, 300), (922, 923, 1000)]
+SYNC, BIAS, TURNS, SEARCH = 120.0, 500.0, 30, [2000, 2, 2600]
+RANGES = [(1.0, 1.0, 120, 1.0, 1.0, 195.0), (1.4, 1.3, 120, 1.0, 1.0, 235.0), (0.45, 0.75, 120, 1.0, 1.8, 180.0), (1.0, 1.0, 250, 1.3, 1.4, 235.0)]
+
 program()
 ORDER, SPAN = schedule()
 SCRATCH = {"p" + k: ("sbuf", [128, v[1]], v[0]) for k, v in POOL.items()}

@@ -81,9 +81,13 @@ def psum(ap):
     return ap[0] in SHAPES and SHAPES[ap[0]][0] == "psum"
 
 
+def reg(ap):
+    st = ap[1][1].step if len(ap[1]) == 2 and isinstance(ap[1][1], slice) and ap[1][1].step else 1
+    return ap[0:1] + ap[2:4] + (st, sum(1 << p for p in range(128)[ap[1][0]]))
+
+
 def op(alts, outs, ins, **kw):
     rd, wr = [], []
-    reg = lambda ap: ap[0:1] + ap[2:4] + (ap[1][1].step if len(ap[1]) == 2 and isinstance(ap[1][1], slice) and ap[1][1].step else 1,)
     for ap in ins:
         if isinstance(ap, tuple):
             rd.append(reg(ap))
@@ -194,18 +198,26 @@ def iota(out, pat, base, cm=0):
     op([("g", f, 160 + 2 * out[4])], [out], [])
 
 
-def asel(out, cmp, fill, base, cm):
-    op([("g", lambda g, T: g.affine_select(real(T, out), real(T, out), [[0, 1]], cmp, fill, base, cm), 205)], [out], [out])
+def asel(out, cmp, fill, base, cm, pat=None, in_=None):
+    in_ = in_ or out
+    op([("g", lambda g, T: g.affine_select(real(T, out), real(T, in_), pat or [[0, 1]], cmp, fill, base, cm), 205 + 2 * out[4])], [out], [in_])
 
 
-def dma(out, in_, q="y", lat=2600):
+def silu(out, in_, once=0):
+    op([("s", lambda g, T: g.scalar.activation(real(T, out), real(T, in_), AF.Silu), 80 + 4.2 * out[4] + once)], [out], [in_])
+
+
+def dma(out, in_, q="y", lat=2600, add=False):
     s = "d%d" % len(SEMS)
     SEMS.append(s)
 
     def f(g, T):
+        if add:
+            return g.dma_start(real(T, out), real(T, in_), accum_op=ADD)
         e = g.sync if q == "y" else g.scalar if q == "s" else g
         return e.dma_start(real(T, out), real(T, in_))
-    op([(q, f, 1200 if q == "g" else 100)], [out], [in_], sem=s, inc=16, lat=lat)
+    op([(q, f, 1200 if q == "g" else 100)], [out], [in_] + [out] * add, sem=s, inc=16, lat=lat)
+    OPS[-1]["wr"] = [(r[0], r[1] // 8 * 8, r[2] // 8 * 8 + 7) + r[3:] for r in OPS[-1]["wr"]]
 
 
 def send(dst, src, step, lat):
@@ -216,20 +228,23 @@ def send(dst, src, step, lat):
 
 
 PEC = 0.6
-OPT = [[], [0, 2], [0, 2, 4]]
+CV = 100
+LOW = 65
+TOP = LOW + 16
+CLAMP = [(0, 21), (21, 45), (45, 66)]
 
 
 def program():
     f, b, h, ii, u = (lambda n: al("f", n)), (lambda n: al("b", n)), (lambda n: al("h", n)), (lambda n: al("i", n)), (lambda n: al("u", n))
-    B = [own("B%d" % k, "psum", [128, 512], "float32") for k in range(6)]
-    C = own("C", "psum", [128, 1024], "float32")
-    DD, CC = f(3168), h(3168)
+    B = [own("B%d" % k, "psum", [128, 512], "float32") for k in range(8)]
+    WS = f(5760 + 16 * (198 - CV))
+    YM, DD, CC = WS[:2] + (3072,), (WS[0], WS[1] + WS[2] - 3168, 3168), h(3168)
     SEL = own("SEL", "sbuf", [128, 16, 144], "bfloat16")
     BL = own("BL", "sbuf", [128, 12, 128], "bfloat16")
     L1, R2 = u(480), f(128)
-    UD = own("UD", "sbuf", [128, 66, 3], "float32")
-    UL, DL, J3, K3 = (own(n, "sbuf", [128, 3, 66], "float32") for n in ("UL", "DL", "J3", "K3"))
     XL = own("XL", "sbuf", [128, 4032], "bfloat16")
+    SD = b(16 * CV + 3520)
+    XM, SF = (SD[0], SD[1] + 16 * CV, 3520), f(16 * (198 - CV))
     XW = [ii(1040), ii(1040)]
     EN, NB = XW[0][:2] + (480,), (XW[0][0], XW[0][1] + 480, 480)
     UW = own("UW", "sbuf", [128, 8704], "bfloat16")
@@ -268,9 +283,9 @@ def program():
              ("pd", [0] * 12 + [1920, 22 * 8192 + 3072, 0, 1]), ("fd", [0] * 12 + [1920, 22.375, 0, 1]),
              ("dg", [1] * 12 + [1 / 128, 0, 0, -13])]
     late = [("vb", {13: 262144, 14: 8192, 15: -90112}), ("got", {13: 32, 14: 1, 15: -12}), ("wa", {0: 1, 1: 16, 2: 48}),
-            ("wb", {0: 1, 1: 16, 3: 48}), ("sa", {1: 192, 2: 16, 3: 1}), ("sb", {1: 192, 2: 1, 3: 16}),
-            ("upd", {12: 1, 13: 262144, 14: 8192, 15: 32}), ("nmc", {12: 1, 13: -0.375, 14: 1, 15: 63})]
-    W16, WC, W = f(16), f(32), {}
+            ("wb", {0: 1, 1: 16, 3: 48}), ("sa", {1: 16, 2: 48, 3: 1}), ("sb", {1: 16, 2: 1, 3: 48}),
+            ("upd", {12: 1, 13: 262144, 14: 8192, 15: 32}), ("zz", {0: 1, 1: 16, 4: 48}), ("aa", {0: 1, 1: 16})]
+    W16, WC, W = f(32), f(48), {}
     for k, (n, w) in enumerate(early):
         for r in range(16, 0, -1):
             if r == 16 or w[r - 1] != w[r]:
@@ -278,22 +293,24 @@ def program():
         W[n] = col(WC, k)
     mm([(A(B[2], 0, 6), A(OH, p=(0, 16)), A(W16, 0, 6, p=(0, 16)), True, True)])
     cp(A(WC, 0, 6), A(B[2], 0, 6))
-    ms(A(W16, 8, 16, p=(0, 16)), 0.0)
+    ms(A(W16, 8, 17, p=(0, 16)), 0.0)
     for e in range(4):
         for k, (n, w) in enumerate(late):
             if e < len(w):
                 r = sorted(w)[e]
                 asel(A(W16, 8 + k, 9 + k, p=(0, 16)), NE, float(w[r]), -r, 1)
             W[n] = col(WC, 8 + k)
-    mm([(A(B[5], 0, 8), A(OH, p=(0, 16)), A(W16, 8, 16, p=(0, 16)), True, True)])
-    cp(A(WC, 8, 16), A(B[5], 0, 8))
-    for k, (n, o, v, w) in enumerate([("s01", LT, 2, 1), ("o14", LT, 14, 1), ("w640", LT, 12, -320), ("l12", LT, 12, 1),
-                                      ("cm", GE, 12, 1), ("cx", EQ, 12, 1920), ("ps", GE, 13, 1), ("n15", LT, 15, 1), ("m12", LT, 12, -1)]):
-        W[n] = col(WC, 16 + k)
+    mm([(A(B[5], 0, 9), A(OH, p=(0, 16)), A(W16, 8, 17, p=(0, 16)), True, True)])
+    cp(A(WC, 8, 17), A(B[5], 0, 9))
+    for k, (n, o, v, w) in enumerate([("s01", LT, 2, 1), ("o14", LT, 14, 1), ("w640", LT, 12, -320), ("l12", LT, 12, 1), ("cm", GE, 12, 1),
+                                      ("cx", EQ, 12, 1920), ("ps", GE, 13, 1), ("n15", LT, 15, 1), ("m12", LT, 12, -1), ("p0", GE, 1, 1)]):
+        W[n] = col(WC, 20 + k)
         ts(W[n], PM, float(v), o, float(w), MUL)
-    W["uba"], W["wu"] = col(WC, 26), col(WC, 27)
+    W["uba"], W["wu"], W["z14"], W["n14"] = col(WC, 32), col(WC, 33), col(WC, 34), col(WC, 35)
     tt(W["uba"], W["vb"], W["n15"], MUL)
     tt(W["wu"], W["got"], W["n15"], MUL)
+    ts(W["z14"], col(OH, 15), 553 / 2048, MUL, W["o14"], ADD)
+    ts(W["n14"], col(OH, 15), -553 / 4096, MUL, W["o14"], SUB)
 
     def zt(n, kind="b"):
         z = al(kind, 144)
@@ -306,59 +323,48 @@ def program():
         return A(z)
     ZKEY = zt("key")
     BKEY, BDG, BS01, BVB, BGOT, PAS = bt("key"), bt("dg"), bt("s01"), bt("vb"), None, bt("ps", ID)
-    Z14, ZL12, ZA, ZBB, ZSA, ZSB, Z640, ZU, ZUP = zt("o14", "h"), zt("l12"), zt("wa"), zt("wb"), zt("sa"), zt("sb"), zt("w640"), zt("wu"), zt("upd")
-    for i in range(16):
-        lin(A3(SEL, i), A(ZB), col(OH, i), 0.0)
-    for i in range(12):
-        lin(A3(BL, i), A(BD), col(OH, i), 0.0)
+    Z14, ZL12, ZA, ZBB, ZSA, ZSB, Z640, ZU, ZUP = zt("z14", "h"), zt("l12"), zt("wa"), zt("wb"), zt("sa"), zt("sb"), zt("w640"), zt("wu"), zt("upd")
+    ZZ, ZAA, ZN14 = zt("zz"), zt("aa"), zt("n14", "f")
+    ZT, ONE = b(1024), b(512)
+    ms(A(ZT), 0.0)
+    for i in range(0, 16, 4):
+        dma(A3(SEL, slice(i, i + 4)), A(ZT, 0, 576), "ys"[i // 4 % 2])
+    asel(A3(SEL, ALL, slice(15, 144, 16)), NE, 1.0, 0, 1, [[-1, 16], [-16, 9]])
+    for i in range(0, 12, 4):
+        dma(A3(BL, slice(i, i + 4)), A(ZT, 0, 512))
+        asel(A3(BL, slice(i, i + 4)), NE, 1.0, -i, 1, [[-1, 4], [-16, 8], [0, 16]])
     PERM, pc = f(96), f(2)
     ts(col(pc, 0), PG, -4.0, MUL, col(PJ, 0), ADD)
     ts(col(pc, 1), W["cx"], col(pc, 0), ADD)
     ts(col(pc, 0), W["ps"], 1920.0, MUL, col(pc, 1), ADD)
     ts(A(PERM), A(XZ, 15, 111), col(pc, 0), EQ)
-    ZN14, NPM = f(144), f(1)
-    ts(A(NPM), PM, -1.0, MUL)
-    ts(A(ZN14), A(ZB), W["o14"], MUL, -1.0, MUL)
-    Z0F = f(144)
-    lin(A(Z0F), A(ZB), col(OH, 0), 0.0)
-    TS, SFX, NBD, UBM, t1, t2 = b(128), b(128), b(128), b(128), f(128), f(128)
-    ts(A(t1), A(X16), PM, GT)
-    tt(A(TS), A(t1), A(BD), MUL)
-    t3 = f(128)
-    ts(A(t3), A(X16), PM, LT, W["m12"], MUL)
-    tt(A(SFX), A(t3), A(BD), MUL)
+    NPM = f(1)
+    ts(A(NPM), PM, -1.0, MUL, -float(TOP), ADD)
+    TS, SFX, NBD, UBM, t2 = b(128), b(128), b(128), b(128), f(128)
+    asel(A(TS), GT, 0.0, 0, -1, [[1, 128]], A(BD))
+    asel(A(SFX), GT, 0.0, 0, 1, [[-1, 128]], bt("m12"))
     lin(A(NBD), A(BD), -1.0, 0.0)
-    ms(A(R2), -88064.0)
-    ms(A(R2, 12, 128, 16), -716.0 * 8192)
-    ms(A(R2, 13, 128, 16), 182272.0)
+    fl = lambda out, c: iota(out, [[0, out[4]]], c)
+    fl(A(R2), -88064)
+    fl(A(R2, 12, 128, 16), -716 * 8192)
+    fl(A(R2, 13, 128, 16), 182272)
+    fl(A(R2, 15, 128, 16), 4096)
     t4, t5 = f(128), f(128)
     ts(A(t2), A(X16), 13.0, LT, W["uba"], MUL)
     lin(A(t4), A(R2), col(OH, 15), 0.0)
     tt(A(t5), A(t2), A(t4), ADD)
     tt(A(UBM), A(t5), A(BD), MUL)
-    ZT, ONE = b(1024), b(512)
-    ms(A(ZT), 0.0)
-
-    def fl(out, c):
-        ms(out, c)
-        z = A(ZT, 0, out[4])
-        OPS[-1]["alts"].append(act_alt(out, z, AF.Identity, c, 1.0, None))
-        OPS[-1]["rd"].append(z[0:1] + z[2:4] + (1,))
-    fl(A(ONE), 1.0)
-    M3, M4, NID = b(512), b(512), b(128)
-    fl(A(M3), 9.0)
-    fl(A(M4), 10.0)
-    fl(A(XL, 2048, 3072), 255.0)
-    fl(A(XL, 3072, 4032), 255.0)
+    fl(A(ONE), 1)
+    MB, MF, NID = b(512), f(512), b(128)
+    fl(A(MB), LOW)
+    fl(A(MF), LOW)
     lin(A(NID), A(ID), -1.0, 0.0)
-    P, F, W2, Y, PFU, ST, WW, RR = f(1280), b(1280), b(656), b(656), b(656), f(592), f(256), ii(208)
+    P, F, W2, Y, PFU, ST, WW = f(1280), b(1280), b(656), b(576), b(656), b(592), b(256)
     lin(A(P, 0, 16), A(ZT, 0, 16), 1.0, W["pd"])
     lin(A(P, 656, 1280), A(ZT, 0, 624), 1.0, W["pd"], "s")
     lin(A(F, 0, 16), A(ZT, 0, 16), 1.0, W["fd"])
     lin(A(F, 656, 1280), A(ZT, 0, 624), 1.0, W["fd"])
     ms(A(W2, 0, 16), 0.0)
-    ms(A(Y, 576, 624), 255.0)
-    ms(A(Y, 624, 656), 0.0)
     ms(A(PFU, 576, 656), 0.0)
     ms(A(ST, 576, 592), 0.0)
     GR, LGT, gi, gc_, gf = f(96), u(4), ii(3), f(3), f(3)
@@ -374,7 +380,6 @@ def program():
     tt(A(gf), A(gf), A(gc_), ADD)
     cp(A(LGT, 0, 3), A(gf))
     ms(A(WW, 192, 256), 0.0)
-    ms(A(RR, 192, 208), 0)
 
     def clear():
         for k in range(8):
@@ -382,7 +387,8 @@ def program():
 
     def fill(t):
         for k in range(5 + t):
-            dma(A(MW, 512 * k, 512 * (k + 1)), A(M3 if k < 4 + t else M4), "y", 4000)
+            dma(A(MW, 512 * k, 512 * (k + 1)), A(MB), "y", 4000)
+            dma(A(WS, 512 * k, 512 * (k + 1)), A(MF), "y", 4000)
     fill(0)
     CI, CE, CF, LVS = ii(40), ii(40), f(40), u(40)
     iota(A(CI), [[1, 40]], 0)
@@ -421,80 +427,73 @@ def program():
     tr(A(TT, 0, 640), A(TIN, 16, 656))
     tr(A(TT, 640, 1312), A(TIN))
     cp(A(P, 16, 656), IND(A(TT), A(LVS)), "vs")
-    off = [0]
-    for d in range(1, 12):
-        off.append(off[-1] + 12 - d)
     lex = [0]
     for j in range(11):
         lex.append(lex[-1] + 11 - j)
-    for d in range(1, 12):
-        iota(A3(UD, slice(off[d - 1], off[d])), [[17, 12 - d], [192, 3]], d + 1)
+    row = lambda t, r, *s: A(t, *s, p=(r, 128, 16))
+    DG, DC, DJ, DQ, OI = b(208), b(208), b(208), b(208), f(16)
     for j in range(11):
-        iota(A3(UL, ALL, slice(lex[j], lex[j + 1])), [[192, 3], [1, 11 - j]], 17 * j + 2)
-        iota(A3(DL, ALL, slice(lex[j], lex[j + 1])), [[192, 3], [16, 11 - j]], 17 * j + 17)
-        iota(A3(J3, ALL, slice(lex[j], lex[j + 1])), [[0, 3], [0, 11 - j]], j)
-        iota(A3(K3, ALL, slice(lex[j], lex[j + 1])), [[0, 3], [1, 11 - j]], j + 1)
-    YM = f(3072)
-    sub = lambda o, n: (YM[0], YM[1] + o, n)
-    R3, E2, CR, KK, JJ = sub(0, 624), sub(624, 208), b(198), b(198), b(198)
-    iota(A(E2), [[1, 208]], 0)
-    iota(A(CR), [[1, 3], [0, 66]], 0)
-    for k in range(3):
-        lin(A(R3, 208 * k + 198, 208 * k + 208), A(E2, 0, 10), 1.0, 576.0)
-        cp(A(R3, 208 * k, 208 * k + 198), A3((UD, UL, DL)[k]), "vs")
-    cp(A(JJ), A3(J3), "vs")
-    cp(A(KK), A3(K3), "vs")
-    parts = acc(A(B[5], 0, 39), ext(None, Z0F, R3, 39))
-    for k in range(0, 16, 4):
-        mm(parts[k:k + 4])
-    LUD, LUP, LDN, LEX, LSQ = u(14), u(14), u(14), u(14), u(36)
-    for k, l in enumerate((LUD, LUP, LDN)):
-        cp(A(l, 0, 13), A(B[5], 13 * k, 13 * k + 13))
-    S1, S2, SX = sub(1248, 592), sub(1840, 592), sub(2432, 208)
-    fl(A(S1), 198.0)
-    fl(A(S2), 198.0)
-    iota(A(S2, 0, 576, 16), [[1, 3], [3, 12]], 200)
-    cp(IND(A(S1), A(LUD, 0, 13)), A(E2))
-    cp(IND(A(S2), A(LUP, 0, 13)), A(E2))
-    cp(IND(A(S2), A(LDN, 0, 13)), A(E2))
-    cp(A(SX), IND(A(S1), A(LUP, 0, 13)))
-    parts = acc(A(B[5], 0, 13), ext(None, Z0F, SX, 13)) + acc(A(B[5], 16, 52), ext(None, Z0F, S2, 36))
-    for k in range(0, 32, 4):
-        mm(parts[k:k + 4])
-    cp(A(LEX, 0, 13), A(B[5], 0, 13))
-    cp(A(LSQ), A(B[5], 16, 52))
-    DG, SD, OI = f(198), b(3168), f(16)
-    mm(acc(A(B[5], 0, 198), [(A3(SEL, 0, slice(14, 142)), A(CR)), (A3(SEL, 0, slice(13, 141)), A(JJ)), (A3(SEL, 0, slice(12, 140)), A(KK))]))
-    cp(A(DG), A(B[5], 0, 198), "vs")
-    lin(A(OI), A(X16, 0, 16), col(OH, 0), 0.0)
+        iota(A(DG, 3 * lex[j], 3 * lex[j + 1]), [[1, 11 - j], [0, 3]], 17 + j)
+        fl(A(DJ, 3 * lex[j], 3 * lex[j + 1]), 16 + j)
+    fl(A(DG, 198, 208), LOW)
+    iota(A(DC, 0, 198), [[0, 66], [1, 3]], 16)
+    iota(A(DQ, 0, 198), [[1, 66], [0, 3]], 16)
+    for r, t in ((1, DC), (2, DJ), (4, DQ)):
+        dma(row(DG, r, 0, 198), row(t, r, 0, 198))
+    LUP, LDN, LSQ = u(14), u(14), u(36)
+    mm(acc(A(B[5], 0, 13), ext(None, ZSA, DG, 13)) + acc(A(B[5], 16, 29), ext(None, ZSB, DG, 13)))
+    ts(A(LUP, 0, 13), A(B[5], 0, 13), 1.0 - 16 * 65, ADD, 591.0, MIN)
+    ts(A(LDN, 0, 13), A(B[5], 16, 29), 1.0 - 16 * 65, ADD, 591.0, MIN)
+    QJ, QC3, QE, q1, q2, q3, qk = f(36), f(36), f(36), f(36), f(36), f(36), f(4)
+    iota(A(QJ), [[1, 12], [0, 3]], 0)
+    iota(A(QC3), [[0, 12], [1, 3]], -3)
+    iota(A(QE), [[1, 36]], -3)
+    ts(col(qk, 0), PM, -1.0, ADD)
+    ts(col(qk, 1), col(qk, 0), -1.5, MUL, 31.5, ADD)
+    ts(col(qk, 1), col(qk, 1), col(qk, 0), MUL)
+    ts(col(qk, 1), col(OH, 0), 236.0, MUL, col(qk, 1), ADD)
+    ts(col(qk, 2), col(qk, 0), 3.0, MUL)
+    ts(A(q1), A(QJ), -1.5, MUL, 31.5, ADD)
+    tt(A(q1), A(q1), A(QJ), MUL)
+    tt(A(q1), A(q1), A(QC3), ADD)
+    ts(A(q1), A(q1), col(qk, 2), ADD)
+    ts(A(q2), A(QJ), col(qk, 0), LT)
+    tt(A(q1), A(q1), A(q2), MUL)
+    ts(A(q2), A(QE), col(qk, 1), ADD)
+    ts(A(q3), A(QJ), col(qk, 0), GT)
+    tt(A(q2), A(q2), A(q3), MUL)
+    ts(A(q3), A(QJ), col(qk, 0), EQ, 198.0, MUL)
+    tt(A(q1), A(q1), A(q2), ADD)
+    tt(A(q1), A(q1), A(q3), ADD)
+    cp(A(LSQ), A(q1))
+    ts(A(OI), A(X16, 0, 16), 16.0, ADD, col(OH, 0), MUL)
     for i in range(16):
-        lin(A(SD, i, 3168, 16), A(DG), 1.0, col(OI, i))
-    RS1, RS2 = f(576), f(198)
-    fl(A(RS1), 1.0)
-    ms(A(RS1, 0, 576, 16), 0.0)
-    fl(A(RS2), 1.0)
-    ms(A(RS2, 0, 198, 66), 0.0)
+        lin(A(SD, i, 3168, 16), A(DG, 0, 198), W["p0"], col(OI, i))
+    dma(A(SF), A(SD, 16 * CV, 3168), "g", 4000)
+    RS1 = b(576)
+    fl(A(RS1), 1)
+    fl(A(RS1, 0, 576, 16), 0)
     N1, N2, NM = b(512), b(512), [b(512), b(512)]
-    iota(A(N1), [[0, 16], [1, 32]], 0)
-    iota(A(N2), [[1, 16], [0, 32]], 0)
-    lin(A(N1), A(N1), col(OH, 12), W["nmc"])
-    lin(A(N2), A(N2), col(OH, 15), 0.0)
-    mm(acc(A(B[5]), [(A(ID), A(N1)), (A(ID), A(N2))]))
-    cp(A(NM[0]), A(B[5]), "vs")
-    O16 = f(1)
-    ts(A(O16), col(OH, 15), 16.0, MUL)
-    lin(A(NM[1]), A(NM[0]), 1.0, A(O16))
+    fl(A(N1), -11)
+    for t in range(2):
+        iota(A(NM[t]), [[0, 16], [1, 32]], 1)
+        iota(A(N2), [[1, 16], [0, 32]], 63 + 16 * t)
+        for r, s in ((13, ZT), (14, N1), (15, N2)):
+            dma(row(NM[t], r), row(s, r, 0, 512))
     JG, JU, JM, JP, JQ = f(3), f(36), f(198), f(64), f(64)
-    for t, n, m, c in ((JG, 3, 1.0, 656.0), (JU, 36, 8192.0, 641.0 * 8192), (JM, 198, 1.0, 5760.0), (JP, 64, 1.0, 7681.0), (JQ, 64, 1.0, 3852.0)):
+    for t, n, m, c in ((JG, 3, 1.0, 656.0), (JU, 36, 8192.0, 641.0 * 8192), (JP, 64, 1.0, 7681.0), (JQ, 64, 1.0, 3852.0)):
         lin(A(t), A(J, 0, n), m, c)
-    MID, GOT = f(192), f(1200)
-    fl(A(MID), 0.0)
-    ms(A(GOT, 0, 16), -1.0)
-    ms(A(GOT, 592, 608), -1.0)
-    ms(A(GOT, 1184, 1200), -1.0)
+    lin(A(JM, 0, CV), A(J, 0, CV), 1.0, 5760.0 - 552)
+    lin(A(JM, CV, 198), A(J, 0, 198 - CV), 1.0, 5760.0 - 552)
+    MID, GOT = f(192), f(128)
+    fl(A(MID), 0)
+    fl(A(GOT), -1)
 
     RH, PV = UW, NX
-    GA, GB, LTT = b(3072), b(3072), (MW, 5760, 3072)
+    ZD, GB, LTT = b(3200), b(1920), (MW, 5760, 3072)
+    ms(A(ZD, 3168, 3184), 0.0)
+    ms(A(ZD, 3184, 3200), 255.0)
+    GA = ZD
 
     def choose(t):
         SCOPE[:] = ["a", 0]
@@ -562,26 +561,40 @@ def program():
         ts(A(GH), A(GV, 0, 36), MAGIC, ADD, MAGIC, SUB)
         tt(A(GH), A(GV, 0, 36), A(GH), SUB)
         ts(A(LE_), A(GH), -1.0, ADD)
-        cp(A(Y, 0, 576), IND(A(XL), A(LE_)), "s")
+        XO, XN = (XL, XM)[t], (XM, XL)[t]
+        cp(A(Y), IND(A(XO, 0, n0), A(LE_)), "s")
         if store:
             store()
-        mm([(A(C, 0, 512), A(UBM), A(FU, 0, 512), True, True), (A(C, 512, 576), A(UBM), A(FU, 512, 576), True, True)])
-        for d0, d1 in ((1, 3), (3, 6), (6, 12)):
-            for d in range(d0, d1):
-                tt(A(DD, 48 * off[d - 1], 48 * off[d]), A(NR, 0, 48 * (12 - d)), A(C, 48 * d, 576), SUB)
-            q0, q1 = off[d0 - 1], off[d1 - 1]
-            if d0 == 1:
-                act(A(DD, 0, 1008), A(DD, 0, 1008), AF.Relu, 2048.0)
-                act(A(DD, 0, 1008), A(DD, 0, 1008), AF.Relu, 4096.0, -1.0)
-                mm(acc(A(B[3], 0, 63), ext(None, ZN14, DD, 63)))
+        tiles = [(0, 6), (6, 11), (11, 21), (21, 30), (30, 38), (38, 45), (45, 51), (51, 60), (60, 66)]
+        runs = lambda q0, q1: [(j, max(q0, lex[j]), min(q1, lex[j + 1])) for j in range(11) if lex[j] < q1 and q0 < lex[j + 1]]
+        for x, (q0, q1) in enumerate(tiles):
+            bk = B[4 + x % 4]
+            mm([(A(bk, 48 * (q - q0), 48 * (q - q0 + 1)), A(UBM), A(FU, 48 * j, 48 * j + 48), True, True) for j, a0, a1 in runs(q0, q1) for q in range(a0, a1)])
+            for j, a0, a1 in runs(q0, q1):
+                k0 = j + 1 - lex[j]
+                tt(A(DD, 48 * a0, 48 * a1), A(NR, 48 * (k0 + a0), 48 * (k0 + a1)), A(bk, 48 * (a0 - q0), 48 * (a1 - q0)), SUB)
+        for x, (q0, q1) in enumerate(CLAMP):
+            if x == 0:
+                act(A(DD, 0, 48 * q1), A(DD, 0, 48 * q1), AF.Relu, 2048.0)
+                act(A(DD, 0, 48 * q1), A(DD, 0, 48 * q1), AF.Relu, 4096.0, -1.0)
+                mm(acc(A(B[0], 0, 3 * q1), ext(None, ZN14, DD, 3 * q1)))
                 continue
             ts(A(CC, 48 * q0, 48 * q1), A(DD, 48 * q0, 48 * q1), -2048.0, MAX, 2048.0, MIN)
             mm(acc(A(B[0], 3 * q0, 3 * q1), ext(None, Z14, CC, 3 * (q1 - q0), 48 * q0)))
+        for x, q0 in enumerate(range(0, 66, 10)):
+            q1, bk, parts = min(q0 + 10, 66), B[4 + x % 2], []
+            for j, a0, a1 in runs(q0, q1):
+                k0 = j + 1 - lex[j]
+                parts += [(A(bk, 48 * (a0 - q0), 48 * (a1 - q0)), A(ID), A(Y, 48 * (k0 + a0), 48 * (k0 + a1)), True, False)]
+                parts += [(A(bk, 48 * (q - q0), 48 * (q - q0 + 1)), A(ID), A(Y, 48 * j, 48 * j + 48), False, q == a1 - 1) for q in range(a0, a1)]
+            mm(parts)
+            cp(A(ZD, 48 * q0, 48 * q1), A(bk, 0, 48 * (q1 - q0)), "vs")
         act(A(NK), A(NR), AF.Identity, MAGIC)
         act(A(NH), A(NK), AF.Identity, -MAGIC)
         for k in range(2):
             mm([(A(B[1 + k], 48 * j, 48 * j + 48), BVB, A(FG), True, True) for j in range(6)])
-            lin(A(GOT, 592 * t + 16 + 288 * k, 592 * t + 304 + 288 * k), A(B[1 + k], 0, 288), U13, -1.0, "s")
+            if k == 0:
+                lin(A(GOT, 64 * t + 16, 64 * t + 64), A(B[1], 0, 48), U13, -1.0)
             s = (288 * k, 288 * k + 288)
             tt(A(NK, *s), A(B[1 + k], 0, 288), A(NH, *s), SUB)
             act(A(B[1 + k], 0, 288), A(NK, *s), AF.Abs, 0.0, 1024.0)
@@ -597,40 +610,42 @@ def program():
             cp(IND(A(P), A(LU, c, c + 12)), A(NK, 16 * c, 16 * c + 192))
         ts(A(GC), A(GR, 16, 64), W["cm"], MUL, W["cx"], MAX)
         cp(IND(A(P), LG), A(GC))
-        RI, RL, SQ, SU, SV, IN, TO, OF, JC, EE, LM = ii(198), f(208), f(576), f(208), f(208), f(198), b(4), f(198), f(198), f(198), u(198)
-        NW = f(198)
-        ts(A(RI, 0, 63), A(B[3], 0, 63), 65535.0, ADD)
-        ts(A(RI, 63, 198), A(B[0], 63, 198), 65535.0, ADD)
-        ts(A(RR, 0, 198), A(RI), 4095, AND)
-        cp(A(RL), IND(A(RR), A(LEX, 0, 13)))
-        ts(A(WW, 0, 198), A(RL, 0, 198), 4095.0, EQ)
-        NW, JC, EE = (C, 0, 198), (C, 512, 198), (B[2], 0, 198)
-        act(A(NW), A(RL, 0, 198), AF.Relu, 4095.0, -1.0)
-        act(A(JC), A(RL, 0, 198), AF.Relu, -2559.5 * 32768, 32768.0)
+        RH_, RL, SQ, SU, SV, IN, OF, LM = f(198), f(198), b(576), b(208), b(208), b(198), f(198), u(200)
+        ts(A(RH_), A(B[0], 0, 198), MAGIC / 2, ADD, MAGIC / 2, SUB)
+        tt(A(RL), A(B[0], 0, 198), A(RH_), SUB)
+        ts(A(WW, 0, 198), A(RL), -553.0, EQ)
+        NW, JC, EE = (B[6], 0, 198), (B[7], 0, 198), (B[2], 0, 198)
+        act(A(NW), A(RL), AF.Abs, 553.0)
+        lin(A(JC), A(RL), -32768.0, -552.5 * 32768)
         cp(A(SQ), IND(A(WW), A(LSQ)))
         scan(A(ST, 0, 576), A(RS1), A(SQ), MUL, ADD)
         cp(A(SU), IND(A(ST), A(LUP, 0, 13)))
         tt(A(SV), IND(A(ST), A(LDN, 0, 13)), A(SU), MAX)
         tt(A(SV, 0, 198), A(SV, 0, 198), A(NW), MAX)
         ts(A(SU, 0, 198), A(SV, 0, 198), 0.0, LE)
-        scan(A(IN), A(RS2), A(SU, 0, 198), MUL, ADD)
-        act(A(EE), A(SV, 0, 198), AF.Relu, 0.0, 16384.0)
-        cp(A(TO, 0, 3), A(IN, 65, 198, 66))
-        mm([(A(B[1], 0, 3), A(TS), A(TO, 0, 3), True, False), (A(B[1], 1, 3), A(BD), A(TO, 0, 2), False, False), (A(B[1], 2, 3), A(BD), A(TO, 0, 1), False, True)])
-        tt(A(JC), A(JC), A(JM), MIN)
-        tt(A(JC), A(JC), A(RL, 0, 198), MAX)
-        tt(A(IN), A(IN), A(EE), ADD)
         for c in range(3):
-            ts(A(OF, 66 * c, 66 * c + 66), A(IN, 66 * c, 66 * c + 66), col(B[1], c), ADD, float(n0 - 1), ADD)
+            scan(A(IN, c, 198, 3), A(ONE, 0, 66), A(SU, c, 198, 3), MUL, ADD)
+        act(A(EE), A(SV, 0, 198), AF.Relu, 0.0, 16384.0)
+        mm([(A(B[1], 0, 3), A(TS), A(IN, 195, 198), True, False), (A(B[1], 1, 3), A(BD), A(IN, 195, 197), False, False), (A(B[1], 2, 3), A(BD), A(IN, 195, 196), False, True)])
+        tt(A(JC), A(JC), A(JM), MIN)
+        tt(A(JC), A(JC), A(RL), MAX)
+        tt(A(OF), A(IN), A(EE), ADD)
+        for c in range(3):
+            ts(A(OF, c, 198, 3), A(OF, c, 198, 3), col(B[1], c), ADD, float(n0 - 553), ADD)
         tt(A(OF), A(JC), A(OF), MIN)
-        cp(A(LM), A(OF))
-        cp(IND(A(MW), A(LM)), A(SD))
-        LA, LB, LN, LS, AN = u(192)[:2] + (nc,), u(192)[:2] + (nc,), u(64), u(64), f(64)
+        ts(A(LM, 0, 198), A(OF), 552.0, ADD)
+        cp(IND(A(MW), A(LM, 0, CV)), A(SD, 0, 16 * CV))
+        silu(IND(A(WS), A(LM, CV, 198)), A(SF), 1570 * (t == 0))
+        tt(A(MW, n0, n), A(MW, n0, n), A(WS, n0, n), ADD)
+        olds = [(c, min(c + 1024, n0)) for c in range(0, n0, 1024)]
+        for c0, c1 in olds:
+            dma(A(MW, c0, c1), A(WS, c0, c1), "g", 4000, True)
+        LA, LN, LS, AN = u(192)[:2] + (nc,), u(64), u(64), f(64)
         mm(acc(A(B[0], 0, 32), ext(None, ZA, MW, 32, n0)) + acc(A(B[0], 32, 64), ext(None, ZBB, MW, 32, n0)))
-        cp(A(LN), A(B[0], 0, 64))
-        ts(A(AN), A(B[0], 0, 64), 576.0, LT)
+        ts(A(LN), A(B[0], 0, 64), -65.0 * TOP, ADD, 640.0, MIN)
+        ts(A(AN), A(B[0], 0, 64), 576.0 + 65 * TOP, LT)
         mm(acc(A(B[1], 0, 32), ext(None, ZSA, MW, 32, n0)) + acc(A(B[1], 32, 64), ext(None, ZSB, MW, 32, n0)))
-        ts(A(LS), A(B[1], 0, 64), 1.0, ADD, 591.0, MIN)
+        ts(A(LS), A(B[1], 0, 64), 1.0 - 65 * TOP, ADD, 591.0, MIN)
         mm([(A(B[2]), A3(BL, 0), A(MW, n0, n), True, True)])
         MK, SM, G, CM, PO, PE_, LP = b(512), b(1024), b(1024), b(1024), f(64), f(64), u(64)
         act(A(CM, 0, 512), A(B[2]), AF.Abs, A(NPM))
@@ -652,25 +667,18 @@ def program():
             mm(acc(A(B[k], 0, v1 - v0), [(Z(ZUP, l), A(UW, 640 * l + v0, 640 * l + v1)) for l in range(12)]))
             tt(A(P, 16 + v0, 16 + v1), A(B[k], 0, v1 - v0), A(P, 16 + v0, 16 + v1), ADD)
         AC2, WN = f(192)[:2] + (nc,), f(192)[:2] + (nc,)
-        mm(acc(A(B[3], 0, nc), ext(None, ZA, MW, nc)))
-        cp(A(LA), A(B[3], 0, nc))
-        lin(A(AC2), A(B[3], 0, nc), 1.0, float(592 * t + 16), "v")
-        mm(acc(A(B[4], 0, nc), ext(None, ZBB, MW, nc)))
-        cp(A(LB), A(B[4], 0, nc))
-        for k in range(n // 512):
+        for x, (c0, c1) in enumerate([(n0, n)] + olds):
+            s, w = (c0 // 16, c1 // 16), (c1 - c0) // 16
+            mm(acc(A(B[3 + x % 2], 0, w), ext(None, ZZ, MW, w, c0)))
+            ts(A(LA, *s), A(B[3 + x % 2], 0, w), -65.0 * TOP, ADD, 3185.0 if x else 3170.0, MIN)
+        mm(acc(A(B[4], 0, nc), ext(None, ZAA, MW, nc)))
+        lin(A(AC2), A(B[4], 0, nc), 1.0, float(64 * t + 16 - 17 * TOP))
+        ts(A(XN, n0, n), IND(A(ZD), A(LA, n0 // 16, nc)), 255.0, MIN)
+        for k in range(n0 // 512):
             s = (512 * k, 512 * k + 512)
-            cp(A(GA, *s), IND(A(Y), A(LA, 32 * k, 32 * k + 32)), "vs")
-            cp(A(GB, *s), IND(A(Y), A(LB, 32 * k, 32 * k + 32)), "vs")
-            bk, dk = A(B[3 + k % 2]), A(C if k % 2 else B[5], 0, 512)
-            if k < n0 // 512:
-                mm(acc(dk, [(A(ID), A(XL, *s)), (A(NID), A(GA, *s)), (A(NID), A(GB, *s))]))
-                act(A(LTT, *s), dk, AF.Sign, -0.5)
-            if k in OPT[1 + t]:
-                act(bk, dk, AF.Relu)
-                tt(A(XL, *s), A(XL, *s), bk, SUB)
-            else:
-                mm(acc(bk, [(A(ID), A(GA, *s)), (A(ID), A(GB, *s))]))
-                tt(A(XL, *s), bk, A(XL, *s), MIN)
+            tt(A(XN, *s), IND(A(ZD), A(LA, 32 * k, 32 * k + 32)), A(XO, *s), MIN)
+            mm(acc(A(B[5 + k % 2]), [(A(ID), A(XO, *s)), (A(NID), A(XN, *s))]))
+            act(A(LTT, *s), A(B[5 + k % 2]), AF.Sign, -0.5)
         mm(acc(A(B[3], 0, n0 // 16), ext(None, ZB, LTT, n0 // 16)))
         ts(A(WN, 0, n0 // 16), A(B[3], 0, n0 // 16), 2.0, GE, 4096.0, MUL)
         ts(A(WN, n0 // 16, nc), A(AN, 0, 32), 4096.0, MUL)
@@ -690,6 +698,7 @@ def program():
         tt(A(NMF), A(PS, 0, 120), A(HS), SUB)
         ts(A(LN_), A(NMF), -1.0, ADD)
         tt(A(O1), A(HS), A(AV), LE)
+        XN, n, JX = (XM, XL)[t], 2560 + 512 * t, JXS[t]
         tt(A(O1), A(O1), A(JX), MUL)
         tt(A(O1), A(O1), A(NMF), MAX)
         for e in range(2):
@@ -705,9 +714,9 @@ def program():
             send(A(TR[1 - e]), A(TB[e]), 2 * e - 1, 4000)
         own_ = (A(GA, 0, 960), A(GA, 960, 1920))
         for e in range(2):
-            cp(own_[e], IND(A(XL), A(LN_, 60 * e, 60 * e + 60)), "vs")
-            mm(acc(A(B[3], 0, 480), [(A(ID), A(GA, 960 * e, 960 * e + 480)), (A(I256), A(GA, 960 * e + 480, 960 * e + 960))]))
-            cp(A(XS[e]), A(B[3], 0, 480))
+            cp(own_[e], IND(A(XN, 0, n), A(LN_, 60 * e, 60 * e + 60)), "vs")
+            mm(acc(A(B[6 + e], 0, 480), [(A(ID), A(GA, 960 * e, 960 * e + 480)), (A(I256), A(GA, 960 * e + 480, 960 * e + 960))]))
+            cp(A(XS[e]), A(B[6 + e], 0, 480))
             send(A(XR[1 - e]), A(XS[e]), 2 * e - 1, 5500)
         for e in range(2):
             Q = b(80)
@@ -715,11 +724,7 @@ def program():
             for k in range(2):
                 s = (960 * e + 480 * k, 960 * e + 480 * k + 480)
                 mm(sum([acc(A(B[4 + k], 80 * l, 80 * l + 80), [(A3(BL, 6 * k + l), A(TB[e])), (A(NID), A(Q))]) for l in range(6)], []))
-                if t == 0 and (e, k) in OPT[0]:
-                    act(A(DD, *s), A(B[4 + k], 0, 480), AF.Abs)
-                    act(A(LTT, *s), A(DD, *s), AF.Relu, 1.0, -1.0)
-                else:
-                    ts(A(LTT, *s), A(B[4 + k], 0, 480), 0.0, EQ)
+                ts(A(LTT, *s), A(B[4 + k], 0, 480), 0.0, EQ)
             mm(acc(A(B[4], 0, 60), ext(None, ZM, LTT, 60, 960 * e)))
             s = (60 * e, 60 * e + 60)
             tt(A(RI, *s), A(JA, *s), A(B[4], 0, 60), SUB)
@@ -746,10 +751,10 @@ def program():
         def store():
             for e in range(2):
                 for c0, c1 in ((0, 10), (10, 20), (20, 30), (30, 40), (40, 50), (50, 60)) if t == 0 else ((0, 30), (30, 60)):
-                    cp(IND(A(XL), A(LS_, 60 * e + c0, 60 * e + c1)), A(GB, 960 * e + 16 * c0, 960 * e + 16 * c1))
+                    cp(IND(A(XN), A(LS_, 60 * e + c0, 60 * e + c1)), A(GB, 960 * e + 16 * c0, 960 * e + 16 * c1))
         return store
 
-    LSE, s1, s2, s3, s4, si, JA, AV, JX, QC, I256 = u(8), f(8), f(8), f(8), f(8), ii(8), f(120), f(120), f(120), f(1), b(128)
+    LSE, s1, s2, s3, s4, si, JA, AV, JXS, QC, I256 = u(8), f(8), f(8), f(8), f(8), ii(8), f(120), f(120), [f(120), f(120)], f(1), b(128)
     ts(A(s1), A(J, 0, 8), 60.0, GE)
     ts(A(s2), A(s1), -60.0, MUL)
     tt(A(s2), A(s2), A(J, 0, 8), ADD)
@@ -772,8 +777,9 @@ def program():
     lin(A(JA), A(JB), 1.0, PM)
     for e in range(2):
         lin(A(AV, 60 * e, 60 * e + 60), A(JA, 0, 60), 8192.0, 8192.0 * (560 * e - 959))
-        lin(A(JX, 60 * e, 60 * e + 60), A(J, 0, 60), 1.0, 3073.0)
-        ms(A(XW[e], 960, 1040), 255)
+        for t in range(2):
+            lin(A(JXS[t], 60 * e, 60 * e + 60), A(J, 0, 60), 1.0, 2561.0 + 512 * t)
+        fl(A(XW[e], 960, 1040), 255)
     ts(A(QC), PM, -80.0, MUL, 960.0, ADD)
     ts(A(QC), A(QC), 0.0, MAX)
     W["m1"] = A(QC)
@@ -819,17 +825,17 @@ def schedule():
     for k, o in enumerate(OPS):
         dep = {}
         for kind, regs in (("r", o["rd"]), ("w", o["wr"])):
-            for nm, lo, hi, st in regs:
+            for nm, lo, hi, st, pm in regs:
                 ps = nm in SHAPES and SHAPES[nm][0] == "psum"
-                for j, kd, l2, h2, s2 in hist.get(nm, []):
-                    meet = l2 <= hi and lo <= h2 and (kd == "w" or kind == "w") and not (st == s2 and (lo - l2) % st)
+                for j, kd, l2, h2, s2, p2 in hist.get(nm, []):
+                    meet = l2 <= hi and lo <= h2 and pm & p2 != 0 and (kd == "w" or kind == "w") and not (st == s2 and (lo - l2) % st)
                     if ps or meet:
                         dep[j] = dep.get(j, False) or (meet and not (ps and o["alts"][0][0] == "t"))
         dep.pop(k, None)
         for kind, regs in (("r", o["rd"]), ("w", o["wr"])):
-            for nm, lo, hi, st in regs:
+            for nm, lo, hi, st, pm in regs:
                 if hi < 1 << 30:
-                    hist.setdefault(nm, []).append((k, kind, lo, hi, st))
+                    hist.setdefault(nm, []).append((k, kind, lo, hi, st, pm))
         o["dep"] = dep
     succ, after, near, above = [[] for _ in range(n)], [[] for _ in range(n)], [], []
     pred = [set(o["dep"]) | ({o["after"]} if "after" in o else set()) for o in OPS]

@@ -163,8 +163,8 @@ def ms(out, c):
     op([("v", lambda g, T: g.vector.memset(real(T, out), c), max(40, out[4] * (0.5 if two(out) else 1)))], [out], [])
 
 
-def scan(out, d0, d1, o0, o1):
-    op([("v", lambda g, T: g.vector.tensor_tensor_scan(real(T, out), real(T, d0), real(T, d1), 0.0, o0, o1), vcost(out, [d1]))], [out], [d0, d1])
+def scan(out, d0, d1, o0, o1, first=0.0):
+    op([("v", lambda g, T: g.vector.tensor_tensor_scan(real(T, out), real(T, d0), real(T, d1), first, o0, o1), vcost(out, [d1]))], [out], [d0, d1])
 
 
 def tr(out, in_):
@@ -220,6 +220,14 @@ def dma(out, in_, q="y", lat=2600, add=False):
     OPS[-1]["wr"] = [(r[0], r[1] // 8 * 8, r[2] // 8 * 8 + 7) + r[3:] for r in OPS[-1]["wr"]]
 
 
+def dmas(pairs, lat):
+    s = "d%d" % len(SEMS)
+    SEMS.append(s)
+    op([("y", [(lambda g, T, o=o, i=i: g.sync.dma_start(real(T, o), real(T, i))) for o, i in pairs], 100 * len(pairs))],
+       [o for o, i in pairs], [i for o, i in pairs], sem=s, inc=16 * len(pairs), lat=lat)
+    OPS[-1]["wr"] = [(r[0], r[1] // 8 * 8, r[2] // 8 * 8 + 7) + r[3:] for r in OPS[-1]["wr"]]
+
+
 def send(dst, src, step, lat):
     k = len(SEMS)
     SEMS.extend(["l%d" % k, "r%d" % k])
@@ -228,27 +236,31 @@ def send(dst, src, step, lat):
 
 
 PEC = 0.6
-CV = 100
+CV = [100, 50]
+MAPS = [(0, 20, "v"), (20, 40, "v"), (40, 60, "v"), (60, 90, "s"), (90, 120, "s")]
+C0 = min(CV + [m[0] for m in MAPS if m[2] == "s"])
+MKV = [0]
+OUTS = [(0, 1024), (1024, 2048), (2048, 2560), (2560, 3072)]
 LOW = 65
 TOP = LOW + 16
+EQS = [(1, 0, 0), (1, 0, 1), (1, 1, 0), (1, 1, 1)]
 CLAMP = [(0, 21), (21, 45), (45, 66)]
 
 
 def program():
     f, b, h, ii, u = (lambda n: al("f", n)), (lambda n: al("b", n)), (lambda n: al("h", n)), (lambda n: al("i", n)), (lambda n: al("u", n))
     B = [own("B%d" % k, "psum", [128, 512], "float32") for k in range(8)]
-    WS = f(5760 + 16 * (198 - CV))
-    YM, DD, CC = WS[:2] + (3072,), (WS[0], WS[1] + WS[2] - 3168, 3168), h(3168)
-    SEL = own("SEL", "sbuf", [128, 16, 144], "bfloat16")
+    WS = f(5760 + 16 * (198 - min(CV)))
+    YM, DD, CC = (WS[0], WS[1] + 4096, 3072), (WS[0], WS[1] + WS[2] - 3168, 3168), h(3168)
     BL = own("BL", "sbuf", [128, 12, 128], "bfloat16")
     L1, R2 = u(480), f(128)
     XL = own("XL", "sbuf", [128, 4032], "bfloat16")
-    SD = b(16 * CV + 3520)
-    XM, SF = (SD[0], SD[1] + 16 * CV, 3520), f(16 * (198 - CV))
+    SD = b(16 * max(CV) + 3520)
+    XM, SF = (SD[0], SD[1] + 16 * max(CV), 3520), f(16 * (198 - C0))
     XW = [ii(1040), ii(1040)]
     EN, NB = XW[0][:2] + (480,), (XW[0][0], XW[0][1] + 480, 480)
     UW = own("UW", "sbuf", [128, 8704], "bfloat16")
-    MW = own("MW", "sbuf", [128, 8928], "bfloat16")
+    MW = own("MW", "sbuf", [128, max(7168, 5760 + 16 * max(CV))], "bfloat16")
     col = lambda t, k: A(t, k, k + 1)
     Z = lambda z, t: A(z, 15 - t, 143 - t)
 
@@ -282,9 +294,9 @@ def program():
     early = [("key", [1024] * 12 + [128, 32, 1, -229376]), ("fs", [1] * 13 + [U13, 1, 1]), ("fc", [1] * 12 + [4096] * 4),
              ("pd", [0] * 12 + [1920, 22 * 8192 + 3072, 0, 1]), ("fd", [0] * 12 + [1920, 22.375, 0, 1]),
              ("dg", [1] * 12 + [1 / 128, 0, 0, -13])]
-    late = [("vb", {13: 262144, 14: 8192, 15: -90112}), ("got", {13: 32, 14: 1, 15: -12}), ("wa", {0: 1, 1: 16, 2: 48}),
+    late = [("vb", {13: 262144, 14: 8192, 15: -88064}), ("got", {13: 32, 14: 1, 15: -12}), ("wa", {0: 1, 1: 16, 2: 48}),
             ("wb", {0: 1, 1: 16, 3: 48}), ("sa", {1: 16, 2: 48, 3: 1}), ("sb", {1: 16, 2: 1, 3: 48}),
-            ("upd", {12: 1, 13: 262144, 14: 8192, 15: 32}), ("zz", {0: 1, 1: 16, 4: 48}), ("aa", {0: 1, 1: 16})]
+            ("upd", {12: 1, 13: 262144, 14: 8192, 15: 32}), ("zz", {0: 1, 1: 16, 4: 48}), ("aa", {0: 1, 1: 16}), ("ab", {0: 1, 1: 16, 5: 0.5}), ("zd", {0: 1, 1: 16, 6: 48})]
     W16, WC, W = f(32), f(48), {}
     for k, (n, w) in enumerate(early):
         for r in range(16, 0, -1):
@@ -293,15 +305,15 @@ def program():
         W[n] = col(WC, k)
     mm([(A(B[2], 0, 6), A(OH, p=(0, 16)), A(W16, 0, 6, p=(0, 16)), True, True)])
     cp(A(WC, 0, 6), A(B[2], 0, 6))
-    ms(A(W16, 8, 17, p=(0, 16)), 0.0)
+    ms(A(W16, 8, 19, p=(0, 16)), 0.0)
     for e in range(4):
         for k, (n, w) in enumerate(late):
             if e < len(w):
                 r = sorted(w)[e]
                 asel(A(W16, 8 + k, 9 + k, p=(0, 16)), NE, float(w[r]), -r, 1)
             W[n] = col(WC, 8 + k)
-    mm([(A(B[5], 0, 9), A(OH, p=(0, 16)), A(W16, 8, 17, p=(0, 16)), True, True)])
-    cp(A(WC, 8, 17), A(B[5], 0, 9))
+    mm([(A(B[5], 0, 11), A(OH, p=(0, 16)), A(W16, 8, 19, p=(0, 16)), True, True)])
+    cp(A(WC, 8, 19), A(B[5], 0, 11))
     for k, (n, o, v, w) in enumerate([("s01", LT, 2, 1), ("o14", LT, 14, 1), ("w640", LT, 12, -320), ("l12", LT, 12, 1), ("cm", GE, 12, 1),
                                       ("cx", EQ, 12, 1920), ("ps", GE, 13, 1), ("n15", LT, 15, 1), ("m12", LT, 12, -1), ("p0", GE, 1, 1)]):
         W[n] = col(WC, 20 + k)
@@ -324,12 +336,9 @@ def program():
     ZKEY = zt("key")
     BKEY, BDG, BS01, BVB, BGOT, PAS = bt("key"), bt("dg"), bt("s01"), bt("vb"), None, bt("ps", ID)
     Z14, ZL12, ZA, ZBB, ZSA, ZSB, Z640, ZU, ZUP = zt("z14", "h"), zt("l12"), zt("wa"), zt("wb"), zt("sa"), zt("sb"), zt("w640"), zt("wu"), zt("upd")
-    ZZ, ZAA, ZN14 = zt("zz"), zt("aa"), zt("n14", "f")
+    ZZ, ZQ, ZAA, ZN14 = zt("zz"), zt("zd"), [zt("aa"), zt("ab")], zt("n14", "f")
     ZT, ONE = b(1024), b(512)
     ms(A(ZT), 0.0)
-    for i in range(0, 16, 4):
-        dma(A3(SEL, slice(i, i + 4)), A(ZT, 0, 576), "ys"[i // 4 % 2])
-    asel(A3(SEL, ALL, slice(15, 144, 16)), NE, 1.0, 0, 1, [[-1, 16], [-16, 9]])
     for i in range(0, 12, 4):
         dma(A3(BL, slice(i, i + 4)), A(ZT, 0, 512))
         asel(A3(BL, slice(i, i + 4)), NE, 1.0, -i, 1, [[-1, 4], [-16, 8], [0, 16]])
@@ -338,8 +347,9 @@ def program():
     ts(col(pc, 1), W["cx"], col(pc, 0), ADD)
     ts(col(pc, 0), W["ps"], 1920.0, MUL, col(pc, 1), ADD)
     ts(A(PERM), A(XZ, 15, 111), col(pc, 0), EQ)
-    NPM = f(1)
-    ts(A(NPM), PM, -1.0, MUL, -float(TOP), ADD)
+    NPM = f(2)
+    ts(col(NPM, 0), PM, -1.0, MUL, -float(TOP), ADD)
+    ts(col(NPM, 1), PM, float(TOP), ADD)
     TS, SFX, NBD, UBM, t2 = b(128), b(128), b(128), b(128), f(128)
     asel(A(TS), GT, 0.0, 0, -1, [[1, 128]], A(BD))
     asel(A(SFX), GT, 0.0, 0, 1, [[-1, 128]], bt("m12"))
@@ -382,13 +392,11 @@ def program():
     ms(A(WW, 192, 256), 0.0)
 
     def clear():
-        for k in range(8):
-            dma(A(UW, 960 * k, 960 * (k + 1)), A(ZT, 0, 960), "y", 5000)
+        dmas([(A(UW, 960 * k, 960 * (k + 1)), A(ZT, 0, 960)) for k in range(8)], 5000)
 
     def fill(t):
-        for k in range(5 + t):
-            dma(A(MW, 512 * k, 512 * (k + 1)), A(MB), "y", 4000)
-            dma(A(WS, 512 * k, 512 * (k + 1)), A(MF), "y", 4000)
+        dmas([(A(MW, 512 * k, 512 * (k + 1)), A(MB)) for k in range(5 + t)], 4000)
+        dmas([(A(WS, 512 * k, 512 * (k + 1)), A(MF)) for k in range(5 + t)], 5000)
     fill(0)
     CI, CE, CF, LVS = ii(40), ii(40), f(40), u(40)
     iota(A(CI), [[1, 40]], 0)
@@ -409,17 +417,28 @@ def program():
     tt(A(KF), A(KF), A(KI), ADD)
     cp(A(LSV), A(KF))
     TIN, TT, NX, VI, VH = f(672), f(1312), f(480), ii(40), ii(40)
-    ms(A(TIN, 0, 16), 0.0)
-    ms(A(TIN, 656, 672), 0.0)
-    ms(A(TIN, 28, 28 + 80, 16), 1920.0)
-    ms(A(TIN, 28 + 80, 28 + 560, 16), 1792.0)
-    ms(A(TIN, 28 + 560, 656, 16), 1920.0)
-    ms(A(TIN, 31, 656, 16), 1.0)
+    XI_, XT = b(672), b(1312)
     cp(A(VI), A(J, 0, 40))
     ts(A(VH), A(VI), 5, SHR)
-    ts(A(TIN, 29, 656, 16), A(VH), 8192.0, MUL, 3072.0, ADD)
     ts(A(VI), A(VI), 31, AND)
-    cp(A(TIN, 30, 656, 16), A(VI))
+    for t, put in ((XI_, lambda o, c: ms(o, float(c))), (TIN, fl)):
+        put(A(t, 0, 16), 0)
+        put(A(t, 656, 672), 0)
+        put(A(t, 28, 28 + 80, 16), 1920)
+        put(A(t, 28 + 80, 28 + 560, 16), 1792)
+        put(A(t, 28 + 560, 656, 16), 1920)
+        put(A(t, 31, 656, 16), 1)
+        cp(A(t, 30, 656, 16), A(VI))
+    ts(A(XI_, 29, 656, 16), A(VH), 0.375, ADD)
+    ts(A(TIN, 29, 656, 16), A(VH), 8192.0, MUL, 3072.0, ADD)
+    for k in range(12):
+        ts(A(XI_, 16 + k, 656, 16), A(NB, 40 * k, 40 * k + 40), 0.0, GE)
+
+    def turn(out):
+        tr(A(XT, 0, 640), A(XI_, 16, 656))
+        tr(A(XT, 640, 1312), A(XI_))
+        cp(out, IND(A(XT), A(LVS)), "vs")
+    turn(A(F, 16, 656))
     ts(A(L1), A(NB), 16.0, ADD)
     lin(A(NX), A(NB), 8192.0, 8193.0, "v")
     for k in range(12):
@@ -438,8 +457,14 @@ def program():
     fl(A(DG, 198, 208), LOW)
     iota(A(DC, 0, 198), [[0, 66], [1, 3]], 16)
     iota(A(DQ, 0, 198), [[1, 66], [0, 3]], 16)
-    for r, t in ((1, DC), (2, DJ), (4, DQ)):
-        dma(row(DG, r, 0, 198), row(t, r, 0, 198))
+    D1, D2, D3 = b(198), b(198), b(198)
+    mm(acc(A(B[5], 0, 198), [(A(ID), A(DG, 0, 198)), (A(NID), A(DJ, 0, 198))]))
+    lin(A(D1), A(B[5], 0, 198), -0.5, 12.0)
+    lin(A(D2), A(B[5], 0, 198), 1.0, -1.0)
+    tt(A(D1), A(D1), A(D2), MUL)
+    mm(acc(A(B[5], 0, 198), [(A(ID), A(D1)), (A(ID), A(DJ, 0, 198))]))
+    cp(A(D3), A(B[5], 0, 198), "vs")
+    dmas([(row(DG, r, 0, 198), row(t, r, 0, 198)) for r, t in ((1, DC), (2, DJ), (4, DQ), (5, MB), (6, D3))], 2600)
     LUP, LDN, LSQ = u(14), u(14), u(36)
     mm(acc(A(B[5], 0, 13), ext(None, ZSA, DG, 13)) + acc(A(B[5], 16, 29), ext(None, ZSB, DG, 13)))
     ts(A(LUP, 0, 13), A(B[5], 0, 13), 1.0 - 16 * 65, ADD, 591.0, MIN)
@@ -467,9 +492,10 @@ def program():
     tt(A(q1), A(q1), A(q3), ADD)
     cp(A(LSQ), A(q1))
     ts(A(OI), A(X16, 0, 16), 16.0, ADD, col(OH, 0), MUL)
-    for i in range(16):
+    for i in range(15):
         lin(A(SD, i, 3168, 16), A(DG, 0, 198), W["p0"], col(OI, i))
-    dma(A(SF), A(SD, 16 * CV, 3168), "g", 4000)
+    op([("s", act_alt(A(SD, 15, 3168, 16), A(DG, 0, 198), AF.Silu, col(OI, 15), W["p0"], None)[1], 1800)], [A(SD, 15, 3168, 16)], [A(DG), W["p0"], A(OI)])
+    dma(A(SF), A(SD, 16 * C0, 3168), "g", 4000)
     RS1 = b(576)
     fl(A(RS1), 1)
     fl(A(RS1, 0, 576, 16), 0)
@@ -480,25 +506,29 @@ def program():
         iota(A(N2), [[1, 16], [0, 32]], 63 + 16 * t)
         for r, s in ((13, ZT), (14, N1), (15, N2)):
             dma(row(NM[t], r), row(s, r, 0, 512))
-    JG, JU, JM, JP, JQ = f(3), f(36), f(198), f(64), f(64)
-    for t, n, m, c in ((JG, 3, 1.0, 656.0), (JU, 36, 8192.0, 641.0 * 8192), (JP, 64, 1.0, 7681.0), (JQ, 64, 1.0, 3852.0)):
+    JG, JU, JM, JQ = f(3), f(36), [f(198), f(198)], f(32)
+    for t, n, m, c in ((JG, 3, 1.0, 656.0), (JU, 36, 8192.0, 641.0 * 8192), (JQ, 32, 1.0, 3852.0)):
         lin(A(t), A(J, 0, n), m, c)
-    lin(A(JM, 0, CV), A(J, 0, CV), 1.0, 5760.0 - 552)
-    lin(A(JM, CV, 198), A(J, 0, 198 - CV), 1.0, 5760.0 - 552)
-    MID, GOT = f(192), f(128)
-    fl(A(MID), 0)
+    for t in range(2):
+        lin(A(JM[t], 0, CV[t]), A(J, 0, CV[t]), 1.0, 5760.0 - 552)
+        lin(A(JM[t], CV[t], 198), A(J, 0, 198 - CV[t]), 1.0, 5760.0 - 552)
+    MID, GOT, NW = f(192), f(144), b(208)
+    fl(A(MID, 160, 192), 0)
+    fl(A(NW, 198, 208), 0)
     fl(A(GOT), -1)
 
-    RH, PV = UW, NX
-    ZD, GB, LTT = b(3200), b(1920), (MW, 5760, 3072)
-    ms(A(ZD, 3168, 3184), 0.0)
-    ms(A(ZD, 3184, 3200), 255.0)
+    RH = UW
+    ZD, GB, LTT = b(3200), b(1936), (MW, 4096, 3072)
+    fl(A(ZD, 3168, 3184), 0)
+    fl(A(ZD, 3184, 3200), 255)
+    fl(A(GB, 1920, 1936), 255)
     GA = ZD
 
     def choose(t):
         SCOPE[:] = ["a", 0]
-        ts(A(F, 16, 656), A(P, 16, 656) if t else IND(A(TT), A(LVS)), W["fs"], MUL, W["fc"], MIN)
-        KV, E, DS, AC, M1, HL = f(40), f(480), f(480), f(120), f(40), b(80)
+        if t:
+            ts(A(F, 16, 656), A(P, 16, 656), W["fs"], MUL, W["fc"], MIN)
+        KV, E, DS, AC, M1 = f(40), f(480), f(480), f(120), f(40)
         mm(acc(A(B[2], 0, 40), ext(None, ZKEY, F, 40, 16)))
         cp(A(KV), A(B[2], 0, 40), "vs")
         mm([(A(B[2], 0, 480), BDG, A(F, 96, 576), True, True)])
@@ -517,21 +547,19 @@ def program():
             else:
                 tt(A(AC, 0, 80), A(B[c % 2], 0, 80), A(AC, 0, 80), MIN)
         tt(A(M1), A(AC, 0, 40), A(AC, 40, 80), MIN)
-        cp(A(HL, 0, 40), A(M1))
-        tt(A(HL, 40, 80), A(M1), A(HL, 0, 40), SUB)
-        for k, (c0, c1) in enumerate(((0, 20), (20, 40))):
-            parts = []
-            for i in range(16):
-                parts += acc(A(B[k], i, 320, 16), [(A3(SEL, i, slice(15, 143)), A(HL, c0, c1)), (A3(SEL, i, slice(14, 142)), A(HL, 40 + c0, 40 + c1))])
-            mm(parts)
-            cp(A(W2, 16 + 16 * c0, 16 + 16 * c1), A(B[k], 0, 320), "vs")
+        tt(A(XI_, 16, 656, 16), A(AC, 0, 40), A(AC, 40, 80), MIN)
+        tt(A(XI_, 17, 656, 16), A(M1), A(XI_, 16, 656, 16), SUB)
+        turn(A(W2, 16, 656))
         for k in range(12):
             cp(A(RH, 496 * k, 496 * k + 496), IND(A(W2), A(L1, 40 * k + 4, 40 * k + 35)), "vs")
             mm([(A(B[0], 0, 480), BS01, A(W2, 96, 576), True, False)] * (k == 0) + [(A(B[0], 0, 480), BS01, A(RH, 496 * k + 16, 496 * k + 496), False, k == 11)])
-        CH, PR, JK_, GN, G2, LG = b(480), f(480), None, f(3), f(3), u(4)
+        CH, PR, GS, G2, LG = b(480), b(480), f(482), f(3), u(4)
+        GN = (GS[0], GS[1] + 479, 3)
         tt(A(CH), A(B[0], 0, 480), A(E), EQ)
         scan(A(PR), A(ONE, 0, 480), A(CH), MUL, ADD)
-        for c in range(3):
+        ts(A(CH), A(PR), col(JH, 0), LT, 2.0, MUL)
+        scan(A(GS, 0, 480), A(ONE, 0, 480), A(CH), MUL, ADD, -480.0)
+        for c in range(1, 3):
             act(A(RH, 6000 + 480 * c, 6480 + 480 * c), A(PR), AF.Sign, col(JH, c), -1.0, col(GN, c))
         ts(A(G2), A(GN), 480.0, EQ)
         tt(A(G2), A(G2), A(JG), MUL)
@@ -581,23 +609,18 @@ def program():
                 continue
             ts(A(CC, 48 * q0, 48 * q1), A(DD, 48 * q0, 48 * q1), -2048.0, MAX, 2048.0, MIN)
             mm(acc(A(B[0], 3 * q0, 3 * q1), ext(None, Z14, CC, 3 * (q1 - q0), 48 * q0)))
-        for x, q0 in enumerate(range(0, 66, 10)):
-            q1, bk, parts = min(q0 + 10, 66), B[4 + x % 2], []
-            for j, a0, a1 in runs(q0, q1):
-                k0 = j + 1 - lex[j]
-                parts += [(A(bk, 48 * (a0 - q0), 48 * (a1 - q0)), A(ID), A(Y, 48 * (k0 + a0), 48 * (k0 + a1)), True, False)]
-                parts += [(A(bk, 48 * (q - q0), 48 * (q - q0 + 1)), A(ID), A(Y, 48 * j, 48 * j + 48), False, q == a1 - 1) for q in range(a0, a1)]
-            mm(parts)
-            cp(A(ZD, 48 * q0, 48 * q1), A(bk, 0, 48 * (q1 - q0)), "vs")
-        act(A(NK), A(NR), AF.Identity, MAGIC)
-        act(A(NH), A(NK), AF.Identity, -MAGIC)
+        dmas([(A(ZD, 48 * lex[d], 48 * lex[d + 1]), A(Y, 48 * d + 48, 576)) for d in range(11)]
+             + [(A(XN, 48 * lex[d], 48 * lex[d + 1]), A(Y, 0, 528 - 48 * d)) for d in range(11)], 7000)
+        for c in (0, 1584):
+            dma(A(ZD, c, c + 1584), A(XN, c, c + 1584), "g", 4500, True)
         for k in range(2):
             mm([(A(B[1 + k], 48 * j, 48 * j + 48), BVB, A(FG), True, True) for j in range(6)])
             if k == 0:
-                lin(A(GOT, 64 * t + 16, 64 * t + 64), A(B[1], 0, 48), U13, -1.0)
+                lin(A(GOT, 65 * t + 16, 65 * t + 64), A(B[1], 0, 48), U13, -1.25)
             s = (288 * k, 288 * k + 288)
-            tt(A(NK, *s), A(B[1 + k], 0, 288), A(NH, *s), SUB)
-            act(A(B[1 + k], 0, 288), A(NK, *s), AF.Abs, 0.0, 1024.0)
+            tt(A(NK, *s), A(B[1 + k], 0, 288), A(NR, *s), SUB)
+            act(A(NH, *s), A(NK, *s), AF.Abs)
+            act(A(B[1 + k], 0, 288), A(NH, *s), AF.Relu, -3000.0 * 4096, 4096.0)
             tt(A(NK, *s), A(B[1 + k], 0, 288), A(NR, *s), MIN)
         act(A(FRE), A(NK), AF.Relu, 1.0, -1.0)
         mm(acc(A(B[1], 0, 36), ext(None, ZL12, FRE, 36)))
@@ -614,65 +637,70 @@ def program():
         ts(A(RH_), A(B[0], 0, 198), MAGIC / 2, ADD, MAGIC / 2, SUB)
         tt(A(RL), A(B[0], 0, 198), A(RH_), SUB)
         ts(A(WW, 0, 198), A(RL), -553.0, EQ)
-        NW, JC, EE = (B[6], 0, 198), (B[7], 0, 198), (B[2], 0, 198)
-        act(A(NW), A(RL), AF.Abs, 553.0)
+        JC, EE = (B[7], 0, 198), (B[2], 0, 198)
+        act(A(NW, 0, 198), A(RL), AF.Abs, 553.0)
         lin(A(JC), A(RL), -32768.0, -552.5 * 32768)
         cp(A(SQ), IND(A(WW), A(LSQ)))
         scan(A(ST, 0, 576), A(RS1), A(SQ), MUL, ADD)
-        cp(A(SU), IND(A(ST), A(LUP, 0, 13)))
+        tt(A(SU), IND(A(ST), A(LUP, 0, 13)), A(NW), MAX)
         tt(A(SV), IND(A(ST), A(LDN, 0, 13)), A(SU), MAX)
-        tt(A(SV, 0, 198), A(SV, 0, 198), A(NW), MAX)
         ts(A(SU, 0, 198), A(SV, 0, 198), 0.0, LE)
         for c in range(3):
             scan(A(IN, c, 198, 3), A(ONE, 0, 66), A(SU, c, 198, 3), MUL, ADD)
         act(A(EE), A(SV, 0, 198), AF.Relu, 0.0, 16384.0)
         mm([(A(B[1], 0, 3), A(TS), A(IN, 195, 198), True, False), (A(B[1], 1, 3), A(BD), A(IN, 195, 197), False, False), (A(B[1], 2, 3), A(BD), A(IN, 195, 196), False, True)])
-        tt(A(JC), A(JC), A(JM), MIN)
+        tt(A(JC), A(JC), A(JM[t]), MIN)
         tt(A(JC), A(JC), A(RL), MAX)
         tt(A(OF), A(IN), A(EE), ADD)
         for c in range(3):
             ts(A(OF, c, 198, 3), A(OF, c, 198, 3), col(B[1], c), ADD, float(n0 - 553), ADD)
         tt(A(OF), A(JC), A(OF), MIN)
         ts(A(LM, 0, 198), A(OF), 552.0, ADD)
-        cp(IND(A(MW), A(LM, 0, CV)), A(SD, 0, 16 * CV))
-        silu(IND(A(WS), A(LM, CV, 198)), A(SF), 1570 * (t == 0))
+        cp(IND(A(MW), A(LM, 0, CV[t])), A(SD, 0, 16 * CV[t]))
+        silu(IND(A(WS), A(LM, CV[t], 198)), A(SF, 16 * (CV[t] - C0)))
         tt(A(MW, n0, n), A(MW, n0, n), A(WS, n0, n), ADD)
         olds = [(c, min(c + 1024, n0)) for c in range(0, n0, 1024)]
         for c0, c1 in olds:
             dma(A(MW, c0, c1), A(WS, c0, c1), "g", 4000, True)
-        LA, LN, LS, AN = u(192)[:2] + (nc,), u(64), u(64), f(64)
-        mm(acc(A(B[0], 0, 32), ext(None, ZA, MW, 32, n0)) + acc(A(B[0], 32, 64), ext(None, ZBB, MW, 32, n0)))
-        ts(A(LN), A(B[0], 0, 64), -65.0 * TOP, ADD, 640.0, MIN)
-        ts(A(AN), A(B[0], 0, 64), 576.0 + 65 * TOP, LT)
-        mm(acc(A(B[1], 0, 32), ext(None, ZSA, MW, 32, n0)) + acc(A(B[1], 32, 64), ext(None, ZSB, MW, 32, n0)))
-        ts(A(LS), A(B[1], 0, 64), 1.0 - 65 * TOP, ADD, 591.0, MIN)
-        mm([(A(B[2]), A3(BL, 0), A(MW, n0, n), True, True)])
+        LA, LN, LS, AN = u(192)[:2] + (nc,), u(64), u(64), f(32)
         MK, SM, G, CM, PO, PE_, LP = b(512), b(1024), b(1024), b(1024), f(64), f(64), u(64)
-        act(A(CM, 0, 512), A(B[2]), AF.Abs, A(NPM))
-        act(A(MK), A(CM, 0, 512), AF.Relu, 1.0, -1.0)
+        mm([(A(B[2]), A3(BL, 0), A(MW, n0, n), True, True)])
+        if t in MKV:
+            ts(A(MK), A(B[2]), A(NPM, 1, 2), EQ)
+        else:
+            act(A(CM, 0, 512), A(B[2]), AF.Abs, A(NPM, 0, 1))
+            act(A(MK), A(CM, 0, 512), AF.Relu, 1.0, -1.0)
         for e in range(2):
-            s = (512 * e, 512 * e + 512)
-            cp(A(G, *s), IND(A(PFU), A(LN, 32 * e, 32 * e + 32)), "s")
-            tt(A(SM, *s), IND(A(ST), A(LS, 32 * e, 32 * e + 32)), A(MK), MUL)
+            s, l = (512 * e, 512 * e + 512), (32 * e, 32 * e + 32)
+            mm(acc(A(B[1 + 3 * e], 0, 32), ext(None, (ZSA, ZSB)[e], MW, 32, n0)))
+            ts(A(LS, *l), A(B[1 + 3 * e], 0, 32), 1.0 - 65 * TOP, ADD, 591.0, MIN)
+            mm(acc(A(B[3 * e], 0, 32), ext(None, (ZA, ZBB)[e], MW, 32, n0)))
+            ts(A(LN, *l), A(B[3 * e], 0, 32), -65.0 * TOP, ADD, 640.0, MIN)
+            if e == 0:
+                lin(A(AN), A(B[0], 0, 32), 16384.0, -16384 * (575.5 + 65 * TOP))
+            tt(A(PE_, *l), A(AN), A(JQ), MIN)
+            cp(A(G, *s), IND(A(PFU), A(LN, *l)), "s")
+            tt(A(SM, *s), IND(A(ST), A(LS, *l)), A(MK), MUL)
+        for e in range(2):
+            s, l = (512 * e, 512 * e + 512), (32 * e, 32 * e + 32)
             mm(acc(A(B[e]), [(A(ID), A(G, *s)), (A(NBD), A(SM, *s))]))
             act(A(CM, *s), A(B[e]), AF.Sign, 0.5)
-        mm(acc(A(B[2], 0, 64), ext(None, ZU, G, 64) + ext(None, Z640, CM, 64)))
-        tt(A(PO), A(B[2], 0, 64), A(JQ), SUB)
-        tt(A(PO), A(PO), A(AN), MUL)
-        tt(A(PO), A(PO), A(JP), ADD)
-        ts(A(LP), A(PO), -1.0, ADD)
-        tt(IND(A(UW), A(LP, 0, 32)), A(G, 512, 1024), A(NM[t]), ADD)
-        tt(IND(A(UW), A(LP, 32, 64)), A(G, 0, 512), A(NM[t]), ADD)
-        for k, (v0, v1) in enumerate(((0, 96), (544, 640), (96, 544))):
-            mm(acc(A(B[k], 0, v1 - v0), [(Z(ZUP, l), A(UW, 640 * l + v0, 640 * l + v1)) for l in range(12)]))
-            tt(A(P, 16 + v0, 16 + v1), A(B[k], 0, v1 - v0), A(P, 16 + v0, 16 + v1), ADD)
-        AC2, WN = f(192)[:2] + (nc,), f(192)[:2] + (nc,)
+            mm(acc(A(B[2 + e], 0, 32), ext(None, ZU, G, 32, s[0]) + ext(None, Z640, CM, 32, s[0])))
+            tt(A(PO, *l), A(B[2 + e], 0, 32), A(PE_, *l), MAX)
+            ts(A(LP, *l), A(PO, *l), 3828.0, ADD)
+            tt(IND(A(UW), A(LP, *l)), A(G, 512 - s[0], 1024 - s[0]), A(NM[t]), ADD)
+        for k, (v0, v1) in enumerate(((0, 96), (544, 640), (96, 320), (320, 544))):
+            mm(acc(A(B[k % 3], 0, v1 - v0), [(Z(ZUP, l), A(UW, 640 * l + v0, 640 * l + v1)) for l in range(12)]))
+            tt(A(P, 16 + v0, 16 + v1), A(B[k % 3], 0, v1 - v0), A(P, 16 + v0, 16 + v1), ADD)
+        for v0, v1 in ((0, 96), (544, 640)) + ((96, 320), (320, 544)) * (t == 0):
+            tr(A(TT, v0, v1), A(P, 16 + v0, 16 + v1))
+        for v0, v1 in ((0, 96), (576, 672)) + ((96, 320), (320, 576)) * (t == 0):
+            tr(A(TT, 640 + v0, 640 + v1), A(P, v0, v1))
+        WN = f(192)[:2] + (nc,)
         for x, (c0, c1) in enumerate([(n0, n)] + olds):
             s, w = (c0 // 16, c1 // 16), (c1 - c0) // 16
-            mm(acc(A(B[3 + x % 2], 0, w), ext(None, ZZ, MW, w, c0)))
+            mm(acc(A(B[3 + x % 2], 0, w), ext(None, ZQ, MW, w, c0)))
             ts(A(LA, *s), A(B[3 + x % 2], 0, w), -65.0 * TOP, ADD, 3185.0 if x else 3170.0, MIN)
-        mm(acc(A(B[4], 0, nc), ext(None, ZAA, MW, nc)))
-        lin(A(AC2), A(B[4], 0, nc), 1.0, float(64 * t + 16 - 17 * TOP))
         ts(A(XN, n0, n), IND(A(ZD), A(LA, n0 // 16, nc)), 255.0, MIN)
         for k in range(n0 // 512):
             s = (512 * k, 512 * k + 512)
@@ -680,37 +708,31 @@ def program():
             mm(acc(A(B[5 + k % 2]), [(A(ID), A(XO, *s)), (A(NID), A(XN, *s))]))
             act(A(LTT, *s), A(B[5 + k % 2]), AF.Sign, -0.5)
         mm(acc(A(B[3], 0, n0 // 16), ext(None, ZB, LTT, n0 // 16)))
-        ts(A(WN, 0, n0 // 16), A(B[3], 0, n0 // 16), 2.0, GE, 4096.0, MUL)
-        ts(A(WN, n0 // 16, nc), A(AN, 0, 32), 4096.0, MUL)
-        tt(A(AC2), A(AC2), A(WN), MIN)
-        tt(A(MID, 0, nc), A(MID, 0, nc), A(AC2), MAX)
+        lin(A(WN, 0, n0 // 16), A(B[3], 0, n0 // 16), 4096.0, -4096.0)
+        lin(A(WN, n0 // 16, nc), A(AN), -1.0, 0.0)
+        mm(acc(A(B[4], 0, nc), ext(None, ZAA[t], MW, nc)))
+        tt(A(B[4], 0, nc) if t else A(MID, 0, nc), A(B[4], 0, nc), A(WN), MIN)
+        if t:
+            tt(A(MID), A(MID), A(B[4], 0, nc), MAX)
 
     def seam(t):
         SCOPE[:] = ["c", 0]
         side = (A(P, 16, 96), A(P, 576, 656))
         buf = lambda nm, w, d: [own("%s%d%d" % (nm, t, e), "sbuf", [128, w], d) for e in range(2)]
         TB, TR, XS, XR = buf("TB", 80, "bfloat16"), buf("TR", 80, "bfloat16"), buf("XS", 480, "uint16"), buf("XR", 480, "uint16")
-        T4, PS, HS, LN_, NMF, O1, RI, O2, LI, LS_ = f(384), f(128), f(120), u(120), f(120), f(120), f(120), f(120), u(120), u(120)
-        for o, c in ((0, 16), (96, 0), (192, 560), (288, 576)):
-            tr(A(T4, o, o + 96), A(P, c, c + 96))
-        cp(A(PS), IND(A(T4), A(LSE)))
+        PS, HS, LN_, NMF, O1, RI, LI, LS_ = f(128), f(120), u(120), f(120), f(120), f(120), u(120), u(120)
+        cp(A(PS), IND(A(TT), A(LSE)))
         ts(A(HS), A(PS, 0, 120), MAGIC, ADD, MAGIC, SUB)
         tt(A(NMF), A(PS, 0, 120), A(HS), SUB)
         ts(A(LN_), A(NMF), -1.0, ADD)
-        tt(A(O1), A(HS), A(AV), LE)
         XN, n, JX = (XM, XL)[t], 2560 + 512 * t, JXS[t]
+        tt(A(O1), A(PS, 0, 120), A(AV), LE)
         tt(A(O1), A(O1), A(JX), MUL)
         tt(A(O1), A(O1), A(NMF), MAX)
+        ts(A(LS_), A(O1), -1.0, ADD)
+        ts(A(TB[0]), side[0], 127.0 * 8192, ADD, 208.0 * 8192, MIN)
+        ts(A(TB[1]), side[1], (127.0 - 560) * 8192, ADD, 127.5 * 8192, MAX)
         for e in range(2):
-            H, V1, V2 = f(80), f(80), f(80)
-            ts(A(H), side[e], MAGIC, ADD, MAGIC + 0.0, SUB)
-            lin(A(H), A(H), 1.0, -8192.0 * (705 + 560 * e), "v")
-            ts(A(V1), A(H), -8192.0 * 704, GE, W["l12"], MUL)
-            if e == 0:
-                ts(A(V2), A(H), -8192.0 * 624, LT)
-                tt(A(V1), A(V1), A(V2), MUL)
-            tt(A(H), A(H), A(V1), MUL)
-            ts(A(TB[e]), A(H), 704.0 * 8192, ADD)
             send(A(TR[1 - e]), A(TB[e]), 2 * e - 1, 4000)
         own_ = (A(GA, 0, 960), A(GA, 960, 1920))
         for e in range(2):
@@ -719,20 +741,18 @@ def program():
             cp(A(XS[e]), A(B[6 + e], 0, 480))
             send(A(XR[1 - e]), A(XS[e]), 2 * e - 1, 5500)
         for e in range(2):
-            Q = b(80)
-            ts(A(Q), A(TR[e]), 600.0 * 8192, MIN)
             for k in range(2):
                 s = (960 * e + 480 * k, 960 * e + 480 * k + 480)
-                mm(sum([acc(A(B[4 + k], 80 * l, 80 * l + 80), [(A3(BL, 6 * k + l), A(TB[e])), (A(NID), A(Q))]) for l in range(6)], []))
-                ts(A(LTT, *s), A(B[4 + k], 0, 480), 0.0, EQ)
+                mm(sum([acc(A(B[4 + k], 80 * l, 80 * l + 80), [(A3(BL, 6 * k + l), A(TB[e])), (A(NID), A(TR[e]))]) for l in range(6)], []))
+                if (t, e, k) in EQS:
+                    act(A(B[4 + k], 0, 480), A(B[4 + k], 0, 480), AF.Abs)
+                    act(A(LTT, *s), A(B[4 + k], 0, 480), AF.Relu, 1.0, -1.0)
+                else:
+                    ts(A(LTT, *s), A(B[4 + k], 0, 480), 0.0, EQ)
             mm(acc(A(B[4], 0, 60), ext(None, ZM, LTT, 60, 960 * e)))
             s = (60 * e, 60 * e + 60)
             tt(A(RI, *s), A(JA, *s), A(B[4], 0, 60), SUB)
             cp(A(LI, *s), A(RI, *s))
-            ts(A(O2, *s), A(RI, *s), 960.0, GE, 8192.0, MUL)
-            tt(A(O2, *s), A(O2, *s), A(JX, *s), MIN)
-            tt(A(O2, *s), A(O2, *s), A(O1, *s), MAX)
-            ts(A(LS_, *s), A(O2, *s), -1.0, ADD)
         for e in range(2):
             XI, KP = ii(480), f(80)
             mn, sg = A(GB, 960 * e, 960 * e + 960), A(LTT, 960 * e, 960 * e + 960)
@@ -749,10 +769,24 @@ def program():
             tt(side[e], side[e], A(KP), MUL)
 
         def store():
-            for e in range(2):
-                for c0, c1 in ((0, 10), (10, 20), (20, 30), (30, 40), (40, 50), (50, 60)) if t == 0 else ((0, 30), (30, 60)):
-                    cp(IND(A(XN), A(LS_, 60 * e + c0, 60 * e + c1)), A(GB, 960 * e + 16 * c0, 960 * e + 16 * c1))
-        return store
+            for c in range(0, 120, 10):
+                cp(IND(A(XN), A(LS_, c, c + 10)), A(GB, 16 * c, 16 * c + 160))
+
+        def last():
+            for c0, c1, e in MAPS:
+                if e == "v":
+                    cp(IND(A(MW, 0, 4032), A(LS_, c0, c1)), A(SD, 16 * c0, 16 * c1))
+                else:
+                    silu(IND(A(WS, 0, 4032), A(LS_, c0, c1)), A(SF, 16 * (c0 - C0), 16 * (c1 - C0)))
+            LF = u(192)
+            for x in range(2):
+                dma(A(MW, 1536 * x, 1536 * x + 1536), A(WS, 1536 * x, 1536 * x + 1536), "g", 4000, True)
+                mm(acc(A(B[6 + x], 0, 96), ext(None, ZZ, MW, 96, 1536 * x)))
+                ts(A(LF, 96 * x, 96 * x + 96), A(B[6 + x], 0, 96), -65.0 * TOP, ADD, 1920.0, MIN)
+            for c0, c1 in OUTS:
+                tt(A(XL, c0, c1), IND(A(GB), A(LF, c0 // 16, c1 // 16)), A(XL, c0, c1), MIN)
+                dma(X("ylen", ALL, slice(c0, c1)), A(XL, c0, c1), "y", 2600 + (c1 - c0) // 2)
+        return last if t else store
 
     LSE, s1, s2, s3, s4, si, JA, AV, JXS, QC, I256 = u(8), f(8), f(8), f(8), f(8), ii(8), f(120), f(120), [f(120), f(120)], f(1), b(128)
     ts(A(s1), A(J, 0, 8), 60.0, GE)
@@ -766,9 +800,8 @@ def program():
     tt(A(s2), A(s2), A(s1), ADD)
     ts(A(si), A(s2), PH, ADD)
     ts(A(si), A(si), 1, AND)
-    ts(A(s4), A(s1), -32.0, MUL, 112.0, ADD)
-    tt(A(s4), A(s4), A(si), MUL)
-    ts(A(s1), A(s1), 208.0, MUL)
+    ts(A(s4), A(si), 656.0, MUL)
+    ts(A(s1), A(s1), 560.0, MUL)
     tt(A(s3), A(s3), A(s1), ADD)
     tt(A(s3), A(s3), A(s4), ADD)
     cp(A(LSE), A(s3))
@@ -776,7 +809,7 @@ def program():
     iota(A(JB), [[0, 24], [16, 5]], 960)
     lin(A(JA), A(JB), 1.0, PM)
     for e in range(2):
-        lin(A(AV, 60 * e, 60 * e + 60), A(JA, 0, 60), 8192.0, 8192.0 * (560 * e - 959))
+        lin(A(AV, 60 * e, 60 * e + 60), A(JA, 0, 60), 8192.0, 8192.0 * (560 * e - 958.5))
         for t in range(2):
             lin(A(JXS[t], 60 * e, 60 * e + 60), A(J, 0, 60), 1.0, 2561.0 + 512 * t)
         fl(A(XW[e], 960, 1040), 255)
@@ -788,21 +821,19 @@ def program():
     lg = choose(0)
     contract(0, lg)
     fill(1)
-    tr(A(TT, 0, 640), A(P, 16, 656))
-    tr(A(TT, 640, 1312), A(P, 0, 672))
-    cp(A(PV), IND(A(TT), A(LSV)), "vs")
-    ts(A(L1), A(PV), U13, MUL, 15.0, ADD)
+    for c in range(0, 30, 10):
+        ts(A(L1, 16 * c, 16 * c + 160), IND(A(TT), A(LSV, c, c + 10)), U13, MUL, 15.0, ADD)
     lg = choose(1)
     contract(1, lg, seam(0))
+    fill(1)
     SCOPE[0] = None
     LMID = u(192)
-    cp(A(LMID), A(MID))
+    ts(A(LMID), A(MID), 16.0 - 17 * TOP, ADD)
     for k in range(4):
         cp(A(YM, 768 * k, 768 * k + 768), IND(A(GOT), A(LMID, 48 * k, 48 * k + 48)), "vs")
     dma(X("ymid", ALL, ALL), A(YM, p=(0, 128, 16)), "y")
     seam(1)()
-    YL, HF, YE, YN = GA, TIN, (TT[0], TT[1], 640), (TT[0], TT[1] + 640, 640)
-    dma(X("ylen", ALL, ALL), A(XL, 0, 3072), "y", 4000)
+    HF, YE, YN = TIN, (TT[0], TT[1], 640), (TT[0], TT[1] + 640, 640)
     q = (0, 96)
     for bk, v0, v1 in ((0, 80, 560), (1, 0, 80), (2, 560, 640)):
         o = A(B[bk], 0, v1 - v0, p=q)
@@ -1028,8 +1059,9 @@ def rank_program(g, core, T, topo):
             g.remote_dma(real(T, dst), real(T, src), T.sem[rs], T.sem[o["sem"]], pid, rid, sum(1 << x for x in es))
             mark[k] = (o["sem"], len(es))
         elif "sem" in o:
-            fn(g, T).then_inc(T.sem[o["sem"]], 16)
-            mark[k] = (o["sem"], 16)
+            for one in fn if isinstance(fn, list) else [fn]:
+                one(g, T).then_inc(T.sem[o["sem"]], 16)
+            mark[k] = (o["sem"], o["inc"])
         else:
             s = "e" + e
             fn(g, T).then_inc(T.sem[s], 1)

@@ -236,14 +236,17 @@ def send(dst, src, step, lat):
 
 
 PEC = 0.6
-CV = [100, 50]
-MAPS = [(0, 20, "v"), (20, 40, "v"), (40, 60, "v"), (60, 90, "s"), (90, 120, "s")]
-C0 = min(CV + [m[0] for m in MAPS if m[2] == "s"])
+CV = [100, 100]
+MAPC = 20
+C0 = min(CV + [78])
+XNC = 512
+PSC = 12
 MKV = [0]
 OUTS = [(0, 1024), (1024, 2048), (2048, 2560), (2560, 3072)]
 LOW = 65
 TOP = LOW + 16
-EQS = [(1, 0, 0), (1, 0, 1), (1, 1, 0), (1, 1, 1)]
+EQS = []
+EQT = [(1, 0, 0), (1, 0, 1), (1, 1, 0), (1, 1, 1)]
 CLAMP = [(0, 21), (21, 45), (45, 66)]
 
 
@@ -251,15 +254,15 @@ def program():
     f, b, h, ii, u = (lambda n: al("f", n)), (lambda n: al("b", n)), (lambda n: al("h", n)), (lambda n: al("i", n)), (lambda n: al("u", n))
     B = [own("B%d" % k, "psum", [128, 512], "float32") for k in range(8)]
     WS = f(5760 + 16 * (198 - min(CV)))
-    YM, DD, CC = (WS[0], WS[1] + 4096, 3072), (WS[0], WS[1] + WS[2] - 3168, 3168), h(3168)
+    YM, CC = (WS[0], WS[1], 3072), h(3168)
     BL = own("BL", "sbuf", [128, 12, 128], "bfloat16")
     L1, R2 = u(480), f(128)
-    XL = own("XL", "sbuf", [128, 4032], "bfloat16")
-    SD = b(16 * max(CV) + 3520)
-    XM, SF = (SD[0], SD[1] + 16 * max(CV), 3520), f(16 * (198 - C0))
+    XL = own("XL", "sbuf", [128, 3072], "bfloat16")
+    SD = b(16 * max(CV) + 4992)
+    GB, XM, SF = (SD[0], SD[1] + 16 * max(CV), 1920), (SD[0], SD[1] + 16 * max(CV) + 1920, 3072), f(16 * (198 - C0))
     XW = [ii(1040), ii(1040)]
     EN, NB = XW[0][:2] + (480,), (XW[0][0], XW[0][1] + 480, 480)
-    UW = own("UW", "sbuf", [128, 8704], "bfloat16")
+    UW = own("UW", "sbuf", [128, 8192], "bfloat16")
     MW = own("MW", "sbuf", [128, max(7168, 5760 + 16 * max(CV))], "bfloat16")
     col = lambda t, k: A(t, k, k + 1)
     Z = lambda z, t: A(z, 15 - t, 143 - t)
@@ -294,9 +297,9 @@ def program():
     early = [("key", [1024] * 12 + [128, 32, 1, -229376]), ("fs", [1] * 13 + [U13, 1, 1]), ("fc", [1] * 12 + [4096] * 4),
              ("pd", [0] * 12 + [1920, 22 * 8192 + 3072, 0, 1]), ("fd", [0] * 12 + [1920, 22.375, 0, 1]),
              ("dg", [1] * 12 + [1 / 128, 0, 0, -13])]
-    late = [("vb", {13: 262144, 14: 8192, 15: -88064}), ("got", {13: 32, 14: 1, 15: -12}), ("wa", {0: 1, 1: 16, 2: 48}),
+    late = [("vb", {13: 2048, 14: 64, 15: -688}), ("wu", {13: 32, 14: 1}), ("wa", {0: 1, 1: 16, 2: 48}),
             ("wb", {0: 1, 1: 16, 3: 48}), ("sa", {1: 16, 2: 48, 3: 1}), ("sb", {1: 16, 2: 1, 3: 48}),
-            ("upd", {12: 1, 13: 262144, 14: 8192, 15: 32}), ("zz", {0: 1, 1: 16, 4: 48}), ("aa", {0: 1, 1: 16}), ("ab", {0: 1, 1: 16, 5: 0.5}), ("zd", {0: 1, 1: 16, 6: 48})]
+            ("upd", {12: 1, 13: 262144, 14: 8192, 15: 32}), ("zz", {0: 1, 1: 16, 4: 48}), ("zd", {0: 1, 1: 16, 5: 48})]
     W16, WC, W = f(32), f(48), {}
     for k, (n, w) in enumerate(early):
         for r in range(16, 0, -1):
@@ -305,24 +308,23 @@ def program():
         W[n] = col(WC, k)
     mm([(A(B[2], 0, 6), A(OH, p=(0, 16)), A(W16, 0, 6, p=(0, 16)), True, True)])
     cp(A(WC, 0, 6), A(B[2], 0, 6))
-    ms(A(W16, 8, 19, p=(0, 16)), 0.0)
+    ms(A(W16, 8, 17, p=(0, 16)), 0.0)
     for e in range(4):
         for k, (n, w) in enumerate(late):
             if e < len(w):
                 r = sorted(w)[e]
                 asel(A(W16, 8 + k, 9 + k, p=(0, 16)), NE, float(w[r]), -r, 1)
             W[n] = col(WC, 8 + k)
-    mm([(A(B[5], 0, 11), A(OH, p=(0, 16)), A(W16, 8, 19, p=(0, 16)), True, True)])
-    cp(A(WC, 8, 19), A(B[5], 0, 11))
-    for k, (n, o, v, w) in enumerate([("s01", LT, 2, 1), ("o14", LT, 14, 1), ("w640", LT, 12, -320), ("l12", LT, 12, 1), ("cm", GE, 12, 1),
-                                      ("cx", EQ, 12, 1920), ("ps", GE, 13, 1), ("n15", LT, 15, 1), ("m12", LT, 12, -1), ("p0", GE, 1, 1)]):
+    mm([(A(B[5], 0, 9), A(OH, p=(0, 16)), A(W16, 8, 17, p=(0, 16)), True, True)])
+    cp(A(WC, 8, 17), A(B[5], 0, 9))
+    for k, (n, o, v, w) in enumerate([("s01", LT, 2, 1), ("o14", LT, 14, 128), ("w640", LT, 12, -320), ("l12", LT, 12, 1), ("cm", GE, 12, 1),
+                                      ("cx", EQ, 12, 1920), ("ps", GE, 13, 1), ("n15", LT, 15, 1), ("mh", LT, 12, -0.5), ("p0", GE, 1, 1),
+                                      ("m2", LT, 12, -2), ("k16", LT, 12, 16)]):
         W[n] = col(WC, 20 + k)
         ts(W[n], PM, float(v), o, float(w), MUL)
-    W["uba"], W["wu"], W["z14"], W["n14"] = col(WC, 32), col(WC, 33), col(WC, 34), col(WC, 35)
-    tt(W["uba"], W["vb"], W["n15"], MUL)
-    tt(W["wu"], W["got"], W["n15"], MUL)
-    ts(W["z14"], col(OH, 15), 553 / 2048, MUL, W["o14"], ADD)
-    ts(W["n14"], col(OH, 15), -553 / 4096, MUL, W["o14"], SUB)
+    W["uba"], W["z14"] = col(WC, 32), col(WC, 34)
+    ts(W["uba"], W["vb"], W["n15"], MUL)
+    ts(W["z14"], col(OH, 15), 553 / 16, MUL, W["o14"], ADD)
 
     def zt(n, kind="b"):
         z = al(kind, 144)
@@ -336,7 +338,7 @@ def program():
     ZKEY = zt("key")
     BKEY, BDG, BS01, BVB, BGOT, PAS = bt("key"), bt("dg"), bt("s01"), bt("vb"), None, bt("ps", ID)
     Z14, ZL12, ZA, ZBB, ZSA, ZSB, Z640, ZU, ZUP = zt("z14", "h"), zt("l12"), zt("wa"), zt("wb"), zt("sa"), zt("sb"), zt("w640"), zt("wu"), zt("upd")
-    ZZ, ZQ, ZAA, ZN14 = zt("zz"), zt("zd"), [zt("aa"), zt("ab")], zt("n14", "f")
+    ZZ, ZQ, ZM2 = zt("zz"), zt("zd"), zt("m2")
     ZT, ONE = b(1024), b(512)
     ms(A(ZT), 0.0)
     for i in range(0, 12, 4):
@@ -350,15 +352,26 @@ def program():
     NPM = f(2)
     ts(col(NPM, 0), PM, -1.0, MUL, -float(TOP), ADD)
     ts(col(NPM, 1), PM, float(TOP), ADD)
-    TS, SFX, NBD, UBM, t2 = b(128), b(128), b(128), b(128), f(128)
+    TS, SFH, SFF, NBD, UBM, t1, t2, t3 = b(128), b(128), b(128), b(128), b(128), b(128), f(128), f(1)
     asel(A(TS), GT, 0.0, 0, -1, [[1, 128]], A(BD))
-    asel(A(SFX), GT, 0.0, 0, 1, [[-1, 128]], bt("m12"))
+    asel(A(SFH), GT, 0.0, 0, 1, [[-1, 128]], bt("mh"))
+    ts(A(t3), col(OH, 15), 1.5, MUL)
+    ts(A(t1), A(X16), 11.0, MIN, -11.0, ADD)
+    ts(A(t1), A(t1), A(t3), MUL)
+    tt(A(t1), A(t1), A(BD), MUL)
+    tt(A(t1), A(t1), PAS, ADD)
+    ts(A(SFF), A(SFH), -2.0, MUL)
+    tt(A(SFF), A(SFF), A(t1), ADD)
     lin(A(NBD), A(BD), -1.0, 0.0)
-    fl = lambda out, c: iota(out, [[0, out[4]]], c)
-    fl(A(R2), -88064)
-    fl(A(R2, 12, 128, 16), -716 * 8192)
-    fl(A(R2, 13, 128, 16), 182272)
-    fl(A(R2, 15, 128, 16), 4096)
+
+    def fl(out, c):
+        iota(out, [[0, out[4]]], c)
+        ms(out, c if out[0] == "pi" else float(c))
+        OPS[-2]["alts"] += OPS.pop()["alts"]
+    fl(A(R2), -688)
+    fl(A(R2, 12, 128, 16), -716 * 64)
+    fl(A(R2, 13, 128, 16), 1424)
+    fl(A(R2, 15, 128, 16), 32)
     t4, t5 = f(128), f(128)
     ts(A(t2), A(X16), 13.0, LT, W["uba"], MUL)
     lin(A(t4), A(R2), col(OH, 15), 0.0)
@@ -366,14 +379,15 @@ def program():
     tt(A(UBM), A(t5), A(BD), MUL)
     fl(A(ONE), 1)
     MB, MF, NID = b(512), f(512), b(128)
-    fl(A(MB), LOW)
+    op([("s", act_alt(A(MB), A(ZT, 0, 512), AF.Silu, float(LOW), 1.0, None)[1], 2110)], [A(MB)], [A(ZT, 0, 512)])
     fl(A(MF), LOW)
     lin(A(NID), A(ID), -1.0, 0.0)
     P, F, W2, Y, PFU, ST, WW = f(1280), b(1280), b(656), b(576), b(656), b(592), b(256)
     lin(A(P, 0, 16), A(ZT, 0, 16), 1.0, W["pd"])
-    lin(A(P, 656, 1280), A(ZT, 0, 624), 1.0, W["pd"], "s")
     lin(A(F, 0, 16), A(ZT, 0, 16), 1.0, W["fd"])
-    lin(A(F, 656, 1280), A(ZT, 0, 624), 1.0, W["fd"])
+    for t, w in ((P, "pd"), (F, "fd")):
+        lin(A(t, 656, 760), A(ZT, 0, 104), 1.0, W[w])
+        dmas([(A(t, c, c + 104), A(t, 656, 760)) for c in range(760, 1280, 104)], 3000)
     ms(A(W2, 0, 16), 0.0)
     ms(A(PFU, 576, 656), 0.0)
     ms(A(ST, 576, 592), 0.0)
@@ -437,8 +451,9 @@ def program():
     def turn(out):
         tr(A(XT, 0, 640), A(XI_, 16, 656))
         tr(A(XT, 640, 1312), A(XI_))
-        cp(out, IND(A(XT), A(LVS)), "vs")
-    turn(A(F, 16, 656))
+        for c in (0, 20):
+            cp(A(out, 16 + 16 * c, 336 + 16 * c), IND(A(XT), A(LVS, c, c + 20)), "vs")
+    turn(F)
     ts(A(L1), A(NB), 16.0, ADD)
     lin(A(NX), A(NB), 8192.0, 8193.0, "v")
     for k in range(12):
@@ -450,21 +465,23 @@ def program():
     for j in range(11):
         lex.append(lex[-1] + 11 - j)
     row = lambda t, r, *s: A(t, *s, p=(r, 128, 16))
-    DG, DC, DJ, DQ, OI = b(208), b(208), b(208), b(208), f(16)
+    LT2 = b(2560)
+    part = lambda o, n: (LT2[0], LT2[1] + o, n)
+    DG, DC, DJ, DQ, OI = b(208), part(0, 208), part(208, 208), part(416, 208), f(16)
     for j in range(11):
         iota(A(DG, 3 * lex[j], 3 * lex[j + 1]), [[1, 11 - j], [0, 3]], 17 + j)
         fl(A(DJ, 3 * lex[j], 3 * lex[j + 1]), 16 + j)
     fl(A(DG, 198, 208), LOW)
     iota(A(DC, 0, 198), [[0, 66], [1, 3]], 16)
     iota(A(DQ, 0, 198), [[1, 66], [0, 3]], 16)
-    D1, D2, D3 = b(198), b(198), b(198)
+    D1, D2, D3 = part(624, 198), part(832, 198), part(1040, 198)
     mm(acc(A(B[5], 0, 198), [(A(ID), A(DG, 0, 198)), (A(NID), A(DJ, 0, 198))]))
     lin(A(D1), A(B[5], 0, 198), -0.5, 12.0)
     lin(A(D2), A(B[5], 0, 198), 1.0, -1.0)
     tt(A(D1), A(D1), A(D2), MUL)
     mm(acc(A(B[5], 0, 198), [(A(ID), A(D1)), (A(ID), A(DJ, 0, 198))]))
     cp(A(D3), A(B[5], 0, 198), "vs")
-    dmas([(row(DG, r, 0, 198), row(t, r, 0, 198)) for r, t in ((1, DC), (2, DJ), (4, DQ), (5, MB), (6, D3))], 2600)
+    dmas([(row(DG, r, 0, 198), row(t, r, 0, 198)) for r, t in ((1, DC), (2, DJ), (4, DQ), (5, D3))], 2600)
     LUP, LDN, LSQ = u(14), u(14), u(36)
     mm(acc(A(B[5], 0, 13), ext(None, ZSA, DG, 13)) + acc(A(B[5], 16, 29), ext(None, ZSB, DG, 13)))
     ts(A(LUP, 0, 13), A(B[5], 0, 13), 1.0 - 16 * 65, ADD, 591.0, MIN)
@@ -492,14 +509,13 @@ def program():
     tt(A(q1), A(q1), A(q3), ADD)
     cp(A(LSQ), A(q1))
     ts(A(OI), A(X16, 0, 16), 16.0, ADD, col(OH, 0), MUL)
-    for i in range(15):
+    for i in range(16):
         lin(A(SD, i, 3168, 16), A(DG, 0, 198), W["p0"], col(OI, i))
-    op([("s", act_alt(A(SD, 15, 3168, 16), A(DG, 0, 198), AF.Silu, col(OI, 15), W["p0"], None)[1], 1800)], [A(SD, 15, 3168, 16)], [A(DG), W["p0"], A(OI)])
     dma(A(SF), A(SD, 16 * C0, 3168), "g", 4000)
     RS1 = b(576)
     fl(A(RS1), 1)
     fl(A(RS1, 0, 576, 16), 0)
-    N1, N2, NM = b(512), b(512), [b(512), b(512)]
+    N1, N2, NM = part(1248, 512), part(1760, 512), [b(512), b(512)]
     fl(A(N1), -11)
     for t in range(2):
         iota(A(NM[t]), [[0, 16], [1, 32]], 1)
@@ -507,21 +523,22 @@ def program():
         for r, s in ((13, ZT), (14, N1), (15, N2)):
             dma(row(NM[t], r), row(s, r, 0, 512))
     JG, JU, JM, JQ = f(3), f(36), [f(198), f(198)], f(32)
-    for t, n, m, c in ((JG, 3, 1.0, 656.0), (JU, 36, 8192.0, 641.0 * 8192), (JQ, 32, 1.0, 3852.0)):
+    for t, n, m, c in ((JG, 3, 1.0, 656.0), (JU, 36, 8192.0, 641.0 * 8192), (JQ, 32, 1.0, 7692.0)):
         lin(A(t), A(J, 0, n), m, c)
     for t in range(2):
         lin(A(JM[t], 0, CV[t]), A(J, 0, CV[t]), 1.0, 5760.0 - 552)
         lin(A(JM[t], CV[t], 198), A(J, 0, 198 - CV[t]), 1.0, 5760.0 - 552)
     MID, GOT, NW = f(192), f(144), b(208)
-    fl(A(MID, 160, 192), 0)
     fl(A(NW, 198, 208), 0)
     fl(A(GOT), -1)
 
     RH = UW
-    ZD, GB, LTT = b(3200), b(1936), (MW, 4096, 3072)
+    ZD, LTT = b(3200), (MW, 4096, 1920)
     fl(A(ZD, 3168, 3184), 0)
     fl(A(ZD, 3184, 3200), 255)
-    fl(A(GB, 1920, 1936), 255)
+    MT, MR, MQ, LA, WN, JF, MG = f(192), f(192), ii(192), u(192), f(32), f(192), f(512)
+    fl(A(MG), 200)
+    lin(A(JF), A(J, 0, 192), 1.0, 1920.0 + 16 * (65 + C0))
     GA = ZD
 
     def choose(t):
@@ -549,7 +566,7 @@ def program():
         tt(A(M1), A(AC, 0, 40), A(AC, 40, 80), MIN)
         tt(A(XI_, 16, 656, 16), A(AC, 0, 40), A(AC, 40, 80), MIN)
         tt(A(XI_, 17, 656, 16), A(M1), A(XI_, 16, 656, 16), SUB)
-        turn(A(W2, 16, 656))
+        turn(W2)
         for k in range(12):
             cp(A(RH, 496 * k, 496 * k + 496), IND(A(W2), A(L1, 40 * k + 4, 40 * k + 35)), "vs")
             mm([(A(B[0], 0, 480), BS01, A(W2, 96, 576), True, False)] * (k == 0) + [(A(B[0], 0, 480), BS01, A(RH, 496 * k + 16, 496 * k + 496), False, k == 11)])
@@ -566,15 +583,11 @@ def program():
         ts(A(GN), A(GN), 0.5, MUL, 336.0, ADD)
         tt(A(GN), A(GN), A(G2), ADD)
         cp(A(LG, 0, 3), A(GN))
-        clear()
         return A(LG, 0, 3)
 
-    def contract(t, LG, store=None):
-        n, n0 = 2560 + 512 * t, 2048 + 512 * t
-        nc = n // 16
-        SCOPE[:] = ["b", 0]
-        GT2, GV, FG, U1, U2, GH, GC, LU, LE_, FU = f(128), f(48), b(48), f(36), f(36), f(36), f(48), u(36), u(36), b(576)
-        NR, NH, NK, FRE, VS = f(576), f(576), f(576), b(576), f(48)
+    GT2, GV, FG, U1, U2, GH, GC, LU, LE_, FU = f(128), f(48), b(48), f(36), f(36), f(36), f(48), u(36), u(36), b(576)
+
+    def lists(t, LG):
         cp(A(GR, 16, 64), IND(A(P), LG))
         cp(A(FG), IND(A(F), LG), "s")
         tr(A(GT2, 0, 64), A(GR, 16, 80))
@@ -584,15 +597,19 @@ def program():
         tt(A(U2), A(U2), A(JU), MUL)
         tt(A(U1), A(GV, 0, 36), A(U2), ADD)
         ts(A(LU), A(U1), U13, MUL, 15.0, ADD)
-        cp(A(NR), IND(A(P), A(LU)))
-        cp(A(FU), IND(A(F), A(LU)), "s")
         ts(A(GH), A(GV, 0, 36), MAGIC, ADD, MAGIC, SUB)
         tt(A(GH), A(GV, 0, 36), A(GH), SUB)
         ts(A(LE_), A(GH), -1.0, ADD)
-        XO, XN = (XL, XM)[t], (XM, XL)[t]
-        cp(A(Y), IND(A(XO, 0, n0), A(LE_)), "s")
-        if store:
-            store()
+        cp(A(Y), IND(A(XM, 0, 2560) if t else A(XL, 0, 2048), A(LE_)), "s")
+
+    def contract(t, LG, store=None):
+        n, n0 = 2560 + 512 * t, 2048 + 512 * t
+        nc = n // 16
+        SCOPE[:] = ["b", 0]
+        NS, NK, SG, KW = f(576), f(576), b(576), f(1280)
+        ts(A(NS), IND(A(P), A(LU)), 1 / 128, MUL)
+        cp(A(FU), IND(A(F), A(LU)), "vs")
+        XO, XN = XL, XM
         tiles = [(0, 6), (6, 11), (11, 21), (21, 30), (30, 38), (38, 45), (45, 51), (51, 60), (60, 66)]
         runs = lambda q0, q1: [(j, max(q0, lex[j]), min(q1, lex[j + 1])) for j in range(11) if lex[j] < q1 and q0 < lex[j + 1]]
         for x, (q0, q1) in enumerate(tiles):
@@ -600,37 +617,35 @@ def program():
             mm([(A(bk, 48 * (q - q0), 48 * (q - q0 + 1)), A(UBM), A(FU, 48 * j, 48 * j + 48), True, True) for j, a0, a1 in runs(q0, q1) for q in range(a0, a1)])
             for j, a0, a1 in runs(q0, q1):
                 k0 = j + 1 - lex[j]
-                tt(A(DD, 48 * a0, 48 * a1), A(NR, 48 * (k0 + a0), 48 * (k0 + a1)), A(bk, 48 * (a0 - q0), 48 * (a1 - q0)), SUB)
+                tt(A(CC, 48 * a0, 48 * a1), A(NS, 48 * (k0 + a0), 48 * (k0 + a1)), A(bk, 48 * (a0 - q0), 48 * (a1 - q0)), SUB)
         for x, (q0, q1) in enumerate(CLAMP):
-            if x == 0:
-                act(A(DD, 0, 48 * q1), A(DD, 0, 48 * q1), AF.Relu, 2048.0)
-                act(A(DD, 0, 48 * q1), A(DD, 0, 48 * q1), AF.Relu, 4096.0, -1.0)
-                mm(acc(A(B[0], 0, 3 * q1), ext(None, ZN14, DD, 3 * q1)))
-                continue
-            ts(A(CC, 48 * q0, 48 * q1), A(DD, 48 * q0, 48 * q1), -2048.0, MAX, 2048.0, MIN)
+            ts(A(CC, 48 * q0, 48 * q1), A(CC, 48 * q0, 48 * q1), -16.0, MAX, 16.0, MIN)
             mm(acc(A(B[0], 3 * q0, 3 * q1), ext(None, Z14, CC, 3 * (q1 - q0), 48 * q0)))
         dmas([(A(ZD, 48 * lex[d], 48 * lex[d + 1]), A(Y, 48 * d + 48, 576)) for d in range(11)]
-             + [(A(XN, 48 * lex[d], 48 * lex[d + 1]), A(Y, 0, 528 - 48 * d)) for d in range(11)], 7000)
+             + [(A(UW, 48 * lex[d], 48 * lex[d + 1]), A(Y, 0, 528 - 48 * d)) for d in range(11)], 7000)
         for c in (0, 1584):
-            dma(A(ZD, c, c + 1584), A(XN, c, c + 1584), "g", 4500, True)
+            dma(A(ZD, c, c + 1584), A(UW, c, c + 1584), "g", 4500, True)
+        clear()
+        if store:
+            middles(0)
+            store()
         for k in range(2):
             mm([(A(B[1 + k], 48 * j, 48 * j + 48), BVB, A(FG), True, True) for j in range(6)])
             if k == 0:
-                lin(A(GOT, 65 * t + 16, 65 * t + 64), A(B[1], 0, 48), U13, -1.25)
-            s = (288 * k, 288 * k + 288)
-            tt(A(NK, *s), A(B[1 + k], 0, 288), A(NR, *s), SUB)
-            act(A(NH, *s), A(NK, *s), AF.Abs)
-            act(A(B[1 + k], 0, 288), A(NH, *s), AF.Relu, -3000.0 * 4096, 4096.0)
-            tt(A(NK, *s), A(B[1 + k], 0, 288), A(NR, *s), MIN)
-        act(A(FRE), A(NK), AF.Relu, 1.0, -1.0)
-        mm(acc(A(B[1], 0, 36), ext(None, ZL12, FRE, 36)))
-        lin(A(WW, 200, 236), A(B[1], 0, 36), -1.0, 0.0)
+                lin(A(GOT, 65 * t + 16, 65 * t + 64), A(B[1], 0, 48), 1 / 64, -1.25)
+            tt(A(NK, 288 * k, 288 * k + 288), A(B[1 + k], 0, 288), A(NS, 288 * k, 288 * k + 288), SUB)
+        act(A(NK), A(NK), AF.Square, 0.0, 1 / 32)
+        act(A(SG), A(NK), AF.Sign, 1.0, -1.0)
+        mm(acc(A(B[1], 0, 36), ext(None, ZL12, SG, 36) + ext(None, ZM2, FU, 36)))
+        lin(A(WW, 200, 236), A(B[1], 0, 36), -0.5, -18.0)
         for k in range(2):
             s = (288 * k, 288 * k + 288)
-            mm(acc(A(B[2 - k], 0, 288), [(A(SFX), A(FRE, *s)), (PAS, A(FU, *s))]))
+            mm(acc(A(B[2 - k], 0, 288), [(A(SFH), A(SG, *s)), (A(SFF), A(FU, *s))]))
             cp(A(PFU, *s), A(B[2 - k], 0, 288), "s")
-        for c in range(0, 36, 12):
-            cp(IND(A(P), A(LU, c, c + 12)), A(NK, 16 * c, 16 * c + 192))
+        fl(A(KW, 0, 656), 32)
+        lin(A(NK), A(SG), W["k16"], 48.0, "s")
+        for c in range(0, 36, PSC):
+            silu(IND(A(KW), A(LU, c, c + PSC)), A(NK, 16 * c, 16 * (c + PSC)))
         ts(A(GC), A(GR, 16, 64), W["cm"], MUL, W["cx"], MAX)
         cp(IND(A(P), LG), A(GC))
         RH_, RL, SQ, SU, SV, IN, OF, LM = f(198), f(198), b(576), b(208), b(208), b(198), f(198), u(200)
@@ -659,11 +674,17 @@ def program():
         cp(IND(A(MW), A(LM, 0, CV[t])), A(SD, 0, 16 * CV[t]))
         silu(IND(A(WS), A(LM, CV[t], 198)), A(SF, 16 * (CV[t] - C0)))
         tt(A(MW, n0, n), A(MW, n0, n), A(WS, n0, n), ADD)
-        olds = [(c, min(c + 1024, n0)) for c in range(0, n0, 1024)]
+        olds = [(0, 1024), (1024, n0)]
         for c0, c1 in olds:
             dma(A(MW, c0, c1), A(WS, c0, c1), "g", 4000, True)
-        LA, LN, LS, AN = u(192)[:2] + (nc,), u(64), u(64), f(32)
-        MK, SM, G, CM, PO, PE_, LP = b(512), b(1024), b(1024), b(1024), f(64), f(64), u(64)
+        for k in range(2):
+            act(A(B[6], 0, 320), A(KW, 16 + 320 * k, 336 + 320 * k), AF.Relu, 56.0 * 2 ** 20, -2.0 ** 20)
+            tt(A(P, 16 + 320 * k, 336 + 320 * k), A(B[6], 0, 320), A(P, 16 + 320 * k, 336 + 320 * k), MIN)
+        LN, LS, AN = u(64), u(64), f(32)
+        dmas([(A(WS, 3072 + c, 3584 + c), A(MG)) for c in range(0, n0, 512)], 5000)
+        for c in range(0, 120, MAPC):
+            silu(IND(A(WS, 3072, 4032 + n0), A(LS_, c, c + MAPC)), A(SF, 16 * c, 16 * (c + MAPC)))
+        MK, SM, G, CM, PO, PE_, UX, LP = b(512), b(1024), b(1024), b(1024), f(64), f(32), f(64), u(64)
         mm([(A(B[2]), A3(BL, 0), A(MW, n0, n), True, True)])
         if t in MKV:
             ts(A(MK), A(B[2]), A(NPM, 1, 2), EQ)
@@ -678,58 +699,101 @@ def program():
             ts(A(LN, *l), A(B[3 * e], 0, 32), -65.0 * TOP, ADD, 640.0, MIN)
             if e == 0:
                 lin(A(AN), A(B[0], 0, 32), 16384.0, -16384 * (575.5 + 65 * TOP))
-            tt(A(PE_, *l), A(AN), A(JQ), MIN)
+                tt(A(PE_), A(AN), A(JQ), MIN)
             cp(A(G, *s), IND(A(PFU), A(LN, *l)), "s")
             tt(A(SM, *s), IND(A(ST), A(LS, *l)), A(MK), MUL)
+        mm(acc(A(B[5], 0, 64), ext(None, ZU, G, 64)))
+        for e in range(2):
+            tt(A(UX, 32 * e, 32 * e + 32), A(B[5], 32 * e, 32 * e + 32), A(PE_), MAX)
         for e in range(2):
             s, l = (512 * e, 512 * e + 512), (32 * e, 32 * e + 32)
             mm(acc(A(B[e]), [(A(ID), A(G, *s)), (A(NBD), A(SM, *s))]))
             act(A(CM, *s), A(B[e]), AF.Sign, 0.5)
-            mm(acc(A(B[2 + e], 0, 32), ext(None, ZU, G, 32, s[0]) + ext(None, Z640, CM, 32, s[0])))
-            tt(A(PO, *l), A(B[2 + e], 0, 32), A(PE_, *l), MAX)
+            mm(acc(A(B[2 + e], 0, 32), ext(None, Z640, CM, 32, s[0])))
+            tt(A(PO, *l), A(B[2 + e], 0, 32), A(UX, *l), ADD)
             ts(A(LP, *l), A(PO, *l), 3828.0, ADD)
             tt(IND(A(UW), A(LP, *l)), A(G, 512 - s[0], 1024 - s[0]), A(NM[t]), ADD)
+        a1, a2, a3 = f(32), f(32), f(32)
+        lin(A(a3), A(B[2], 0, 32), 0.125, 468.0 + 16 * (65 + C0))
+        tt(A(a1), A(UX, 0, 32), A(UX, 32, 64), MAX)
+        tt(A(a2), A(UX, 0, 32), A(UX, 32, 64), MIN)
+        ts(A(a1), A(a1), 92.0, GE, 8192.0, MUL)
+        ts(A(a2), A(a2), 572.0, GE, -7792.0, MUL)
+        tt(A(a1), A(a1), A(a2), ADD)
+        tt(A(a1), A(a1), A(UX, 0, 32), ADD)
+        tt(A(a1), A(a1), A(a3), ADD)
+        tt(A(a1), A(a1), A(JF, n0 // 16, nc), MIN)
+        ts(A(LF, n0 // 16, nc), A(a1), -16.0 * (65 + C0), ADD)
         for k, (v0, v1) in enumerate(((0, 96), (544, 640), (96, 320), (320, 544))):
-            mm(acc(A(B[k % 3], 0, v1 - v0), [(Z(ZUP, l), A(UW, 640 * l + v0, 640 * l + v1)) for l in range(12)]))
-            tt(A(P, 16 + v0, 16 + v1), A(B[k % 3], 0, v1 - v0), A(P, 16 + v0, 16 + v1), ADD)
+            bk = A(B[min(k, 2) if t else k % 3], 0, v1 - v0)
+            mm(acc(bk, [(Z(ZUP, l), A(UW, 640 * l + v0, 640 * l + v1)) for l in range(12)]))
+            tt(A(P, 16 + v0, 16 + v1), bk, A(P, 16 + v0, 16 + v1), ADD)
         for v0, v1 in ((0, 96), (544, 640)) + ((96, 320), (320, 544)) * (t == 0):
             tr(A(TT, v0, v1), A(P, 16 + v0, 16 + v1))
         for v0, v1 in ((0, 96), (576, 672)) + ((96, 320), (320, 576)) * (t == 0):
             tr(A(TT, 640 + v0, 640 + v1), A(P, v0, v1))
-        WN = f(192)[:2] + (nc,)
+        a4 = f(160)
         for x, (c0, c1) in enumerate([(n0, n)] + olds):
             s, w = (c0 // 16, c1 // 16), (c1 - c0) // 16
-            mm(acc(A(B[3 + x % 2], 0, w), ext(None, ZQ, MW, w, c0)))
-            ts(A(LA, *s), A(B[3 + x % 2], 0, w), -65.0 * TOP, ADD, 3185.0 if x else 3170.0, MIN)
+            mm(acc(A(B[7 - 3 * (x % 2)], 0, w), ext(None, ZQ, MW, w, c0)))
+            ts(A(LA, *s), A(B[7 - 3 * (x % 2)], 0, w), -65.0 * TOP, ADD, 3185.0 if x else 3170.0, MIN)
         ts(A(XN, n0, n), IND(A(ZD), A(LA, n0 // 16, nc)), 255.0, MIN)
+        for c in range(0, n0, XNC):
+            tt(A(XN, c, c + XNC), IND(A(ZD), A(LA, c // 16, (c + XNC) // 16)), A(XO, c, c + XNC), MIN)
+        lin(A(WN), A(AN), -1.0, 0.0)
+        dma(A(MW, 0, n0), A(WS, 3072, 3072 + n0), "g", 4500)
+        mm(acc(A(B[3], 0, n0 // 16), ext(None, ZZ, MW, n0 // 16)))
+        tt(A(a4, 0, n0 // 16), A(B[3], 0, n0 // 16), A(JF, 0, n0 // 16), MIN)
+        ts(A(LF, 0, n0 // 16), A(a4, 0, n0 // 16), -16.0 * (65 + C0), ADD)
+
+    def middles(t):
+        n0 = 2048 + 512 * t
+        nc = n0 // 16 + 32
+        ts(A(MQ, 0, nc), A(LA, 0, nc), -23.5, ADD, 1 / 48, MUL)
+        cp(A(MT, 0, nc), A(LA, 0, nc))
+        ts(A(MR, 0, nc), A(MQ, 0, nc), -48.0, MUL, 65.0 * t, ADD)
+        tt(A(MT, 0, nc), A(MT, 0, nc), A(MR, 0, nc), ADD)
+        tt(A(MID, nc - 32, nc), A(MT, nc - 32, nc), A(WN), MIN)
         for k in range(n0 // 512):
             s = (512 * k, 512 * k + 512)
-            tt(A(XN, *s), IND(A(ZD), A(LA, 32 * k, 32 * k + 32)), A(XO, *s), MIN)
-            mm(acc(A(B[5 + k % 2]), [(A(ID), A(XO, *s)), (A(NID), A(XN, *s))]))
-            act(A(LTT, *s), A(B[5 + k % 2]), AF.Sign, -0.5)
-        mm(acc(A(B[3], 0, n0 // 16), ext(None, ZB, LTT, n0 // 16)))
-        lin(A(WN, 0, n0 // 16), A(B[3], 0, n0 // 16), 4096.0, -4096.0)
-        lin(A(WN, n0 // 16, nc), A(AN), -1.0, 0.0)
-        mm(acc(A(B[4], 0, nc), ext(None, ZAA[t], MW, nc)))
-        tt(A(B[4], 0, nc) if t else A(MID, 0, nc), A(B[4], 0, nc), A(WN), MIN)
+            mm(acc(A(B[5 + k % 2]), [(A(ID), A(XL, *s)), (A(NID), A(XM, *s))]))
+            act(A(LT2, *s), A(B[5 + k % 2]), AF.Sign, -0.5)
+        o, m = A(B[3 + 4 * t], 0, n0 // 16), A(MID, 0, n0 // 16)
+        mm(acc(o, ext(None, ZB, LT2, n0 // 16)))
+        lin(o, o, 4096.0, -4096.0)
+        tt(o if t else m, o, A(MT, 0, n0 // 16), MIN)
         if t:
-            tt(A(MID), A(MID), A(B[4], 0, nc), MAX)
+            tt(m, m, o, MAX)
+
+    def places(t):
+        SCOPE[:] = ["d", 0]
+        PS, HS, O1, O2 = f(128), f(120), f(120), f(60)
+        if t:
+            for v0 in (0, 544):
+                tr(A(TT, v0, v0 + 96), A(P, 16 + v0, 112 + v0))
+            for v0 in (0, 576):
+                tr(A(TT, 640 + v0, 736 + v0), A(P, v0, v0 + 96))
+        cp(A(PS), IND(A(TT), A(LSE)) if t else IND(A(TIN), A(LS0)))
+        ts(A(HS), A(PS, 0, 120), MAGIC, ADD, MAGIC, SUB)
+        tt(A(HS), A(PS, 0, 120), A(HS), SUB)
+        tt(A(O1), A(PS, 0, 120), A(AV), LE)
+        ts(A(O2), A(PS, 0, 60), 81.0 * 8192, GE)
+        tt(A(O1, 0, 60), A(O1, 0, 60), A(O2), MAX)
+        tt(A(O1), A(O1), A(JXS[t]), MUL)
+        tt(A(O1), A(O1), A(HS), MAX)
+        ts(A(LS_), A(O1), -1.0, ADD)
 
     def seam(t):
         SCOPE[:] = ["c", 0]
         side = (A(P, 16, 96), A(P, 576, 656))
         buf = lambda nm, w, d: [own("%s%d%d" % (nm, t, e), "sbuf", [128, w], d) for e in range(2)]
         TB, TR, XS, XR = buf("TB", 80, "bfloat16"), buf("TR", 80, "bfloat16"), buf("XS", 480, "uint16"), buf("XR", 480, "uint16")
-        PS, HS, LN_, NMF, O1, RI, LI, LS_ = f(128), f(120), u(120), f(120), f(120), f(120), u(120), u(120)
+        PS, HS, LN_, NMF, RI, LI = f(128), f(120), u(120), f(120), f(120), u(120)
         cp(A(PS), IND(A(TT), A(LSE)))
         ts(A(HS), A(PS, 0, 120), MAGIC, ADD, MAGIC, SUB)
         tt(A(NMF), A(PS, 0, 120), A(HS), SUB)
         ts(A(LN_), A(NMF), -1.0, ADD)
-        XN, n, JX = (XM, XL)[t], 2560 + 512 * t, JXS[t]
-        tt(A(O1), A(PS, 0, 120), A(AV), LE)
-        tt(A(O1), A(O1), A(JX), MUL)
-        tt(A(O1), A(O1), A(NMF), MAX)
-        ts(A(LS_), A(O1), -1.0, ADD)
+        XN, n = XM, 2560 + 512 * t
         ts(A(TB[0]), side[0], 127.0 * 8192, ADD, 208.0 * 8192, MIN)
         ts(A(TB[1]), side[1], (127.0 - 560) * 8192, ADD, 127.5 * 8192, MAX)
         for e in range(2):
@@ -737,17 +801,30 @@ def program():
         own_ = (A(GA, 0, 960), A(GA, 960, 1920))
         for e in range(2):
             cp(own_[e], IND(A(XN, 0, n), A(LN_, 60 * e, 60 * e + 60)), "vs")
-            mm(acc(A(B[6 + e], 0, 480), [(A(ID), A(GA, 960 * e, 960 * e + 480)), (A(I256), A(GA, 960 * e + 480, 960 * e + 960))]))
-            cp(A(XS[e]), A(B[6 + e], 0, 480))
+            bk = A(B[6 - 6 * t + e], 0, 480)
+            mm(acc(bk, [(A(ID), A(GA, 960 * e, 960 * e + 480)), (A(I256), A(GA, 960 * e + 480, 960 * e + 960))]))
+            cp(A(XS[e]), bk)
             send(A(XR[1 - e]), A(XS[e]), 2 * e - 1, 5500)
+        for v0, v1 in ((0, 320), (320, 640)) * t:
+            o = A(B[2], 0, v1 - v0, p=q)
+            mm([(o, A(PERM), A(P, 16 + v0, 16 + v1), True, True)])
+            ts(A(HF, v0, v1, p=q), o, MAGIC, ADD, MAGIC, SUB)
+            lin(A(YN, v0, v1, p=q), A(HF, v0, v1, p=q), U13, -1.0)
+            tt(A(HF, v0, v1, p=q), o, A(HF, v0, v1, p=q), SUB)
+            lin(A(YE, v0, v1, p=q), A(HF, v0, v1, p=q), 1.0, -1.0)
         for e in range(2):
             for k in range(2):
                 s = (960 * e + 480 * k, 960 * e + 480 * k + 480)
-                mm(sum([acc(A(B[4 + k], 80 * l, 80 * l + 80), [(A3(BL, 6 * k + l), A(TB[e])), (A(NID), A(TR[e]))]) for l in range(6)], []))
                 if (t, e, k) in EQS:
+                    mm(sum([acc(A(B[4 + k], 80 * l, 80 * l + 80), [(A3(BL, 6 * k + l), A(TB[e])), (A(NID), A(TR[e]))]) for l in range(6)], []))
                     act(A(B[4 + k], 0, 480), A(B[4 + k], 0, 480), AF.Abs)
                     act(A(LTT, *s), A(B[4 + k], 0, 480), AF.Relu, 1.0, -1.0)
+                elif (t, e, k) in EQT:
+                    mm([(A(B[4 + k], 80 * l, 80 * l + 80), A3(BL, 6 * k + l), A(TB[e]), True, True) for l in range(6)])
+                    for l in range(6):
+                        tt(A(LTT, s[0] + 80 * l, s[0] + 80 * l + 80), A(B[4 + k], 80 * l, 80 * l + 80), A(TR[e]), EQ)
                 else:
+                    mm(sum([acc(A(B[4 + k], 80 * l, 80 * l + 80), [(A3(BL, 6 * k + l), A(TB[e])), (A(NID), A(TR[e]))]) for l in range(6)], []))
                     ts(A(LTT, *s), A(B[4 + k], 0, 480), 0.0, EQ)
             mm(acc(A(B[4], 0, 60), ext(None, ZM, LTT, 60, 960 * e)))
             s = (60 * e, 60 * e + 60)
@@ -758,35 +835,31 @@ def program():
             mn, sg = A(GB, 960 * e, 960 * e + 960), A(LTT, 960 * e, 960 * e + 960)
             cp(A(XI), A(XR[e]))
             ts(A(XW[e], 0, 480), A(XI), 255, AND)
-            ts(A(XW[e], 480, 960), A(XI), 8, SHR)
+            ts(A(XW[e], 480, 960), A(XR[e]), 1 / 256, MUL, -0.5, ADD)
             tt(mn, IND(A(XW[e]), A(LI, 60 * e, 60 * e + 60)), own_[e], MIN)
             for k in range(2):
                 s = (960 * e + 480 * k, 960 * e + 480 * k + 480)
                 mm(acc(A(B[4 + k], 0, 480), [(A(ID), A(GA, *s)), (A(NID), A(GB, *s))]))
                 act(A(LTT, *s), A(B[4 + k], 0, 480), AF.Sign, -0.5)
-            mm(acc(A(B[3], 0, 80), [(Z(ZB, l), A(LTT, 960 * e + 80 * l, 960 * e + 80 * l + 80)) for l in range(12)]))
-            ts(A(KP), A(B[3], 0, 80), 2.0, LT)
-            tt(side[e], side[e], A(KP), MUL)
+            signs = [A(LTT, 960 * e + 80 * l, 960 * e + 80 * l + 80) for l in range(12)]
+            if t == 0:
+                mm(acc(A(B[3], 0, 80), [(Z(ZB, l), signs[l]) for l in range(12)]))
+                ts(A(KP), A(B[3], 0, 80), 2.0, LT)
+                tt(side[e], side[e], A(KP), MUL)
+                tt(A(F, 16 + 560 * e, 96 + 560 * e), A(F, 16 + 560 * e, 96 + 560 * e), A(KP), MUL)
+                continue
+            o = A(B[3 - e], 0, 80, p=q)
+            mm(acc(o, [(A(NID, 0, 96), A(ONE, 0, 80))] + [(A(ZP, 15 - l, 111 - l), signs[l]) for l in range(12)]))
+            ts(o, o, -4096.0, MUL, -1.0, MAX)
+            for y in (YN, YE):
+                tt(A(y, 560 * e, 560 * e + 80, p=q), o, A(y, 560 * e, 560 * e + 80, p=q), MIN)
 
         def store():
-            for c in range(0, 120, 10):
-                cp(IND(A(XN), A(LS_, c, c + 10)), A(GB, 16 * c, 16 * c + 160))
-
-        def last():
-            for c0, c1, e in MAPS:
-                if e == "v":
-                    cp(IND(A(MW, 0, 4032), A(LS_, c0, c1)), A(SD, 16 * c0, 16 * c1))
-                else:
-                    silu(IND(A(WS, 0, 4032), A(LS_, c0, c1)), A(SF, 16 * (c0 - C0), 16 * (c1 - C0)))
-            LF = u(192)
-            for x in range(2):
-                dma(A(MW, 1536 * x, 1536 * x + 1536), A(WS, 1536 * x, 1536 * x + 1536), "g", 4000, True)
-                mm(acc(A(B[6 + x], 0, 96), ext(None, ZZ, MW, 96, 1536 * x)))
-                ts(A(LF, 96 * x, 96 * x + 96), A(B[6 + x], 0, 96), -65.0 * TOP, ADD, 1920.0, MIN)
-            for c0, c1 in OUTS:
-                tt(A(XL, c0, c1), IND(A(GB), A(LF, c0 // 16, c1 // 16)), A(XL, c0, c1), MIN)
-                dma(X("ylen", ALL, slice(c0, c1)), A(XL, c0, c1), "y", 2600 + (c1 - c0) // 2)
-        return last if t else store
+            for c0, c1 in OUTS if t else [(c, c + 512) for c in range(0, n, 512)]:
+                cp(A(XL, c0, c1), IND(A(GB[:2] + (1920 + n,)), A(LF, c0 // 16, c1 // 16)), "vs")
+                if t:
+                    dma(X("ylen", ALL, slice(c0, c1)), A(XL, c0, c1), "y", 2600 + (c1 - c0) // 2)
+        return store
 
     LSE, s1, s2, s3, s4, si, JA, AV, JXS, QC, I256 = u(8), f(8), f(8), f(8), f(8), ii(8), f(120), f(120), [f(120), f(120)], f(1), b(128)
     ts(A(s1), A(J, 0, 8), 60.0, GE)
@@ -803,6 +876,8 @@ def program():
     ts(A(s4), A(si), 656.0, MUL)
     ts(A(s1), A(s1), 560.0, MUL)
     tt(A(s3), A(s3), A(s1), ADD)
+    LS0 = u(8)
+    ts(A(LS0), A(s3), 16.0, ADD)
     tt(A(s3), A(s3), A(s4), ADD)
     cp(A(LSE), A(s3))
     JB = f(120)
@@ -811,41 +886,38 @@ def program():
     for e in range(2):
         lin(A(AV, 60 * e, 60 * e + 60), A(JA, 0, 60), 8192.0, 8192.0 * (560 * e - 958.5))
         for t in range(2):
-            lin(A(JXS[t], 60 * e, 60 * e + 60), A(J, 0, 60), 1.0, 2561.0 + 512 * t)
+            lin(A(JXS[t], 60 * e, 60 * e + 60), A(J, 0, 60), 1.0, 2049.0 + 512 * t)
         fl(A(XW[e], 960, 1040), 255)
     ts(A(QC), PM, -80.0, MUL, 960.0, ADD)
     ts(A(QC), A(QC), 0.0, MAX)
     W["m1"] = A(QC)
     ZM = zt("m1")
     lin(A(I256), A(ID), 256.0, 0.0)
+    SCOPE[0] = None
+    LS_, LF, ZP, G12 = u(120), u(192), b(144), f(1)
+    HF, YE, YN, q = TIN, (TT[0], TT[1], 640), (TT[0], TT[1] + 640, 640), (0, 96)
+    ts(A(G12), PG, 12.0, MUL)
+    ts(A(ZP), A(XZ), A(G12), EQ)
     lg = choose(0)
+    lists(0, lg)
+    places(0)
     contract(0, lg)
     fill(1)
     for c in range(0, 30, 10):
         ts(A(L1, 16 * c, 16 * c + 160), IND(A(TT), A(LSV, c, c + 10)), U13, MUL, 15.0, ADD)
     lg = choose(1)
-    contract(1, lg, seam(0))
-    fill(1)
+    lists(1, lg)
+    store = seam(0)
+    places(1)
+    contract(1, lg, store)
+    middles(1)
     SCOPE[0] = None
     LMID = u(192)
-    ts(A(LMID), A(MID), 16.0 - 17 * TOP, ADD)
+    ts(A(LMID), A(MID), 16.0, ADD)
     for k in range(4):
         cp(A(YM, 768 * k, 768 * k + 768), IND(A(GOT), A(LMID, 48 * k, 48 * k + 48)), "vs")
     dma(X("ymid", ALL, ALL), A(YM, p=(0, 128, 16)), "y")
     seam(1)()
-    HF, YE, YN = TIN, (TT[0], TT[1], 640), (TT[0], TT[1] + 640, 640)
-    q = (0, 96)
-    for bk, v0, v1 in ((0, 80, 560), (1, 0, 80), (2, 560, 640)):
-        o = A(B[bk], 0, v1 - v0, p=q)
-        mm([(o, A(PERM), A(P, 16 + v0, 16 + v1), True, True)])
-        if bk:
-            ts(A(HF, v0, v1, p=q), o, MAGIC, ADD, MAGIC, SUB)
-        else:
-            act(A(YE, v0, v1, p=q), o, AF.Identity, MAGIC)
-            act(A(HF, v0, v1, p=q), A(YE, v0, v1, p=q), AF.Identity, -MAGIC)
-        lin(A(YN, v0, v1, p=q), A(HF, v0, v1, p=q), U13, -1.0)
-        tt(A(HF, v0, v1, p=q), o, A(HF, v0, v1, p=q), SUB)
-        lin(A(YE, v0, v1, p=q), A(HF, v0, v1, p=q), 1.0, -1.0)
     dma(X("ynb", ALL, ALL), A(YN, p=q), "y")
     dma(X("yen", ALL, ALL), A(YE, p=q), "s")
 
@@ -900,39 +972,67 @@ def schedule():
     for k in range(n - 1, -1, -1):
         pri[k] = min(a[2] for a in OPS[k]["alts"]) + OPS[k].get("lat", 0) + SYNC + max([pri[j] for j in succ[k]] + [0])
 
-    def place(pr, bias):
-        busy = dict(v=[], s=[], t=[], g=[], y=[], n=[])
-        done, use, at, left = {}, {}, {}, [len(p) for p in pred]
-        rdy = [k for k in range(n) if not left[k]]
-        while rdy:
-            k = max(rdy, key=lambda q: pr[q])
-            rdy.remove(k)
+    late = [o.get("lat", 0) + SYNC for o in OPS]
+
+    def ranked(pr, first):
+        seen, out = [False] * n, []
+        for k in np.argsort(-pr, kind="stable").tolist():
+            todo = [k]
+            while todo:
+                q = todo[-1]
+                if seen[q]:
+                    todo.pop()
+                    continue
+                wait = [j for j in first[q] if not seen[j]]
+                if wait:
+                    todo.extend(wait)
+                else:
+                    seen[q] = True
+                    out.append(q)
+                    todo.pop()
+        return out
+
+    def place(pr, bias, base=None):
+        order, x = ranked(pr, pred), 0
+        if base:
+            while x < n and order[x] == base[4][x] and bias[order[x]] == base[5][order[x]]:
+                x += 1
+            if x == n:
+                return base
+            x -= x % 64
+        if x:
+            marks = base[6][:x // 64 + 1]
+            busy = {e: list(q) for e, q in marks[-1].items()}
+            done, use, at = list(base[3]), list(base[1]), list(base[2])
+        else:
+            marks, busy = [None], dict(v=[], s=[], t=[], g=[], y=[], n=[])
+            done, use, at = [0.0] * n, [None] * n, [0.0] * n
+        for y in range(x, n):
+            k = order[y]
+            if y > x and y % 64 == 0:
+                marks.append({e: list(q) for e, q in busy.items()})
             best = None
             for a in OPS[k]["alts"]:
-                st = max([done[i] - (SYNC if soft and use[i][0] == a[0] else 0) for i, soft in near[k]] + [0.0])
-                d = a[2] + 20 if a[0] != "n" else 0
-                st, pos = gap(busy[a[0]], st, d)
-                c = st + d + (bias if a[0] == "v" else 0)
+                e, st = a[0], 0.0
+                for i, soft in near[k]:
+                    r = done[i] - SYNC if soft and use[i][0] == e else done[i]
+                    if r > st:
+                        st = r
+                d = a[2] + 20 if e != "n" else 0
+                st, pos = gap(busy[e], st, d)
+                c = st + d + (bias[k] if e == "v" else 0)
                 if best is None or c < best[0]:
                     best = (c, a, st, d, pos)
             c, a, st, d, pos = best
             if d:
                 busy[a[0]].insert(pos, (st, st + d))
-            use[k], at[k], done[k] = a, st, st + a[2] + OPS[k].get("lat", 0) + SYNC
-            for j in succ[k]:
-                left[j] -= 1
-                if not left[j]:
-                    rdy.append(j)
-        return max(done.values()), use, at, done
+            use[k], at[k], done[k] = a, st, st + a[2] + late[k]
+        return max(done), use, at, done, order, bias, marks
 
     def back(got):
         use, done = got[1], got[3]
         busy, end = dict(v=[], s=[], t=[], g=[], y=[], n=[]), [0.0] * n
-        left = [len(q) for q in succ]
-        rdy = [k for k in range(n) if not left[k]]
-        while rdy:
-            k = max(rdy, key=lambda q: done[q])
-            rdy.remove(k)
+        for k in ranked(np.array(done) + np.arange(n) * 1e-6, succ):
             a = use[k]
             lat = OPS[k].get("lat", 0) + SYNC
             st = max([end[j] + (0 if soft and use[j][0] == a[0] else lat) for j, soft in after[k]] + [lat])
@@ -941,41 +1041,81 @@ def schedule():
             if d:
                 busy[a[0]].insert(pos, (st, st + d))
             end[k] = st + d
-            for j in pred[k]:
-                left[j] -= 1
-                if not left[j]:
-                    rdy.append(j)
         return np.array(end)
 
-    pr = np.array(pri)
-    got = best = place(pr, BIAS)
+    pr, bias = np.array(pri), [BIAS] * n
+    both = [k for k in range(n) if len(OPS[k]["alts"]) > 1]
+    for k in both:
+        c = {a[0]: a[2] for a in OPS[k]["alts"]}
+        bias[k] = BIAS + THRIFT * (c["v"] - c["s"]) if "s" in c else SPARE
+    got = best = place(pr, bias)
     for it in range(TURNS):
         p2 = back(got)
-        got = place(p2, BIAS)
+        got = place(p2, bias)
         if got[0] < best[0]:
             best, pr = got, p2
-    now = best
+
+    def held(got):
+        use, at, done = got[1], got[2], got[3]
+        last, before, out = {}, [None] * n, []
+        for k in sorted(range(n), key=lambda q: at[q]):
+            before[k], last[use[k][0]] = last.get(use[k][0]), k
+        k = max(range(n), key=lambda q: done[q])
+        while k is not None:
+            j = max(pred[k], key=lambda q: done[q]) if pred[k] else None
+            p = before[k] if use[k][0] != "n" else None
+            if p is not None and (j is None or at[p] + use[p][2] + 21 > done[j]) and p != j:
+                out.append((k, p))
+                j = p
+            k = j
+        return out
+
     rng = np.random.RandomState(SEARCH[1])
-    for it in range(SEARCH[0]):
-        a = int(rng.randint(0, n))
-        b, d = a + int(rng.choice([1, 3, 10, 30, 80])), int(rng.choice([-1, 1]) * rng.choice([300, 1000, 3000, 10000, 30000]))
-        p2 = pr.copy()
-        p2[a:b] += d
-        got = place(p2, BIAS)
-        if got[0] < now[0] + 1500 and it % 4 == 0:
-            p3 = back(got)
-            g3 = place(p3, BIAS)
-            if g3[0] < got[0]:
-                got, p2 = g3, p3
-        if got[0] < now[0] + 150 * (1 - it / SEARCH[0]):
-            now, pr = got, p2
-            if got[0] < best[0]:
-                best = got
+    pick = lambda q: q[int(rng.randint(0, len(q)))]
+
+    def walk(pr, bias, steps):
+        now, pairs = place(pr, bias), None
+        best = (now, pr)
+        for it in range(steps):
+            p2, b2 = pr, bias
+            if it % 6 in (1, 3, 4):
+                pairs = pairs if pairs and pairs[0] is now else (now, held(now))
+                k, j = pick(pairs[1])
+                p2, d = pr.copy(), pick([0, 300, 1000, 3000])
+                if len(OPS[j]["alts"]) > 1 and rng.rand() < 0.3:
+                    b2 = list(bias)
+                    b2[j] = -3000 if now[1][j][0] != "v" else 3000
+                elif rng.rand() < 0.5:
+                    p2[k] = max(p2[k], p2[j]) + 1 + d
+                else:
+                    p2[j] = min(p2[k], p2[j]) - 1 - d
+            elif it % 6 == 2:
+                a, b2 = int(rng.randint(0, len(both))), list(bias)
+                for k in both[a:a + pick([1, 1, 2, 4])]:
+                    b2[k] = -3000 if now[1][k][0] != "v" else 3000
+            else:
+                a, p2 = int(rng.randint(0, n)), pr.copy()
+                p2[a:a + pick([1, 3, 10, 30, 80])] += pick([-1, 1]) * pick([300, 1000, 3000, 10000, 30000])
+            got = place(p2, b2, now)
+            if got is not now and got[0] < now[0] + 1500 and it % BACK == 0:
+                p3 = back(got)
+                g3 = place(p3, b2)
+                if g3[0] < got[0]:
+                    got, p2 = g3, p3
+            if got[0] < now[0] + HEAT * (1 - it / steps):
+                now, pr, bias = got, p2, b2
+                if got[0] < best[0][0]:
+                    best = (got, p2)
+        return best
+
+    best, pr = min([walk(pr, bias, SEARCH[3]) for k in range(STARTS)], key=lambda q: q[0][0])
+    best, pr = walk(pr, best[5], SEARCH[0])
+    kept = best[5]
 
     def weigh(got):
         use, total = got[1], 0.0
         order = sorted(range(n), key=lambda k: (got[2][k], k))
-        for sc, ga, sync, pe, far, unit in RANGES:
+        for sc, ga, sync, pe, far, dm, unit in RANGES:
             free, done = dict(v=0.0, s=0.0, t=0.0, g=0.0, y=0.0, n=0.0), [0.0] * n
             for k in order:
                 o, e, c = OPS[k], use[k][0], use[k][2]
@@ -987,7 +1127,7 @@ def schedule():
                         st = r
                 if e != "n":
                     free[e] = st + c + 20
-                done[k] = st + c + o.get("lat", 0) * (far if "send" in o else 1) + sync
+                done[k] = st + c + o.get("lat", 0) * (far if "send" in o else dm) + sync
             total += max(done) / unit
         return total
 
@@ -997,8 +1137,8 @@ def schedule():
         a = int(rng.randint(0, n))
         p2 = pr.copy()
         p2[a:a + int(rng.choice([1, 3, 10, 30]))] += int(rng.choice([-1, 1]) * rng.choice([300, 1000, 3000, 10000]))
-        got = place(p2, BIAS)
-        if got[0] < best[0] + 2500:
+        got = place(p2, kept, best)
+        if got is not best and got[0] < best[0] + 2500:
             m = weigh(got)
             if m < mark:
                 best, pr, mark = got, p2, m
@@ -1007,8 +1147,13 @@ def schedule():
     return sorted(range(n), key=lambda k: (best[2][k], k)), best[0]
 
 
-SYNC, BIAS, TURNS, SEARCH = 120.0, 500.0, 30, [2000, 2, 2600]
-RANGES = [(1.0, 1.0, 120, 1.0, 1.0, 195.0), (1.4, 1.3, 120, 1.0, 1.0, 235.0), (0.45, 0.75, 120, 1.0, 1.8, 180.0), (1.0, 1.0, 250, 1.3, 1.4, 235.0)]
+THRIFT = 3.0
+HEAT = 300.0
+BACK = 3
+STARTS = 4
+SPARE = 3000.0
+SYNC, BIAS, TURNS, SEARCH = 120.0, 500.0, 30, [3500, 2, 1200, 2000]
+RANGES = [(1.0, 1.0, 120, 1.0, 1.0, 1.0, 165.0), (1.4, 1.3, 120, 1.0, 1.0, 1.0, 200.0), (0.45, 0.75, 120, 1.0, 1.8, 1.6, 155.0), (1.0, 1.0, 250, 1.3, 1.4, 1.4, 200.0)]
 
 program()
 ORDER, SPAN = schedule()

import numpy as np
from concourse.mybir import dt, AluOpType, AxisListType, ActivationFunctionType

AL = AluOpType
AF = ActivationFunctionType
ADD, SUB, MUL, MAX, MIN = AL.add, AL.subtract, AL.mult, AL.max, AL.min
GE, GT, LE, LT, EQ, NE = AL.is_ge, AL.is_gt, AL.is_le, AL.is_lt, AL.is_equal, AL.not_equal
AND, SHR = AL.bitwise_and, AL.arith_shift_right
MAGIC = 1.5 * 2.0 ** 36
U13 = 2.0 ** -13
ALL = slice(None)

SHAPES = {}
POOL = {"f": ["float32", 0, 4], "b": ["bfloat16", 0, 2], "h": ["float16", 0, 2], "i": ["int32", 0, 4], "u": ["uint16", 0, 2]}
OPS = []
SEMS = ["ev", "es", "et", "eg"]


SCOPE, SEEN, DBG = [None, 0], {}, {}


def al(kind, n):
    if SCOPE[0] is not None:
        key = (SCOPE[0], SCOPE[1])
        SCOPE[1] += 1
        if key not in SEEN:
            SCOPE[0] = None
            SEEN[key] = al(kind, n)
            SCOPE[0] = key[0]
        return SEEN[key]
    p = POOL[kind]
    o = p[1]
    p[1] = o + (n + 15) // 16 * 16
    return ("p" + kind, o, n)


def own(name, where, shape, dtype):
    SHAPES[name] = (where, shape, dtype)
    return name


def A(b, lo=0, hi=None, st=1, p=None):
    if isinstance(b, str):
        b = (b, 0, SHAPES[b][1][1])
    hi = b[2] if hi is None else hi
    n = (hi - lo + st - 1) // st
    rows = ALL if p is None else slice(*p)
    return (b[0], (rows, slice(b[1] + lo, b[1] + lo + (n - 1) * st + 1, st)), b[1] + lo, b[1] + lo + (n - 1) * st, n, None)


def A3(name, s1=ALL, s2=ALL):
    sh = SHAPES[name][1]
    ix = np.arange(sh[1] * sh[2]).reshape(sh[1], sh[2])[s1, s2]
    return (name, (ALL, s1, s2), int(ix.min()), int(ix.max()), int(ix.size), None)


def IND(win, off):
    return win[:4] + (16 * off[4], off)


def X(name, *ix):
    return (name, ix, 0, 1 << 30, 0, None)


def real(T, ap):
    if not isinstance(ap, tuple):
        return ap
    r = T[ap[0]][ap[1]]
    return r if ap[5] is None else r.indirect(real(T, ap[5]))


def two(ap):
    return ap[0] in ("pb", "ph", "pu") or (ap[0] in SHAPES and SHAPES[ap[0]][2] in ("bfloat16", "float16", "uint16"))


def flt(ap):
    return ap[0] in ("pf", "pb") or (ap[0] in SHAPES and SHAPES[ap[0]][2] in ("bfloat16", "float32"))


def psum(ap):
    return ap[0] in SHAPES and SHAPES[ap[0]][0] == "psum"


def reg(ap):
    st = ap[1][1].step if len(ap[1]) == 2 and isinstance(ap[1][1], slice) and ap[1][1].step else 1
    return ap[0:1] + ap[2:4] + (st, sum(1 << p for p in range(128)[ap[1][0]]))


def op(alts, outs, ins, **kw):
    rd, wr = [], []
    for ap in ins:
        if isinstance(ap, tuple):
            rd.append(reg(ap))
            if ap[5] is not None:
                rd.append(reg(ap[5]))
    for ap in outs:
        wr.append(reg(ap))
        if ap[5] is not None:
            rd.append(reg(ap[5]))
    OPS.append(dict(alts=alts, rd=rd, wr=wr, sc=any(ap[5] is not None for ap in outs), ga=any(isinstance(ap, tuple) and ap[5] is not None for ap in ins), **kw))


def vcost(out, ins, tt=False):
    n = out[4]
    if out[5] is not None:
        return 60 + 4.2 * n
    if ins[0][5] is not None:
        return 60 + 1.5 * n
    if tt:
        return max(64, n * (1 if psum(ins[0]) or psum(ins[1]) else 2))
    return max(64, n * (0.5 if two(out) and two(ins[0]) else 1))


def ts(out, in0, s1, o0, s2=None, o1=None):
    def f(g, T):
        if o1 is None:
            return g.vector.tensor_scalar(real(T, out), real(T, in0), real(T, s1), None, o0)
        return g.vector.tensor_scalar(real(T, out), real(T, in0), real(T, s1), real(T, s2), o0, o1)
    alts = [("v", f, vcost(out, [in0]))]
    if flt(out) and flt(in0) and not any(isinstance(s, tuple) and psum(s) for s in (s1, s2)):
        if o1 is None and o0 in (MUL, ADD):
            alts.append(act_alt(out, in0, AF.Identity, s1 if o0 == ADD else 0.0, s1 if o0 == MUL else 1.0, None))
        elif o0 == MUL and o1 == ADD:
            alts.append(act_alt(out, in0, AF.Identity, s2, s1, None))
    op(alts, [out], [in0, s1, s2])


def tt(out, in0, in1, o):
    op([("v", lambda g, T: g.vector.tensor_tensor(real(T, out), real(T, in0), real(T, in1), o), vcost(out, [in0, in1], True))], [out], [in0, in1])


def act_alt(out, in_, func, bias, scale, acc):
    def f(g, T):
        if acc is None:
            return g.scalar.activation(real(T, out), real(T, in_), func, bias=real(T, bias), scale=real(T, scale))
        return g.scalar.activation(real(T, out), real(T, in_), func, bias=real(T, bias), scale=real(T, scale), accum_out=real(T, acc))
    return ("s", f, 80 + 1.5 * out[4] if in_[5] is not None else max(64, out[4]) + 30)


def act(out, in_, func=None, bias=0.0, scale=1.0, acc=None):
    op([act_alt(out, in_, func or AF.Identity, bias, scale, acc)], [out] + ([acc] if acc else []), [in_, bias, scale])


def cp(out, in_, on="v"):
    alts = []
    if "v" in on:
        alts.append(("v", lambda g, T: g.vector.tensor_copy(real(T, out), real(T, in_)), vcost(out, [in_])))
    if flt(out) and flt(in_) and out[5] is None:
        alts.append(act_alt(out, in_, AF.Copy, 0.0, 1.0, None))
    op(alts, [out], [in_])


def lin(out, in_, scale, bias, on="vs"):
    alts = []
    if "v" in on:
        alts.append(("v", lambda g, T: g.vector.tensor_scalar(real(T, out), real(T, in_), real(T, scale), real(T, bias), MUL, ADD), vcost(out, [in_])))
    if flt(out) and flt(in_):
        alts.append(act_alt(out, in_, AF.Identity, bias, scale, None))
    op(alts, [out], [in_, scale, bias])


def ms(out, c):
    op([("v", lambda g, T: g.vector.memset(real(T, out), c), max(40, out[4] * (0.5 if two(out) else 1)))], [out], [])


def scan(out, d0, d1, o0, o1, first=0.0):
    op([("v", lambda g, T: g.vector.tensor_tensor_scan(real(T, out), real(T, d0), real(T, d1), first, o0, o1), vcost(out, [d1]))], [out], [d0, d1])


def tr(out, in_):
    op([("v", lambda g, T: g.vector.transpose(real(T, out), real(T, in_)), vcost(out, [in_]))], [out], [in_])


def mm(parts):
    if len(parts) >= 8 and sum(max(64, q[2][4]) * (1 if two(q[2]) else 4) for q in parts) > 2200:
        mm(parts[:len(parts) // 2])
        mm(parts[len(parts) // 2:])
        return

    def f(g, T):
        r = None
        for o, l, x, s, e in parts:
            r = g.tensor.matmul(real(T, o), real(T, l), real(T, x), s, e)
        return r
    c = sum(max(64, x[4]) * (1 if two(x) else 4) * PEC for o, l, x, s, e in parts)
    op([("t", f, c + 60)], [q[0] for q in parts], [q[1] for q in parts] + [q[2] for q in parts])


def acc(out, pairs):
    return [(out, l, x, i == 0, i == len(pairs) - 1) for i, (l, x) in enumerate(pairs)]


def iota(out, pat, base, cm=0):
    def f(g, T):
        if out[0] == "pi" or SHAPES.get(out[0], "  i")[2] == "int32":
            return g.iota(real(T, out), pat, base, cm)
        return g.iota(real(T, out), pat, base, cm, allow_small_or_imprecise_dtypes=True)
    op([("g", f, 160 + 2 * out[4])], [out], [])


def asel(out, cmp, fill, base, cm, pat=None, in_=None):
    in_ = in_ or out
    op([("g", lambda g, T: g.affine_select(real(T, out), real(T, in_), pat or [[0, 1]], cmp, fill, base, cm), 205 + 2 * out[4])], [out], [in_])


def silu(out, in_, once=0):
    op([("s", lambda g, T: g.scalar.activation(real(T, out), real(T, in_), AF.Silu), 80 + 4.2 * out[4] + once)], [out], [in_])


def dma(out, in_, q="y", lat=2600, add=False):
    s = "d%d" % len(SEMS)
    SEMS.append(s)

    def f(g, T):
        if add:
            return g.dma_start(real(T, out), real(T, in_), accum_op=ADD)
        e = g.sync if q == "y" else g.scalar if q == "s" else g
        return e.dma_start(real(T, out), real(T, in_))
    op([(q, f, 1200 if q == "g" else 100)], [out], [in_] + [out] * add, sem=s, inc=16, lat=lat)
    OPS[-1]["wr"] = [(r[0], r[1] // 8 * 8, r[2] // 8 * 8 + 7) + r[3:] for r in OPS[-1]["wr"]]


def dmas(pairs, lat):
    s = "d%d" % len(SEMS)
    SEMS.append(s)
    op([("y", [(lambda g, T, o=o, i=i: g.sync.dma_start(real(T, o), real(T, i))) for o, i in pairs], 100 * len(pairs))],
       [o for o, i in pairs], [i for o, i in pairs], sem=s, inc=16 * len(pairs), lat=lat)
    OPS[-1]["wr"] = [(r[0], r[1] // 8 * 8, r[2] // 8 * 8 + 7) + r[3:] for r in OPS[-1]["wr"]]


def send(dst, src, step, lat):
    k = len(SEMS)
    SEMS.extend(["l%d" % k, "r%d" % k])
    op([("g", None, 600)], [], [src], sem="l%d" % k, send=(dst, src, step, "r%d" % k), lat=lat)
    op([("n", None, 0)], [dst], [], sem="r%d" % k, step=step, after=len(OPS) - 1, lat=0)


PEC = 0.6
CV = [100, 100]
MAPC = 20
C0 = min(CV + [78])
XNC = 512
PSC = 12
MKV = [0]
OUTS = [(0, 1024), (1024, 2048), (2048, 2560), (2560, 3072)]
LOW = 65
TOP = LOW + 16
EQS = []
EQT = [(1, 0, 0), (1, 0, 1), (1, 1, 0), (1, 1, 1)]
CLAMP = [(0, 21), (21, 45), (45, 66)]


def program():
    f, b, h, ii, u = (lambda n: al("f", n)), (lambda n: al("b", n)), (lambda n: al("h", n)), (lambda n: al("i", n)), (lambda n: al("u", n))
    B = [own("B%d" % k, "psum", [128, 512], "float32") for k in range(8)]
    WS = f(5760 + 16 * (198 - min(CV)))
    YM, CC = (WS[0], WS[1], 3072), h(3168)
    BL = own("BL", "sbuf", [128, 12, 128], "bfloat16")
    L1, R2 = u(480), f(128)
    XL = own("XL", "sbuf", [128, 3072], "bfloat16")
    SD = b(16 * max(CV) + 4992)
    GB, XM, SF = (SD[0], SD[1] + 16 * max(CV), 1920), (SD[0], SD[1] + 16 * max(CV) + 1920, 3072), f(16 * (198 - C0))
    XW = [ii(1040), ii(1040)]
    EN, NB = XW[0][:2] + (480,), (XW[0][0], XW[0][1] + 480, 480)
    UW = own("UW", "sbuf", [128, 8192], "bfloat16")
    MW = own("MW", "sbuf", [128, max(7168, 5760 + 16 * max(CV))], "bfloat16")
    col = lambda t, k: A(t, k, k + 1)
    Z = lambda z, t: A(z, 15 - t, 143 - t)

    def ext(out, z, src, n, lo=0):
        return [(Z(z, i), A(src, lo + i, lo + 16 * n, 16)) for i in range(16)]

    dma(A(NB), X("nb", ALL, ALL), "y")
    dma(A(EN), X("en", ALL, ALL), "s")
    dma(A(XL, 0, 2048), X("lens", ALL, ALL), "y", 4000)
    PI, PJ = ii(4), f(8)
    iota(col(PI, 0), [[0, 1]], 0, 1)
    X16, XG, XZ = f(128), f(128), f(144)
    iota(A(X16), [[0, 8], [1, 16]], 0)
    iota(A(XZ), [[1, 144]], -15)
    iota(A(XG), [[1, 8], [0, 16]], 0)
    J, JH = f(208), f(64)
    iota(A(J), [[16, 208]], 0)
    ts(col(PI, 1), col(PI, 0), 15, AND)
    ts(col(PI, 2), col(PI, 0), 4, SHR)
    ts(col(PI, 3), col(PI, 2), 1, AND)
    cp(A(PJ, 0, 4), A(PI))
    PM, PG, PH, G16 = col(PJ, 1), col(PJ, 2), col(PJ, 3), col(PJ, 4)
    ts(G16, PG, 16.0, MUL)
    ts(A(J), A(J), PM, ADD)
    lin(A(JH), A(J, 0, 64), 1.0, 0.5, "v")
    OH, ZB, BD, ID = f(128), b(144), b(128), b(128)
    ts(A(OH), A(X16), PM, EQ)
    ts(A(ZB), A(XZ), G16, EQ)
    ts(A(BD), A(XG), PG, EQ)
    ts(A(ID), A(XZ, 15, 143), col(PJ, 0), EQ)
    early = [("key", [1024] * 12 + [128, 32, 1, -229376]), ("fs", [1] * 13 + [U13, 1, 1]), ("fc", [1] * 12 + [4096] * 4),
             ("pd", [0] * 12 + [1920, 22 * 8192 + 3072, 0, 1]), ("fd", [0] * 12 + [1920, 22.375, 0, 1]),
             ("dg", [1] * 12 + [1 / 128, 0, 0, -13])]
    late = [("vb", {13: 2048, 14: 64, 15: -688}), ("wu", {13: 32, 14: 1}), ("wa", {0: 1, 1: 16, 2: 48}),
            ("wb", {0: 1, 1: 16, 3: 48}), ("sa", {1: 16, 2: 48, 3: 1}), ("sb", {1: 16, 2: 1, 3: 48}),
            ("upd", {12: 1, 13: 262144, 14: 8192, 15: 32}), ("zz", {0: 1, 1: 16, 4: 48}), ("zd", {0: 1, 1: 16, 5: 48})]
    W16, WC, W = f(32), f(48), {}
    for k, (n, w) in enumerate(early):
        for r in range(16, 0, -1):
            if r == 16 or w[r - 1] != w[r]:
                ms(A(W16, k, k + 1, p=(0, r)), float(w[r - 1]))
        W[n] = col(WC, k)
    mm([(A(B[2], 0, 6), A(OH, p=(0, 16)), A(W16, 0, 6, p=(0, 16)), True, True)])
    cp(A(WC, 0, 6), A(B[2], 0, 6))
    ms(A(W16, 8, 17, p=(0, 16)), 0.0)
    for e in range(4):
        for k, (n, w) in enumerate(late):
            if e < len(w):
                r = sorted(w)[e]
                asel(A(W16, 8 + k, 9 + k, p=(0, 16)), NE, float(w[r]), -r, 1)
            W[n] = col(WC, 8 + k)
    mm([(A(B[5], 0, 9), A(OH, p=(0, 16)), A(W16, 8, 17, p=(0, 16)), True, True)])
    cp(A(WC, 8, 17), A(B[5], 0, 9))
    for k, (n, o, v, w) in enumerate([("s01", LT, 2, 1), ("o14", LT, 14, 128), ("w640", LT, 12, -320), ("l12", LT, 12, 1), ("cm", GE, 12, 1),
                                      ("cx", EQ, 12, 1920), ("ps", GE, 13, 1), ("n15", LT, 15, 1), ("mh", LT, 12, -0.5), ("p0", GE, 1, 1),
                                      ("m2", LT, 12, -2), ("k16", LT, 12, 16)]):
        W[n] = col(WC, 20 + k)
        ts(W[n], PM, float(v), o, float(w), MUL)
    W["uba"], W["z14"] = col(WC, 32), col(WC, 34)
    ts(W["uba"], W["vb"], W["n15"], MUL)
    ts(W["z14"], col(OH, 15), 553 / 16, MUL, W["o14"], ADD)

    def zt(n, kind="b"):
        z = al(kind, 144)
        lin(A(z), A(ZB), W[n], 0.0, "v" if kind == "h" else "vs")
        return z

    def bt(n, src=BD):
        z = b(128)
        lin(A(z), A(src), W[n], 0.0)
        return A(z)
    ZKEY = zt("key")
    BKEY, BDG, BS01, BVB, BGOT, PAS = bt("key"), bt("dg"), bt("s01"), bt("vb"), None, bt("ps", ID)
    Z14, ZL12, ZA, ZBB, ZSA, ZSB, Z640, ZU, ZUP = zt("z14", "h"), zt("l12"), zt("wa"), zt("wb"), zt("sa"), zt("sb"), zt("w640"), zt("wu"), zt("upd")
    ZZ, ZQ, ZM2 = zt("zz"), zt("zd"), zt("m2")
    ZT, ONE = b(1024), b(512)
    ms(A(ZT), 0.0)
    for i in range(0, 12, 4):
        dma(A3(BL, slice(i, i + 4)), A(ZT, 0, 512))
        asel(A3(BL, slice(i, i + 4)), NE, 1.0, -i, 1, [[-1, 4], [-16, 8], [0, 16]])
    PERM, pc = f(96), f(2)
    ts(col(pc, 0), PG, -4.0, MUL, col(PJ, 0), ADD)
    ts(col(pc, 1), W["cx"], col(pc, 0), ADD)
    ts(col(pc, 0), W["ps"], 1920.0, MUL, col(pc, 1), ADD)
    ts(A(PERM), A(XZ, 15, 111), col(pc, 0), EQ)
    NPM = f(2)
    ts(col(NPM, 0), PM, -1.0, MUL, -float(TOP), ADD)
    ts(col(NPM, 1), PM, float(TOP), ADD)
    TS, SFH, SFF, NBD, UBM, t1, t2, t3 = b(128), b(128), b(128), b(128), b(128), b(128), f(128), f(1)
    asel(A(TS), GT, 0.0, 0, -1, [[1, 128]], A(BD))
    asel(A(SFH), GT, 0.0, 0, 1, [[-1, 128]], bt("mh"))
    ts(A(t3), col(OH, 15), 1.5, MUL)
    ts(A(t1), A(X16), 11.0, MIN, -11.0, ADD)
    ts(A(t1), A(t1), A(t3), MUL)
    tt(A(t1), A(t1), A(BD), MUL)
    tt(A(t1), A(t1), PAS, ADD)
    ts(A(SFF), A(SFH), -2.0, MUL)
    tt(A(SFF), A(SFF), A(t1), ADD)
    lin(A(NBD), A(BD), -1.0, 0.0)

    def fl(out, c):
        iota(out, [[0, out[4]]], c)
        ms(out, c if out[0] == "pi" else float(c))
        OPS[-2]["alts"] += OPS.pop()["alts"]
    fl(A(R2), -688)
    fl(A(R2, 12, 128, 16), -716 * 64)
    fl(A(R2, 13, 128, 16), 1424)
    fl(A(R2, 15, 128, 16), 32)
    t4, t5 = f(128), f(128)
    ts(A(t2), A(X16), 13.0, LT, W["uba"], MUL)
    lin(A(t4), A(R2), col(OH, 15), 0.0)
    tt(A(t5), A(t2), A(t4), ADD)
    tt(A(UBM), A(t5), A(BD), MUL)
    fl(A(ONE), 1)
    MB, MF, NID = b(512), f(512), b(128)
    op([("s", act_alt(A(MB), A(ZT, 0, 512), AF.Silu, float(LOW), 1.0, None)[1], 2110)], [A(MB)], [A(ZT, 0, 512)])
    fl(A(MF), LOW)
    lin(A(NID), A(ID), -1.0, 0.0)
    P, F, W2, Y, PFU, ST, WW = f(1280), b(1280), b(656), b(576), b(656), b(592), b(256)
    lin(A(P, 0, 16), A(ZT, 0, 16), 1.0, W["pd"])
    lin(A(F, 0, 16), A(ZT, 0, 16), 1.0, W["fd"])
    for t, w in ((P, "pd"), (F, "fd")):
        lin(A(t, 656, 760), A(ZT, 0, 104), 1.0, W[w])
        dmas([(A(t, c, c + 104), A(t, 656, 760)) for c in range(760, 1280, 104)], 3000)
    ms(A(W2, 0, 16), 0.0)
    ms(A(PFU, 576, 656), 0.0)
    ms(A(ST, 576, 592), 0.0)
    GR, LGT, gi, gc_, gf = f(96), u(4), ii(3), f(3), f(3)
    ms(A(GR), 0.0)
    ts(A(gi), A(J, 0, 3), 1 / 3, MUL, -1 / 3, ADD)
    ts(A(gc_), A(gi), -3.0, MUL)
    tt(A(gc_), A(gc_), A(J, 0, 3), ADD)
    ts(A(gf), A(gc_), 16.0, MUL)
    tt(A(gf), A(gf), A(gi), ADD)
    ts(A(gi), A(gc_), PH, ADD)
    ts(A(gi), A(gi), 1, AND)
    ts(A(gc_), A(gi), 80.0, MUL)
    tt(A(gf), A(gf), A(gc_), ADD)
    cp(A(LGT, 0, 3), A(gf))
    ms(A(WW, 192, 256), 0.0)

    def clear():
        dmas([(A(UW, 960 * k, 960 * (k + 1)), A(ZT, 0, 960)) for k in range(8)], 5000)

    def fill(t):
        dmas([(A(MW, 512 * k, 512 * (k + 1)), A(MB)) for k in range(5 + t)], 4000)
        dmas([(A(WS, 512 * k, 512 * (k + 1)), A(MF)) for k in range(5 + t)], 5000)
    fill(0)
    CI, CE, CF, LVS = ii(40), ii(40), f(40), u(40)
    iota(A(CI), [[1, 40]], 0)
    ts(A(CE), A(CI), PH, ADD)
    ts(A(CE), A(CE), 1, AND)
    ts(A(CF), A(CE), 656.0, MUL)
    tt(A(CF), A(CF), A(J, 0, 40), ADD)
    cp(A(LVS), A(CF))
    KI, KC, KE, KF, LSV = ii(30), f(30), ii(30), f(30), u(30)
    ts(A(KI), A(J, 0, 30), 1 / 40, MUL, -0.4875, ADD)
    ts(A(KC), A(KI), -40.0, MUL)
    tt(A(KC), A(KC), A(J, 0, 30), ADD)
    ts(A(KE), A(KC), PH, ADD)
    ts(A(KE), A(KE), 1, AND)
    ts(A(KF), A(KE), 41.0, MUL)
    tt(A(KF), A(KF), A(KC), ADD)
    ts(A(KF), A(KF), 16.0, MUL)
    tt(A(KF), A(KF), A(KI), ADD)
    cp(A(LSV), A(KF))
    TIN, TT, NX, VI, VH = f(672), f(1312), f(480), ii(40), ii(40)
    XI_, XT = b(672), b(1312)
    cp(A(VI), A(J, 0, 40))
    ts(A(VH), A(VI), 5, SHR)
    ts(A(VI), A(VI), 31, AND)
    for t, put in ((XI_, lambda o, c: ms(o, float(c))), (TIN, fl)):
        put(A(t, 0, 16), 0)
        put(A(t, 656, 672), 0)
        put(A(t, 28, 28 + 80, 16), 1920)
        put(A(t, 28 + 80, 28 + 560, 16), 1792)
        put(A(t, 28 + 560, 656, 16), 1920)
        put(A(t, 31, 656, 16), 1)
        cp(A(t, 30, 656, 16), A(VI))
    ts(A(XI_, 29, 656, 16), A(VH), 0.375, ADD)
    ts(A(TIN, 29, 656, 16), A(VH), 8192.0, MUL, 3072.0, ADD)
    for k in range(12):
        ts(A(XI_, 16 + k, 656, 16), A(NB, 40 * k, 40 * k + 40), 0.0, GE)

    def turn(out):
        tr(A(XT, 0, 640), A(XI_, 16, 656))
        tr(A(XT, 640, 1312), A(XI_))
        for c in (0, 20):
            cp(A(out, 16 + 16 * c, 336 + 16 * c), IND(A(XT), A(LVS, c, c + 20)), "vs")
    turn(F)
    ts(A(L1), A(NB), 16.0, ADD)
    lin(A(NX), A(NB), 8192.0, 8193.0, "v")
    for k in range(12):
        tt(A(TIN, 16 + k, 656, 16), A(NX, 40 * k, 40 * k + 40), A(EN, 40 * k, 40 * k + 40), ADD)
    tr(A(TT, 0, 640), A(TIN, 16, 656))
    tr(A(TT, 640, 1312), A(TIN))
    cp(A(P, 16, 656), IND(A(TT), A(LVS)), "vs")
    lex = [0]
    for j in range(11):
        lex.append(lex[-1] + 11 - j)
    row = lambda t, r, *s: A(t, *s, p=(r, 128, 16))
    LT2 = b(2560)
    part = lambda o, n: (LT2[0], LT2[1] + o, n)
    DG, DC, DJ, DQ, OI = b(208), part(0, 208), part(208, 208), part(416, 208), f(16)
    for j in range(11):
        iota(A(DG, 3 * lex[j], 3 * lex[j + 1]), [[1, 11 - j], [0, 3]], 17 + j)
        fl(A(DJ, 3 * lex[j], 3 * lex[j + 1]), 16 + j)
    fl(A(DG, 198, 208), LOW)
    iota(A(DC, 0, 198), [[0, 66], [1, 3]], 16)
    iota(A(DQ, 0, 198), [[1, 66], [0, 3]], 16)
    D1, D2, D3 = part(624, 198), part(832, 198), part(1040, 198)
    mm(acc(A(B[5], 0, 198), [(A(ID), A(DG, 0, 198)), (A(NID), A(DJ, 0, 198))]))
    lin(A(D1), A(B[5], 0, 198), -0.5, 12.0)
    lin(A(D2), A(B[5], 0, 198), 1.0, -1.0)
    tt(A(D1), A(D1), A(D2), MUL)
    mm(acc(A(B[5], 0, 198), [(A(ID), A(D1)), (A(ID), A(DJ, 0, 198))]))
    cp(A(D3), A(B[5], 0, 198), "vs")
    dmas([(row(DG, r, 0, 198), row(t, r, 0, 198)) for r, t in ((1, DC), (2, DJ), (4, DQ), (5, D3))], 2600)
    LUP, LDN, LSQ = u(14), u(14), u(36)
    mm(acc(A(B[5], 0, 13), ext(None, ZSA, DG, 13)) + acc(A(B[5], 16, 29), ext(None, ZSB, DG, 13)))
    ts(A(LUP, 0, 13), A(B[5], 0, 13), 1.0 - 16 * 65, ADD, 591.0, MIN)
    ts(A(LDN, 0, 13), A(B[5], 16, 29), 1.0 - 16 * 65, ADD, 591.0, MIN)
    QJ, QC3, QE, q1, q2, q3, qk = f(36), f(36), f(36), f(36), f(36), f(36), f(4)
    iota(A(QJ), [[1, 12], [0, 3]], 0)
    iota(A(QC3), [[0, 12], [1, 3]], -3)
    iota(A(QE), [[1, 36]], -3)
    ts(col(qk, 0), PM, -1.0, ADD)
    ts(col(qk, 1), col(qk, 0), -1.5, MUL, 31.5, ADD)
    ts(col(qk, 1), col(qk, 1), col(qk, 0), MUL)
    ts(col(qk, 1), col(OH, 0), 236.0, MUL, col(qk, 1), ADD)
    ts(col(qk, 2), col(qk, 0), 3.0, MUL)
    ts(A(q1), A(QJ), -1.5, MUL, 31.5, ADD)
    tt(A(q1), A(q1), A(QJ), MUL)
    tt(A(q1), A(q1), A(QC3), ADD)
    ts(A(q1), A(q1), col(qk, 2), ADD)
    ts(A(q2), A(QJ), col(qk, 0), LT)
    tt(A(q1), A(q1), A(q2), MUL)
    ts(A(q2), A(QE), col(qk, 1), ADD)
    ts(A(q3), A(QJ), col(qk, 0), GT)
    tt(A(q2), A(q2), A(q3), MUL)
    ts(A(q3), A(QJ), col(qk, 0), EQ, 198.0, MUL)
    tt(A(q1), A(q1), A(q2), ADD)
    tt(A(q1), A(q1), A(q3), ADD)
    cp(A(LSQ), A(q1))
    ts(A(OI), A(X16, 0, 16), 16.0, ADD, col(OH, 0), MUL)
    for i in range(16):
        lin(A(SD, i, 3168, 16), A(DG, 0, 198), W["p0"], col(OI, i))
    dma(A(SF), A(SD, 16 * C0, 3168), "g", 4000)
    RS1 = b(576)
    fl(A(RS1), 1)
    fl(A(RS1, 0, 576, 16), 0)
    N1, N2, NM = part(1248, 512), part(1760, 512), [b(512), b(512)]
    fl(A(N1), -11)
    for t in range(2):
        iota(A(NM[t]), [[0, 16], [1, 32]], 1)
        iota(A(N2), [[1, 16], [0, 32]], 63 + 16 * t)
        for r, s in ((13, ZT), (14, N1), (15, N2)):
            dma(row(NM[t], r), row(s, r, 0, 512))
    JG, JU, JM, JQ = f(3), f(36), [f(198), f(198)], f(32)
    for t, n, m, c in ((JG, 3, 1.0, 656.0), (JU, 36, 8192.0, 641.0 * 8192), (JQ, 32, 1.0, 7692.0)):
        lin(A(t), A(J, 0, n), m, c)
    for t in range(2):
        lin(A(JM[t], 0, CV[t]), A(J, 0, CV[t]), 1.0, 5760.0 - 552)
        lin(A(JM[t], CV[t], 198), A(J, 0, 198 - CV[t]), 1.0, 5760.0 - 552)
    MID, GOT, NW = f(192), f(144), b(208)
    fl(A(NW, 198, 208), 0)
    fl(A(GOT), -1)

    RH = UW
    ZD, LTT = b(3200), (MW, 4096, 1920)
    fl(A(ZD, 3168, 3184), 0)
    fl(A(ZD, 3184, 3200), 255)
    MT, MR, MQ, LA, WN, JF, MG = f(192), f(192), ii(192), u(192), f(32), f(192), f(512)
    fl(A(MG), 200)
    lin(A(JF), A(J, 0, 192), 1.0, 1920.0 + 16 * (65 + C0))
    GA = ZD

    def choose(t):
        SCOPE[:] = ["a", 0]
        if t:
            ts(A(F, 16, 656), A(P, 16, 656), W["fs"], MUL, W["fc"], MIN)
        KV, E, DS, AC, M1 = f(40), f(480), f(480), f(120), f(40)
        mm(acc(A(B[2], 0, 40), ext(None, ZKEY, F, 40, 16)))
        cp(A(KV), A(B[2], 0, 40), "vs")
        mm([(A(B[2], 0, 480), BDG, A(F, 96, 576), True, True)])
        cp(A(DS), A(B[2], 0, 480), "vs")
        mm([(A(B[2], 0, 480), BKEY, A(F, 96, 576), True, True)])
        tt(A(E), A(B[2], 0, 480), A(DS), MUL)
        for c in range(6):
            for s in range(2):
                k = 2 * c + s
                l = A(L1, 40 * k, 40 * k + 40)
                cp(A(RH, 640 * k, 640 * k + 640), IND(A(F, 0, 656), l), "vs")
            mm(acc(A(B[c % 2], 0, 80), ext(None, ZKEY, RH, 80, 1280 * c)))
            if c == 0:
                tt(A(AC, 0, 40), A(B[0], 0, 40), A(KV), MIN)
                cp(A(AC, 40, 80), A(B[0], 40, 80))
            else:
                tt(A(AC, 0, 80), A(B[c % 2], 0, 80), A(AC, 0, 80), MIN)
        tt(A(M1), A(AC, 0, 40), A(AC, 40, 80), MIN)
        tt(A(XI_, 16, 656, 16), A(AC, 0, 40), A(AC, 40, 80), MIN)
        tt(A(XI_, 17, 656, 16), A(M1), A(XI_, 16, 656, 16), SUB)
        turn(W2)
        for k in range(12):
            cp(A(RH, 496 * k, 496 * k + 496), IND(A(W2), A(L1, 40 * k + 4, 40 * k + 35)), "vs")
            mm([(A(B[0], 0, 480), BS01, A(W2, 96, 576), True, False)] * (k == 0) + [(A(B[0], 0, 480), BS01, A(RH, 496 * k + 16, 496 * k + 496), False, k == 11)])
        CH, PR, GS, G2, LG = b(480), b(480), f(482), f(3), u(4)
        GN = (GS[0], GS[1] + 479, 3)
        tt(A(CH), A(B[0], 0, 480), A(E), EQ)
        scan(A(PR), A(ONE, 0, 480), A(CH), MUL, ADD)
        ts(A(CH), A(PR), col(JH, 0), LT, 2.0, MUL)
        scan(A(GS, 0, 480), A(ONE, 0, 480), A(CH), MUL, ADD, -480.0)
        for c in range(1, 3):
            act(A(RH, 6000 + 480 * c, 6480 + 480 * c), A(PR), AF.Sign, col(JH, c), -1.0, col(GN, c))
        ts(A(G2), A(GN), 480.0, EQ)
        tt(A(G2), A(G2), A(JG), MUL)
        ts(A(GN), A(GN), 0.5, MUL, 336.0, ADD)
        tt(A(GN), A(GN), A(G2), ADD)
        cp(A(LG, 0, 3), A(GN))
        return A(LG, 0, 3)

    GT2, GV, FG, U1, U2, GH, GC, LU, LE_, FU = f(128), f(48), b(48), f(36), f(36), f(36), f(48), u(36), u(36), b(576)

    def lists(t, LG):
        cp(A(GR, 16, 64), IND(A(P), LG))
        cp(A(FG), IND(A(F), LG), "s")
        tr(A(GT2, 0, 64), A(GR, 16, 80))
        tr(A(GT2, 64, 128), A(GR, 0, 64))
        cp(A(GV), IND(A(GT2), A(LGT, 0, 3)))
        ts(A(U2), A(GV, 0, 36), 1.0, LT)
        tt(A(U2), A(U2), A(JU), MUL)
        tt(A(U1), A(GV, 0, 36), A(U2), ADD)
        ts(A(LU), A(U1), U13, MUL, 15.0, ADD)
        ts(A(GH), A(GV, 0, 36), MAGIC, ADD, MAGIC, SUB)
        tt(A(GH), A(GV, 0, 36), A(GH), SUB)
        ts(A(LE_), A(GH), -1.0, ADD)
        cp(A(Y), IND(A(XM, 0, 2560) if t else A(XL, 0, 2048), A(LE_)), "s")

    def contract(t, LG, store=None):
        n, n0 = 2560 + 512 * t, 2048 + 512 * t
        nc = n // 16
        SCOPE[:] = ["b", 0]
        NS, NK, SG, KW = f(576), f(576), b(576), f(1280)
        ts(A(NS), IND(A(P), A(LU)), 1 / 128, MUL)
        cp(A(FU), IND(A(F), A(LU)), "vs")
        XO, XN = XL, XM
        tiles = [(0, 6), (6, 11), (11, 21), (21, 30), (30, 38), (38, 45), (45, 51), (51, 60), (60, 66)]
        runs = lambda q0, q1: [(j, max(q0, lex[j]), min(q1, lex[j + 1])) for j in range(11) if lex[j] < q1 and q0 < lex[j + 1]]
        for x, (q0, q1) in enumerate(tiles):
            bk = B[4 + x % 4]
            mm([(A(bk, 48 * (q - q0), 48 * (q - q0 + 1)), A(UBM), A(FU, 48 * j, 48 * j + 48), True, True) for j, a0, a1 in runs(q0, q1) for q in range(a0, a1)])
            for j, a0, a1 in runs(q0, q1):
                k0 = j + 1 - lex[j]
                tt(A(CC, 48 * a0, 48 * a1), A(NS, 48 * (k0 + a0), 48 * (k0 + a1)), A(bk, 48 * (a0 - q0), 48 * (a1 - q0)), SUB)
        for x, (q0, q1) in enumerate(CLAMP):
            ts(A(CC, 48 * q0, 48 * q1), A(CC, 48 * q0, 48 * q1), -16.0, MAX, 16.0, MIN)
            mm(acc(A(B[0], 3 * q0, 3 * q1), ext(None, Z14, CC, 3 * (q1 - q0), 48 * q0)))
        dmas([(A(ZD, 48 * lex[d], 48 * lex[d + 1]), A(Y, 48 * d + 48, 576)) for d in range(11)]
             + [(A(UW, 48 * lex[d], 48 * lex[d + 1]), A(Y, 0, 528 - 48 * d)) for d in range(11)], 7000)
        for c in (0, 1584):
            dma(A(ZD, c, c + 1584), A(UW, c, c + 1584), "g", 4500, True)
        clear()
        if store:
            middles(0)
            store()
        for k in range(2):
            mm([(A(B[1 + k], 48 * j, 48 * j + 48), BVB, A(FG), True, True) for j in range(6)])
            if k == 0:
                lin(A(GOT, 65 * t + 16, 65 * t + 64), A(B[1], 0, 48), 1 / 64, -1.25)
            tt(A(NK, 288 * k, 288 * k + 288), A(B[1 + k], 0, 288), A(NS, 288 * k, 288 * k + 288), SUB)
        act(A(NK), A(NK), AF.Square, 0.0, 1 / 32)
        act(A(SG), A(NK), AF.Sign, 1.0, -1.0)
        mm(acc(A(B[1], 0, 36), ext(None, ZL12, SG, 36) + ext(None, ZM2, FU, 36)))
        lin(A(WW, 200, 236), A(B[1], 0, 36), -0.5, -18.0)
        for k in range(2):
            s = (288 * k, 288 * k + 288)
            mm(acc(A(B[2 - k], 0, 288), [(A(SFH), A(SG, *s)), (A(SFF), A(FU, *s))]))
            cp(A(PFU, *s), A(B[2 - k], 0, 288), "s")
        fl(A(KW, 0, 656), 32)
        lin(A(NK), A(SG), W["k16"], 48.0, "s")
        for c in range(0, 36, PSC):
            silu(IND(A(KW), A(LU, c, c + PSC)), A(NK, 16 * c, 16 * (c + PSC)))
        ts(A(GC), A(GR, 16, 64), W["cm"], MUL, W["cx"], MAX)
        cp(IND(A(P), LG), A(GC))
        RH_, RL, SQ, SU, SV, IN, OF, LM = f(198), f(198), b(576), b(208), b(208), b(198), f(198), u(200)
        ts(A(RH_), A(B[0], 0, 198), MAGIC / 2, ADD, MAGIC / 2, SUB)
        tt(A(RL), A(B[0], 0, 198), A(RH_), SUB)
        ts(A(WW, 0, 198), A(RL), -553.0, EQ)
        JC, EE = (B[7], 0, 198), (B[2], 0, 198)
        act(A(NW, 0, 198), A(RL), AF.Abs, 553.0)
        lin(A(JC), A(RL), -32768.0, -552.5 * 32768)
        cp(A(SQ), IND(A(WW), A(LSQ)))
        scan(A(ST, 0, 576), A(RS1), A(SQ), MUL, ADD)
        tt(A(SU), IND(A(ST), A(LUP, 0, 13)), A(NW), MAX)
        tt(A(SV), IND(A(ST), A(LDN, 0, 13)), A(SU), MAX)
        ts(A(SU, 0, 198), A(SV, 0, 198), 0.0, LE)
        for c in range(3):
            scan(A(IN, c, 198, 3), A(ONE, 0, 66), A(SU, c, 198, 3), MUL, ADD)
        act(A(EE), A(SV, 0, 198), AF.Relu, 0.0, 16384.0)
        mm([(A(B[1], 0, 3), A(TS), A(IN, 195, 198), True, False), (A(B[1], 1, 3), A(BD), A(IN, 195, 197), False, False), (A(B[1], 2, 3), A(BD), A(IN, 195, 196), False, True)])
        tt(A(JC), A(JC), A(JM[t]), MIN)
        tt(A(JC), A(JC), A(RL), MAX)
        tt(A(OF), A(IN), A(EE), ADD)
        for c in range(3):
            ts(A(OF, c, 198, 3), A(OF, c, 198, 3), col(B[1], c), ADD, float(n0 - 553), ADD)
        tt(A(OF), A(JC), A(OF), MIN)
        ts(A(LM, 0, 198), A(OF), 552.0, ADD)
        cp(IND(A(MW), A(LM, 0, CV[t])), A(SD, 0, 16 * CV[t]))
        silu(IND(A(WS), A(LM, CV[t], 198)), A(SF, 16 * (CV[t] - C0)))
        tt(A(MW, n0, n), A(MW, n0, n), A(WS, n0, n), ADD)
        olds = [(0, 1024), (1024, n0)]
        for c0, c1 in olds:
            dma(A(MW, c0, c1), A(WS, c0, c1), "g", 4000, True)
        for k in range(2):
            act(A(B[6], 0, 320), A(KW, 16 + 320 * k, 336 + 320 * k), AF.Relu, 56.0 * 2 ** 20, -2.0 ** 20)
            tt(A(P, 16 + 320 * k, 336 + 320 * k), A(B[6], 0, 320), A(P, 16 + 320 * k, 336 + 320 * k), MIN)
        LN, LS, AN = u(64), u(64), f(32)
        dmas([(A(WS, 3072 + c, 3584 + c), A(MG)) for c in range(0, n0, 512)], 5000)
        for c in range(0, 120, MAPC):
            silu(IND(A(WS, 3072, 4032 + n0), A(LS_, c, c + MAPC)), A(SF, 16 * c, 16 * (c + MAPC)))
        MK, SM, G, CM, PO, PE_, UX, LP = b(512), b(1024), b(1024), b(1024), f(64), f(32), f(64), u(64)
        mm([(A(B[2]), A3(BL, 0), A(MW, n0, n), True, True)])
        if t in MKV:
            ts(A(MK), A(B[2]), A(NPM, 1, 2), EQ)
        else:
            act(A(CM, 0, 512), A(B[2]), AF.Abs, A(NPM, 0, 1))
            act(A(MK), A(CM, 0, 512), AF.Relu, 1.0, -1.0)
        for e in range(2):
            s, l = (512 * e, 512 * e + 512), (32 * e, 32 * e + 32)
            mm(acc(A(B[1 + 3 * e], 0, 32), ext(None, (ZSA, ZSB)[e], MW, 32, n0)))
            ts(A(LS, *l), A(B[1 + 3 * e], 0, 32), 1.0 - 65 * TOP, ADD, 591.0, MIN)
            mm(acc(A(B[3 * e], 0, 32), ext(None, (ZA, ZBB)[e], MW, 32, n0)))
            ts(A(LN, *l), A(B[3 * e], 0, 32), -65.0 * TOP, ADD, 640.0, MIN)
            if e == 0:
                lin(A(AN), A(B[0], 0, 32), 16384.0, -16384 * (575.5 + 65 * TOP))
                tt(A(PE_), A(AN), A(JQ), MIN)
            cp(A(G, *s), IND(A(PFU), A(LN, *l)), "s")
            tt(A(SM, *s), IND(A(ST), A(LS, *l)), A(MK), MUL)
        mm(acc(A(B[5], 0, 64), ext(None, ZU, G, 64)))
        for e in range(2):
            tt(A(UX, 32 * e, 32 * e + 32), A(B[5], 32 * e, 32 * e + 32), A(PE_), MAX)
        for e in range(2):
            s, l = (512 * e, 512 * e + 512), (32 * e, 32 * e + 32)
            mm(acc(A(B[e]), [(A(ID), A(G, *s)), (A(NBD), A(SM, *s))]))
            act(A(CM, *s), A(B[e]), AF.Sign, 0.5)
            mm(acc(A(B[2 + e], 0, 32), ext(None, Z640, CM, 32, s[0])))
            tt(A(PO, *l), A(B[2 + e], 0, 32), A(UX, *l), ADD)
            ts(A(LP, *l), A(PO, *l), 3828.0, ADD)
            tt(IND(A(UW), A(LP, *l)), A(G, 512 - s[0], 1024 - s[0]), A(NM[t]), ADD)
        a1, a2, a3 = f(32), f(32), f(32)
        lin(A(a3), A(B[2], 0, 32), 0.125, 468.0 + 16 * (65 + C0))
        tt(A(a1), A(UX, 0, 32), A(UX, 32, 64), MAX)
        tt(A(a2), A(UX, 0, 32), A(UX, 32, 64), MIN)
        ts(A(a1), A(a1), 92.0, GE, 8192.0, MUL)
        ts(A(a2), A(a2), 572.0, GE, -7792.0, MUL)
        tt(A(a1), A(a1), A(a2), ADD)
        tt(A(a1), A(a1), A(UX, 0, 32), ADD)
        tt(A(a1), A(a1), A(a3), ADD)
        tt(A(a1), A(a1), A(JF, n0 // 16, nc), MIN)
        ts(A(LF, n0 // 16, nc), A(a1), -16.0 * (65 + C0), ADD)
        for k, (v0, v1) in enumerate(((0, 96), (544, 640), (96, 320), (320, 544))):
            bk = A(B[min(k, 2) if t else k % 3], 0, v1 - v0)
            mm(acc(bk, [(Z(ZUP, l), A(UW, 640 * l + v0, 640 * l + v1)) for l in range(12)]))
            tt(A(P, 16 + v0, 16 + v1), bk, A(P, 16 + v0, 16 + v1), ADD)
        for v0, v1 in ((0, 96), (544, 640)) + ((96, 320), (320, 544)) * (t == 0):
            tr(A(TT, v0, v1), A(P, 16 + v0, 16 + v1))
        for v0, v1 in ((0, 96), (576, 672)) + ((96, 320), (320, 576)) * (t == 0):
            tr(A(TT, 640 + v0, 640 + v1), A(P, v0, v1))
        a4 = f(160)
        for x, (c0, c1) in enumerate([(n0, n)] + olds):
            s, w = (c0 // 16, c1 // 16), (c1 - c0) // 16
            mm(acc(A(B[7 - 3 * (x % 2)], 0, w), ext(None, ZQ, MW, w, c0)))
            ts(A(LA, *s), A(B[7 - 3 * (x % 2)], 0, w), -65.0 * TOP, ADD, 3185.0 if x else 3170.0, MIN)
        ts(A(XN, n0, n), IND(A(ZD), A(LA, n0 // 16, nc)), 255.0, MIN)
        for c in range(0, n0, XNC):
            tt(A(XN, c, c + XNC), IND(A(ZD), A(LA, c // 16, (c + XNC) // 16)), A(XO, c, c + XNC), MIN)
        lin(A(WN), A(AN), -1.0, 0.0)
        dma(A(MW, 0, n0), A(WS, 3072, 3072 + n0), "g", 4500)
        mm(acc(A(B[3], 0, n0 // 16), ext(None, ZZ, MW, n0 // 16)))
        tt(A(a4, 0, n0 // 16), A(B[3], 0, n0 // 16), A(JF, 0, n0 // 16), MIN)
        ts(A(LF, 0, n0 // 16), A(a4, 0, n0 // 16), -16.0 * (65 + C0), ADD)

    def middles(t):
        n0 = 2048 + 512 * t
        nc = n0 // 16 + 32
        ts(A(MQ, 0, nc), A(LA, 0, nc), -23.5, ADD, 1 / 48, MUL)
        cp(A(MT, 0, nc), A(LA, 0, nc))
        ts(A(MR, 0, nc), A(MQ, 0, nc), -48.0, MUL, 65.0 * t, ADD)
        tt(A(MT, 0, nc), A(MT, 0, nc), A(MR, 0, nc), ADD)
        tt(A(MID, nc - 32, nc), A(MT, nc - 32, nc), A(WN), MIN)
        for k in range(n0 // 512):
            s = (512 * k, 512 * k + 512)
            mm(acc(A(B[5 + k % 2]), [(A(ID), A(XL, *s)), (A(NID), A(XM, *s))]))
            act(A(LT2, *s), A(B[5 + k % 2]), AF.Sign, -0.5)
        o, m = A(B[3 + 4 * t], 0, n0 // 16), A(MID, 0, n0 // 16)
        mm(acc(o, ext(None, ZB, LT2, n0 // 16)))
        lin(o, o, 4096.0, -4096.0)
        tt(o if t else m, o, A(MT, 0, n0 // 16), MIN)
        if t:
            tt(m, m, o, MAX)

    def places(t):
        SCOPE[:] = ["d", 0]
        PS, HS, O1, O2 = f(128), f(120), f(120), f(60)
        if t:
            for v0 in (0, 544):
                tr(A(TT, v0, v0 + 96), A(P, 16 + v0, 112 + v0))
            for v0 in (0, 576):
                tr(A(TT, 640 + v0, 736 + v0), A(P, v0, v0 + 96))
        cp(A(PS), IND(A(TT), A(LSE)) if t else IND(A(TIN), A(LS0)))
        ts(A(HS), A(PS, 0, 120), MAGIC, ADD, MAGIC, SUB)
        tt(A(HS), A(PS, 0, 120), A(HS), SUB)
        tt(A(O1), A(PS, 0, 120), A(AV), LE)
        ts(A(O2), A(PS, 0, 60), 81.0 * 8192, GE)
        tt(A(O1, 0, 60), A(O1, 0, 60), A(O2), MAX)
        tt(A(O1), A(O1), A(JXS[t]), MUL)
        tt(A(O1), A(O1), A(HS), MAX)
        ts(A(LS_), A(O1), -1.0, ADD)

    def seam(t):
        SCOPE[:] = ["c", 0]
        side = (A(P, 16, 96), A(P, 576, 656))
        buf = lambda nm, w, d: [own("%s%d%d" % (nm, t, e), "sbuf", [128, w], d) for e in range(2)]
        TB, TR, XS, XR = buf("TB", 80, "bfloat16"), buf("TR", 80, "bfloat16"), buf("XS", 480, "uint16"), buf("XR", 480, "uint16")
        PS, HS, LN_, NMF, RI, LI = f(128), f(120), u(120), f(120), f(120), u(120)
        cp(A(PS), IND(A(TT), A(LSE)))
        ts(A(HS), A(PS, 0, 120), MAGIC, ADD, MAGIC, SUB)
        tt(A(NMF), A(PS, 0, 120), A(HS), SUB)
        ts(A(LN_), A(NMF), -1.0, ADD)
        XN, n = XM, 2560 + 512 * t
        ts(A(TB[0]), side[0], 127.0 * 8192, ADD, 208.0 * 8192, MIN)
        ts(A(TB[1]), side[1], (127.0 - 560) * 8192, ADD, 127.5 * 8192, MAX)
        for e in range(2):
            send(A(TR[1 - e]), A(TB[e]), 2 * e - 1, 4000)
        own_ = (A(GA, 0, 960), A(GA, 960, 1920))
        for e in range(2):
            cp(own_[e], IND(A(XN, 0, n), A(LN_, 60 * e, 60 * e + 60)), "vs")
            bk = A(B[6 - 6 * t + e], 0, 480)
            mm(acc(bk, [(A(ID), A(GA, 960 * e, 960 * e + 480)), (A(I256), A(GA, 960 * e + 480, 960 * e + 960))]))
            cp(A(XS[e]), bk)
            send(A(XR[1 - e]), A(XS[e]), 2 * e - 1, 5500)
        for v0, v1 in ((0, 320), (320, 640)) * t:
            o = A(B[2], 0, v1 - v0, p=q)
            mm([(o, A(PERM), A(P, 16 + v0, 16 + v1), True, True)])
            ts(A(HF, v0, v1, p=q), o, MAGIC, ADD, MAGIC, SUB)
            lin(A(YN, v0, v1, p=q), A(HF, v0, v1, p=q), U13, -1.0)
            tt(A(HF, v0, v1, p=q), o, A(HF, v0, v1, p=q), SUB)
            lin(A(YE, v0, v1, p=q), A(HF, v0, v1, p=q), 1.0, -1.0)
        for e in range(2):
            for k in range(2):
                s = (960 * e + 480 * k, 960 * e + 480 * k + 480)
                if (t, e, k) in EQS:
                    mm(sum([acc(A(B[4 + k], 80 * l, 80 * l + 80), [(A3(BL, 6 * k + l), A(TB[e])), (A(NID), A(TR[e]))]) for l in range(6)], []))
                    act(A(B[4 + k], 0, 480), A(B[4 + k], 0, 480), AF.Abs)
                    act(A(LTT, *s), A(B[4 + k], 0, 480), AF.Relu, 1.0, -1.0)
                elif (t, e, k) in EQT:
                    mm([(A(B[4 + k], 80 * l, 80 * l + 80), A3(BL, 6 * k + l), A(TB[e]), True, True) for l in range(6)])
                    for l in range(6):
                        tt(A(LTT, s[0] + 80 * l, s[0] + 80 * l + 80), A(B[4 + k], 80 * l, 80 * l + 80), A(TR[e]), EQ)
                else:
                    mm(sum([acc(A(B[4 + k], 80 * l, 80 * l + 80), [(A3(BL, 6 * k + l), A(TB[e])), (A(NID), A(TR[e]))]) for l in range(6)], []))
                    ts(A(LTT, *s), A(B[4 + k], 0, 480), 0.0, EQ)
            mm(acc(A(B[4], 0, 60), ext(None, ZM, LTT, 60, 960 * e)))
            s = (60 * e, 60 * e + 60)
            tt(A(RI, *s), A(JA, *s), A(B[4], 0, 60), SUB)
            cp(A(LI, *s), A(RI, *s))
        for e in range(2):
            XI, KP = ii(480), f(80)
            mn, sg = A(GB, 960 * e, 960 * e + 960), A(LTT, 960 * e, 960 * e + 960)
            cp(A(XI), A(XR[e]))
            ts(A(XW[e], 0, 480), A(XI), 255, AND)
            ts(A(XW[e], 480, 960), A(XR[e]), 1 / 256, MUL, -0.5, ADD)
            tt(mn, IND(A(XW[e]), A(LI, 60 * e, 60 * e + 60)), own_[e], MIN)
            for k in range(2):
                s = (960 * e + 480 * k, 960 * e + 480 * k + 480)
                mm(acc(A(B[4 + k], 0, 480), [(A(ID), A(GA, *s)), (A(NID), A(GB, *s))]))
                act(A(LTT, *s), A(B[4 + k], 0, 480), AF.Sign, -0.5)
            signs = [A(LTT, 960 * e + 80 * l, 960 * e + 80 * l + 80) for l in range(12)]
            if t == 0:
                mm(acc(A(B[3], 0, 80), [(Z(ZB, l), signs[l]) for l in range(12)]))
                ts(A(KP), A(B[3], 0, 80), 2.0, LT)
                tt(side[e], side[e], A(KP), MUL)
                tt(A(F, 16 + 560 * e, 96 + 560 * e), A(F, 16 + 560 * e, 96 + 560 * e), A(KP), MUL)
                continue
            o = A(B[3 - e], 0, 80, p=q)
            mm(acc(o, [(A(NID, 0, 96), A(ONE, 0, 80))] + [(A(ZP, 15 - l, 111 - l), signs[l]) for l in range(12)]))
            ts(o, o, -4096.0, MUL, -1.0, MAX)
            for y in (YN, YE):
                tt(A(y, 560 * e, 560 * e + 80, p=q), o, A(y, 560 * e, 560 * e + 80, p=q), MIN)

        def store():
            for c0, c1 in OUTS if t else [(c, c + 512) for c in range(0, n, 512)]:
                cp(A(XL, c0, c1), IND(A(GB[:2] + (1920 + n,)), A(LF, c0 // 16, c1 // 16)), "vs")
                if t:
                    dma(X("ylen", ALL, slice(c0, c1)), A(XL, c0, c1), "y", 2600 + (c1 - c0) // 2)
        return store

    LSE, s1, s2, s3, s4, si, JA, AV, JXS, QC, I256 = u(8), f(8), f(8), f(8), f(8), ii(8), f(120), f(120), [f(120), f(120)], f(1), b(128)
    ts(A(s1), A(J, 0, 8), 60.0, GE)
    ts(A(s2), A(s1), -60.0, MUL)
    tt(A(s2), A(s2), A(J, 0, 8), ADD)
    ts(A(si), A(s2), 0.2, MUL, -0.4, ADD)
    ts(A(s3), A(si), -5.0, MUL)
    tt(A(s2), A(s2), A(s3), ADD)
    ts(A(s3), A(s2), 16.0, MUL)
    tt(A(s3), A(s3), A(si), ADD)
    tt(A(s2), A(s2), A(s1), ADD)
    ts(A(si), A(s2), PH, ADD)
    ts(A(si), A(si), 1, AND)
    ts(A(s4), A(si), 656.0, MUL)
    ts(A(s1), A(s1), 560.0, MUL)
    tt(A(s3), A(s3), A(s1), ADD)
    LS0 = u(8)
    ts(A(LS0), A(s3), 16.0, ADD)
    tt(A(s3), A(s3), A(s4), ADD)
    cp(A(LSE), A(s3))
    JB = f(120)
    iota(A(JB), [[0, 24], [16, 5]], 960)
    lin(A(JA), A(JB), 1.0, PM)
    for e in range(2):
        lin(A(AV, 60 * e, 60 * e + 60), A(JA, 0, 60), 8192.0, 8192.0 * (560 * e - 958.5))
        for t in range(2):
            lin(A(JXS[t], 60 * e, 60 * e + 60), A(J, 0, 60), 1.0, 2049.0 + 512 * t)
        fl(A(XW[e], 960, 1040), 255)
    ts(A(QC), PM, -80.0, MUL, 960.0, ADD)
    ts(A(QC), A(QC), 0.0, MAX)
    W["m1"] = A(QC)
    ZM = zt("m1")
    lin(A(I256), A(ID), 256.0, 0.0)
    SCOPE[0] = None
    LS_, LF, ZP, G12 = u(120), u(192), b(144), f(1)
    HF, YE, YN, q = TIN, (TT[0], TT[1], 640), (TT[0], TT[1] + 640, 640), (0, 96)
    ts(A(G12), PG, 12.0, MUL)
    ts(A(ZP), A(XZ), A(G12), EQ)
    lg = choose(0)
    lists(0, lg)
    places(0)
    contract(0, lg)
    fill(1)
    for c in range(0, 30, 10):
        ts(A(L1, 16 * c, 16 * c + 160), IND(A(TT), A(LSV, c, c + 10)), U13, MUL, 15.0, ADD)
    lg = choose(1)
    lists(1, lg)
    store = seam(0)
    places(1)
    contract(1, lg, store)
    middles(1)
    SCOPE[0] = None
    LMID = u(192)
    ts(A(LMID), A(MID), 16.0, ADD)
    for k in range(4):
        cp(A(YM, 768 * k, 768 * k + 768), IND(A(GOT), A(LMID, 48 * k, 48 * k + 48)), "vs")
    dma(X("ymid", ALL, ALL), A(YM, p=(0, 128, 16)), "y")
    seam(1)()
    dma(X("ynb", ALL, ALL), A(YN, p=q), "y")
    dma(X("yen", ALL, ALL), A(YE, p=q), "s")


def schedule():
    n = len(OPS)
    hist = {}
    for k, o in enumerate(OPS):
        dep = {}
        for kind, regs in (("r", o["rd"]), ("w", o["wr"])):
            for nm, lo, hi, st, pm in regs:
                ps = nm in SHAPES and SHAPES[nm][0] == "psum"
                for j, kd, l2, h2, s2, p2 in hist.get(nm, []):
                    meet = l2 <= hi and lo <= h2 and pm & p2 != 0 and (kd == "w" or kind == "w") and not (st == s2 and (lo - l2) % st)
                    if ps or meet:
                        dep[j] = dep.get(j, False) or (meet and not (ps and o["alts"][0][0] == "t"))
        dep.pop(k, None)
        for kind, regs in (("r", o["rd"]), ("w", o["wr"])):
            for nm, lo, hi, st, pm in regs:
                if hi < 1 << 30:
                    hist.setdefault(nm, []).append((k, kind, lo, hi, st, pm))
        o["dep"] = dep
    succ, after, near, above = [[] for _ in range(n)], [[] for _ in range(n)], [], []
    pred = [set(o["dep"]) | ({o["after"]} if "after" in o else set()) for o in OPS]
    for k in range(n):
        far = 0
        for j in pred[k]:
            far |= above[j]
        pred[k] = sorted(j for j in pred[k] if not far >> j & 1 or "sem" in OPS[j])
        for j in pred[k]:
            far |= 1 << j
        above.append(far)
        near.append([(j, "sem" not in OPS[j] and "sem" not in OPS[k] and not OPS[k]["dep"][j]) for j in pred[k]])
        for j, soft in near[k]:
            succ[j].append(k)
            after[j].append((k, soft))

    def gap(busy, st, d):
        lo, hi = 0, len(busy)
        while lo < hi:
            m = (lo + hi) // 2
            if busy[m][1] > st:
                hi = m
            else:
                lo = m + 1
        while lo < len(busy) and st + d > busy[lo][0]:
            st = busy[lo][1]
            lo += 1
        return st, lo

    pri = [0.0] * n
    for k in range(n - 1, -1, -1):
        pri[k] = min(a[2] for a in OPS[k]["alts"]) + OPS[k].get("lat", 0) + SYNC + max([pri[j] for j in succ[k]] + [0])

    late = [o.get("lat", 0) + SYNC for o in OPS]

    def ranked(pr, first):
        seen, out = [False] * n, []
        for k in np.argsort(-pr, kind="stable").tolist():
            todo = [k]
            while todo:
                q = todo[-1]
                if seen[q]:
                    todo.pop()
                    continue
                wait = [j for j in first[q] if not seen[j]]
                if wait:
                    todo.extend(wait)
                else:
                    seen[q] = True
                    out.append(q)
                    todo.pop()
        return out

    def place(pr, bias, base=None):
        order, x = ranked(pr, pred), 0
        if base:
            while x < n and order[x] == base[4][x] and bias[order[x]] == base[5][order[x]]:
                x += 1
            if x == n:
                return base
            x -= x % 64
        if x:
            marks = base[6][:x // 64 + 1]
            busy = {e: list(q) for e, q in marks[-1].items()}
            done, use, at = list(base[3]), list(base[1]), list(base[2])
        else:
            marks, busy = [None], dict(v=[], s=[], t=[], g=[], y=[], n=[])
            done, use, at = [0.0] * n, [None] * n, [0.0] * n
        for y in range(x, n):
            k = order[y]
            if y > x and y % 64 == 0:
                marks.append({e: list(q) for e, q in busy.items()})
            best = None
            for a in OPS[k]["alts"]:
                e, st = a[0], 0.0
                for i, soft in near[k]:
                    r = done[i] - SYNC if soft and use[i][0] == e else done[i]
                    if r > st:
                        st = r
                d = a[2] + 20 if e != "n" else 0
                st, pos = gap(busy[e], st, d)
                c = st + d + (bias[k] if e == "v" else 0)
                if best is None or c < best[0]:
                    best = (c, a, st, d, pos)
            c, a, st, d, pos = best
            if d:
                busy[a[0]].insert(pos, (st, st + d))
            use[k], at[k], done[k] = a, st, st + a[2] + late[k]
        return max(done), use, at, done, order, bias, marks

    def back(got):
        use, done = got[1], got[3]
        busy, end = dict(v=[], s=[], t=[], g=[], y=[], n=[]), [0.0] * n
        for k in ranked(np.array(done) + np.arange(n) * 1e-6, succ):
            a = use[k]
            lat = OPS[k].get("lat", 0) + SYNC
            st = max([end[j] + (0 if soft and use[j][0] == a[0] else lat) for j, soft in after[k]] + [lat])
            d = a[2] + 20 if a[0] != "n" else 0
            st, pos = gap(busy[a[0]], st, d)
            if d:
                busy[a[0]].insert(pos, (st, st + d))
            end[k] = st + d
        return np.array(end)

    pr, bias = np.array(pri), [BIAS] * n
    both = [k for k in range(n) if len(OPS[k]["alts"]) > 1]
    for k in both:
        c = {a[0]: a[2] for a in OPS[k]["alts"]}
        bias[k] = BIAS + THRIFT * (c["v"] - c["s"]) if "s" in c else SPARE
    got = best = place(pr, bias)
    for it in range(TURNS):
        p2 = back(got)
        got = place(p2, bias)
        if got[0] < best[0]:
            best, pr = got, p2

    def held(got):
        use, at, done = got[1], got[2], got[3]
        last, before, out = {}, [None] * n, []
        for k in sorted(range(n), key=lambda q: at[q]):
            before[k], last[use[k][0]] = last.get(use[k][0]), k
        k = max(range(n), key=lambda q: done[q])
        while k is not None:
            j = max(pred[k], key=lambda q: done[q]) if pred[k] else None
            p = before[k] if use[k][0] != "n" else None
            if p is not None and (j is None or at[p] + use[p][2] + 21 > done[j]) and p != j:
                out.append((k, p))
                j = p
            k = j
        return out

    rng = np.random.RandomState(SEARCH[1])
    pick = lambda q: q[int(rng.randint(0, len(q)))]

    def walk(pr, bias, steps):
        now, pairs = place(pr, bias), None
        best = (now, pr)
        for it in range(steps):
            p2, b2 = pr, bias
            if it % 6 in (1, 3, 4):
                pairs = pairs if pairs and pairs[0] is now else (now, held(now))
                k, j = pick(pairs[1])
                p2, d = pr.copy(), pick([0, 300, 1000, 3000])
                if len(OPS[j]["alts"]) > 1 and rng.rand() < 0.3:
                    b2 = list(bias)
                    b2[j] = -3000 if now[1][j][0] != "v" else 3000
                elif rng.rand() < 0.5:
                    p2[k] = max(p2[k], p2[j]) + 1 + d
                else:
                    p2[j] = min(p2[k], p2[j]) - 1 - d
            elif it % 6 == 2:
                a, b2 = int(rng.randint(0, len(both))), list(bias)
                for k in both[a:a + pick([1, 1, 2, 4])]:
                    b2[k] = -3000 if now[1][k][0] != "v" else 3000
            else:
                a, p2 = int(rng.randint(0, n)), pr.copy()
                p2[a:a + pick([1, 3, 10, 30, 80])] += pick([-1, 1]) * pick([300, 1000, 3000, 10000, 30000])
            got = place(p2, b2, now)
            if got is not now and got[0] < now[0] + 1500 and it % BACK == 0:
                p3 = back(got)
                g3 = place(p3, b2)
                if g3[0] < got[0]:
                    got, p2 = g3, p3
            if got[0] < now[0] + HEAT * (1 - it / steps):
                now, pr, bias = got, p2, b2
                if got[0] < best[0][0]:
                    best = (got, p2)
        return best

    best, pr = min([walk(pr, bias, SEARCH[3]) for k in range(STARTS)], key=lambda q: q[0][0])
    best, pr = walk(pr, best[5], SEARCH[0])
    kept = best[5]

    def weigh(got):
        use, total = got[1], 0.0
        order = sorted(range(n), key=lambda k: (got[2][k], k))
        for sc, ga, sync, pe, far, dm, unit in RANGES:
            free, done = dict(v=0.0, s=0.0, t=0.0, g=0.0, y=0.0, n=0.0), [0.0] * n
            for k in order:
                o, e, c = OPS[k], use[k][0], use[k][2]
                c = 60 + (c - 60) * sc if o["sc"] else 70 + (c - 70) * ga if o["ga"] else c * pe if e == "t" else c
                st = free[e]
                for i, soft in near[k]:
                    r = done[i] - sync if soft and use[i][0] == e else done[i]
                    if r > st:
                        st = r
                if e != "n":
                    free[e] = st + c + 20
                done[k] = st + c + o.get("lat", 0) * (far if "send" in o else dm) + sync
            total += max(done) / unit
        return total

    mark = weigh(best)
    pr = np.array([-best[2][k] for k in range(n)])
    for it in range(SEARCH[2]):
        a = int(rng.randint(0, n))
        p2 = pr.copy()
        p2[a:a + int(rng.choice([1, 3, 10, 30]))] += int(rng.choice([-1, 1]) * rng.choice([300, 1000, 3000, 10000]))
        got = place(p2, kept, best)
        if got is not best and got[0] < best[0] + 2500:
            m = weigh(got)
            if m < mark:
                best, pr, mark = got, p2, m
    for k in range(n):
        OPS[k]["use"], OPS[k]["at"] = best[1][k], best[2][k]
    return sorted(range(n), key=lambda k: (best[2][k], k)), best[0]


THRIFT = 3.0
HEAT = 300.0
BACK = 3
STARTS = 4
SPARE = 3000.0
SYNC, BIAS, TURNS, SEARCH = 120.0, 500.0, 30, [3500, 2, 1200, 2000]
RANGES = [(1.0, 1.0, 120, 1.0, 1.0, 1.0, 165.0), (1.4, 1.3, 120, 1.0, 1.0, 1.0, 200.0), (0.45, 0.75, 120, 1.0, 1.8, 1.6, 155.0), (1.0, 1.0, 250, 1.3, 1.4, 1.4, 200.0)]

program()
ORDER, SPAN = schedule()
SCRATCH = {"p" + k: ("sbuf", [128, v[1]], v[0]) for k, v in POOL.items()}
SCRATCH.update(SHAPES)
SEMAPHORES = list(SEMS)


def rank_program(g, core, T, topo):
    rank = T.rank_of(core)
    if rank is None:
        return
    n = len(T.cores)
    Q = dict(v=g.vector, s=g.scalar, t=g.tensor, g=g, y=g.sync)
    known = dict(v={}, s={}, t={}, g={}, y={})
    count, mark, clock = {}, {}, {}

    def engines(src, dst):
        return topo.engines(src, dst)[:8]

    for k in ORDER:
        o = OPS[k]
        e, fn = o["use"][0], o["use"][1]
        if e == "n":
            mark[k] = (o["sem"], len(engines(T.cores[(rank - o["step"]) % n], core)))
            count[o["sem"]] = mark[k][1]
            clock[k] = {}
            continue
        kn = known[e]
        need = {}
        for j, raw in o["dep"].items():
            if raw or OPS[j]["use"][0] != e or "sem" in OPS[j] or "sem" in o:
                s, v = mark[j]
                if kn.get(s, 0) < v and need.get(s, (0, 0))[0] < v:
                    need[s] = (v, j)
        for s, (v, j) in sorted(need.items(), key=lambda q: -OPS[q[1][1]]["at"]):
            if kn.get(s, 0) < v:
                Q[e].wait_ge(T.sem[s], v)
                kn[s] = v
                for s2, v2 in clock[j].items():
                    kn[s2] = max(kn.get(s2, 0), v2)
        clock[k] = dict(kn)
        if "send" in o:
            dst, src, step, rs = o["send"]
            peer = T.cores[(rank + step) % n]
            es = engines(core, peer)
            rid, pid, se = topo.addr(peer)
            g.remote_dma(real(T, dst), real(T, src), T.sem[rs], T.sem[o["sem"]], pid, rid, sum(1 << x for x in es))
            mark[k] = (o["sem"], len(es))
        elif "sem" in o:
            for one in fn if isinstance(fn, list) else [fn]:
                one(g, T).then_inc(T.sem[o["sem"]], 16)
            mark[k] = (o["sem"], o["inc"])
        else:
            s = "e" + e
            fn(g, T).then_inc(T.sem[s], 1)
            mark[k] = (s, count.get(s, 0) + 1)
        count[mark[k][0]] = mark[k][1]
    for s, v in count.items():
        if max(known[e].get(s, 0) for e in known) < v or s[0] == "e":
            g.wait_ge(T.sem[s], v)
